import numpy as np, ml_dtypes
CORES = [2,3,42,43,82,83,122,123]
N = 8
import mx_ref
BF = ml_dtypes.bfloat16
def gcols(t, e):
    v = np.concatenate([t.reshape(8, 16, -1, 4), np.zeros((8, 16, 1, 4), BF)], axis=2)
    return np.ascontiguousarray(np.stack([v[g][:, e[g]] for g in range(8)])).reshape(128, -1)
def tile(rs):
    return np.stack(rs, axis=2).reshape(128, -1).astype(BF)
def pick(q, e):
    c = np.concatenate([q[0].reshape(128, -1, 4), np.zeros((128, 1, 4), np.uint8)], axis=1); s = np.concatenate([q[1], np.ones((16, 1), np.uint8)], axis=1)
    return (np.ascontiguousarray(c[:, e].reshape(128, -1)), np.ascontiguousarray(s[:, e]))
def join(*qs):
    return (np.concatenate([q[0] for q in qs], axis=1), np.concatenate([q[1] for q in qs], axis=1))
def put(q, e, v):
    c, s = q[0].reshape(128, -1, 4).copy(), q[1].copy(); c[:, e] = v[0].reshape(128, -1, 4); s[:, e] = v[1]
    return (c.reshape(128, -1), s)
def pk(c, s):
    return (np.ascontiguousarray(c), mx_ref.live(s))
def emit(q):
    return q[0], q[1]
def packed(v, rng):
    q = [mx_ref.quantize(np.ascontiguousarray(v[r])) for r in range(N)]
    return np.stack([a for a, b in q]), np.stack([mx_ref.plane(b, rng) for a, b in q])
def values_of_codes():
    e, c = np.zeros((128, 128, 4), np.float32), np.zeros((128, 2, 4), np.uint8)
    e[np.arange(128), np.arange(128), 0] = 1
    c[:127, :, 0] = np.arange(256).reshape(2, 128).T[:127]
    return mx_ref.matmul(mx_ref.quantize(e.reshape(128, 512).astype(BF)), (c.reshape(128, 8), np.full((16, 2), 127, np.uint8))).T.reshape(-1).astype(np.float64)
CODE_VALUE, SCALE_VALUE = values_of_codes(), 2.0 ** (np.arange(256) - 127.0)
def decode(q):
    return (CODE_VALUE[q[0]].reshape(16, 8, -1, 4) * SCALE_VALUE[q[1]][:, None, :, None] + 0.0).reshape(128, -1).astype(np.float32)
def f(rng, *shape):
    return mx_ref.flush((rng.standard_normal(shape, dtype=np.float32) * np.exp2(rng.integers(-2, 3, shape[:-1] + (1,)))).astype(BF))
def wide(rng, *shape, cols=0):
    v = rng.standard_normal(shape, dtype=np.float32) * np.exp2(rng.integers(-12, 13, shape)).astype(np.float32)
    if cols: v *= np.repeat(np.exp2(rng.integers(-cols, cols + 1, shape[:-2] + (1, shape[-1] // 4))) * (rng.random(shape[:-2] + (1, shape[-1] // 4)) > 0.0625), 4, axis=-1).astype(np.float32)
    return mx_ref.flush(v.astype(BF))
C, L, R = 256, 64, 3
def big(v):
    v = v.astype(np.float32)
    v[np.abs(v) < np.float32(2.0 ** -16)] = 0
    return v.astype(BF)
def numbers_of(rng):
    return {"x": big(f(rng, N, 128, 4 * C)), "u": np.array(f(rng, N, 128, 512)), "v": np.array(f(rng, N, 128, 512))}
def layers(rng):
    return big(f(rng, N, 128, 2048)).reshape(N, 8, 16, 4, 8, 16, 4)
def weights(rng, w):
    c, p = packed(np.ascontiguousarray(w).reshape(N, 128, 2048), rng)
    return {"wc": c, "ws": p}
def setup_inputs(rng):
    return {**numbers_of(rng), **weights(rng, layers(rng))}
def setup_inputs_ties(rng):
    d = numbers_of(rng)
    x = d["x"].reshape(N, 8, 16, C, 4)
    x[:, :, 0] = 0
    x[:, :, 0, :, 0] = np.floor(rng.integers(2, 7, (N, 8, 1)) * rng.random((N, 8, C))).astype(np.float32).astype(BF)
    u = d["u"].reshape(N, 128, 128, 4)
    u[:, :, ::16] = 0
    o = rng.permutation(N)
    for r in range(N):
        for h in range(0, 128, 16): u[r, h, h, 0] = 0.0 if r == o[0] else -1.0 if r == o[1] else 1.0
    w = layers(rng)
    w[:, :, :, :, :, 0] = 0
    return {"x": x.reshape(N, 128, 4 * C), "u": u.reshape(N, 128, 512), "v": d["v"], **weights(rng, w)}
def setup_inputs_near(rng):
    d = numbers_of(rng)
    x = d["x"].astype(np.float32).reshape(N, 8, 16, C, 4)
    u = d["u"].reshape(N, 128, 128, 4)
    h = rng.permutation(8)
    o = rng.permutation(N)
    x[:, :, 0] = 0
    x[:, :, 8:] = 0
    u[:, :, ::16] = 0
    for r in range(N):
        k = -1.0 if o[r] % 4 == 3 else 1.0
        for g in h[:4]:
            x[r, g, 0, :, 0] = np.where(rng.random(C) < rng.uniform(0.2, 0.9), 1.0, -1.0)
            s = rng.integers(0, 16 if o[r] % 2 else 8, C)
            x[r, g, 8] = ((s[:, None] >> np.arange(4)) & 1) * np.exp2(np.arange(4) - 23.0)
            x[r, g, 11, :, 0] = 2.0 ** -10
            a, m = 16 * int(g), k if o[r] < N // 2 else k * 2.0 ** -30
            u[r, a, a, 0] = m
            u[r, a + 8, a] = m
            u[r, a + 11, a, 0] = m
        for g in h[4:]:
            x[r, g, 10, :, 0] = (1.0 + 0.125 * rng.integers(0, 8, C)) * 2.0 ** -30
            u[r, 16 * int(g) + 10, 16 * int(g), 0] = k * 2.0 ** -30
        for g in h[6:]: x[r, g, 10, rng.integers(C), 0] = 2.0 ** 29
    w = layers(rng)
    w[:, :, 8:] = 0
    w[:, :, :, :, :, 8:] = 0
    w[:, :, 0] = 0
    w[:, :, :, :, :, 0] = 0
    return {"x": x.reshape(N, 128, 4 * C).astype(BF), "u": u.reshape(N, 128, 512), "v": d["v"], **weights(rng, w)}
def setup_inputs_huge(rng):
    d = numbers_of(rng)
    h = rng.permutation(8)
    o = rng.permutation(N)
    c = rng.integers(0, 2, 8) * 2.0 - 1.0
    x = (0.9 + 0.1 * rng.random((N, 8, 1, C, 1))) * (0.95 + 0.05 * rng.random((N, 8, 16, C, 4))) * c[:, None, None, None]
    x[:, h[4:]] *= rng.choice([-1.0, 1.0], (N, 4, 1, C, 1))
    u = d["u"].reshape(N, 128, 128, 4)
    for r in range(N):
        for g in range(8):
            a = 2.0 ** 30 * (1.0 - 0.1 * rng.random((8, 16, 4))) * c[:, None, None]
            if o[r] % 4 == 0: a = -a
            if o[r] % 4 < 2: a[h[4:]] = 0
            else: a[h[:4]] = 0
            u[r, :, 16 * g] = a.reshape(128, 4).astype(np.float32).astype(BF)
    w = np.zeros((N, 128, 4, 128, 4), np.float32)
    i = np.arange(128)
    for b in range(4): w[:, i, b, i, b] = -1
    return {"x": (2.0 ** 30 * x).astype(np.float32).reshape(N, 128, 4 * C).astype(BF), "u": u.reshape(N, 128, 512), "v": d["v"], **weights(rng, w.astype(BF))}
def setup_inputs_ends(rng):
    d = numbers_of(rng)
    x = d["x"].astype(np.float32).reshape(N, 8, 16, C, 4)
    h = rng.permutation(8)
    e = int(rng.integers(N))
    x[:, :, 0] = 0
    for g in range(8):
        p = rng.permutation(N)
        if g in h[:4]: p[(e + np.arange(N)) % N] = np.concatenate([[0, 1, N - 1, N - 2], 2 + rng.permutation(N - 4)])
        x[:, g, 0, :, 0] = np.exp2(p)[:, None] * (1.0 + 0.125 * rng.integers(0, 8, (N, C)))
    m = int(h[7])
    k = np.repeat(np.arange(4.0), [L // 4, L - L // 4, L, C - 2 * L])
    for r in range(N):
        j = rng.permutation(C)
        x[r, m, 0, j] = -np.exp2(k)[:, None]
        x[r, m, 0, j, r % 4] = np.exp2(4.0 - k)
        x[r, m, 0, j[C - 1], r % 4] = -1.5
    s = (N, 8, 8, C, 4)
    x[:, :, 8:] = rng.choice([-1.0, 1.0], s) * (1.0 + (2 * rng.integers(0, 64, s) + 1) * 0.0078125) * np.exp2(rng.integers(-14, -7, s))
    x[:, :, 8, :, 0] = rng.choice([-1.96875, 1.96875], (N, 8, C))
    u = d["u"].reshape(N, 128, 128, 4)
    u[:, :, ::16] = 0
    for a in range(0, 128, 16): u[:, a, a, 0] = 1
    for r in range(N):
        u[r, 16 * m, 16 * m, 0] = 0
        u[r, 16 * m, 16 * m, r % 4] = 1
    w = layers(rng)
    w[:, :, 0] = 0
    w[:, :, :, :, :, 0] = 0
    return {"x": x.reshape(N, 128, 4 * C).astype(BF), "u": u.reshape(N, 128, 512), "v": d["v"], **weights(rng, w)}
def setup_inputs_spread(rng):
    d = setup_inputs(rng)
    d["x"] = big(wide(rng, N, 128, 4 * C, cols=6))
    return d
def check_inputs(d):
    b = []
    for k in ("x", "u", "v"):
        a = np.abs(d[k].astype(np.float32))
        if not (np.isfinite(a).all() and ((a == 0) | (a >= 2.0 ** -30) & (a <= 2.0 ** 30)).all()): b.append("a value of " + k)
    none, least, most = [emit(mx_ref.quantize(np.full((128, 16), k, np.float32).astype(BF)))[1][0, 0] for k in (0.0, 2.0 ** -30, 2.0 ** 30)]
    for r in range(N):
        if ((d["wc"][r] == 0x7F) | (d["wc"][r] == 0xFF)).any(): b.append("wc: a code that is no number")
        s = mx_ref.live(d["ws"][r])
        if ((s != none) & ((s < least) | (s > most))).any(): b.append("ws: a scale out of range")
    return b
def reference(x, u, v, wc, ws):
    qu = [mx_ref.quantize(u[r]) for r in range(N)]
    lay = [pk(wc[r], ws[r]) for r in range(N)]
    now = [x[r] for r in range(N)]
    ls = np.zeros((N, 8, C + 2 * L), np.float32)
    for t in range(R):
        order, kept, gone = [], [], []
        for r in range(N):
            s = mx_ref.matmul(qu[r], mx_ref.quantize(now[r]))[::16] + np.float32(0.0)
            o = np.argsort(-s, axis=1, kind="stable")
            order.append(o)
            kept.append(np.take_along_axis(s, o[:, L:], axis=1))
            gone.append(mx_ref.quantize(gcols(now[r], o[:, :L])))
        came = [decode(gone[r]).astype(BF) for r in range(N)]
        final = []
        for r in range(N):
            said = []
            for e in ((r + 1) % N, (r + 2) % N):
                a = mx_ref.matmul(qu[e], gone[r])[::16] + np.float32(0.0)
                said.append(np.count_nonzero(kept[e][:, None, :] > a[:, :, None], axis=2))
            final.append(np.maximum(said[0], said[1]))
        made = []
        for r in range(N):
            lo, hi = sorted([(r - 1) % N, (r - 2) % N])
            place = np.concatenate([order[r][:, L:], np.tile(C + np.arange(2 * L), (8, 1))], axis=1)
            key = np.concatenate([np.tile(np.arange(C - L), (8, 1)), final[lo], final[hi]], axis=1)
            l = np.take_along_axis(place, np.argsort(key, axis=1, kind="stable")[:, :C], axis=1)
            ls[r] = np.concatenate([l, final[lo], final[hi]], axis=1)
            a = np.concatenate([now[r], came[lo], came[hi]], axis=1)
            before = np.concatenate([l[:, :1], l[:, :-1]], axis=1)
            z = ((gcols(a, l).astype(np.float32) + gcols(a, before).astype(np.float32)) * np.float32(0.5)).astype(BF)
            q = mx_ref.quantize(z)
            made.append(tile([mx_ref.matmul(pick(lay[r], np.arange(128 * b, 128 * b + 128)), q) * np.float32(0.03125) + z[:, b::4].astype(np.float32) for b in range(4)]))
        now = made
    y = np.zeros((N, 128, C), np.float32)
    oc, osc = np.zeros((N, 128, 4 * C), np.uint8), np.zeros((N, 16, C), np.uint8)
    for r in range(N):
        q = mx_ref.quantize(now[r])
        y[r] = mx_ref.matmul(mx_ref.quantize(v[r]), q)
        oc[r], osc[r] = emit(q)
    return {"y": y, "ls": ls, "oc": oc, "osc": osc}

@@ -1,0 +1,572 @@
+from concourse.bass import DstId, RemoteDMATransfer
+from concourse.mybir import dt, AluOpType, ActivationFunctionType
+
+ALU = AluOpType
+ACT = ActivationFunctionType
+R = 3
+BIG = 1.0e29
+F8 = "float8_e4m3fn_x4"
+K = {
+    "su": 9,
+    "vs": 14,
+    "ks": 5,
+    "blend": "g20s g22v g21s b22v a22v e22v b20v g23s a21v b21v o21v a20v o22s a23v o20s b23v e20s o23v e23v e21s "
+             "q00v q10v m01t m00t p01v m02t p00v m11t x01s m10t p02v x00s m13t p11v m03t x02s p10v m12t x11s p03v "
+             "x10s p13v x03s p12v x13s x12v",
+}
+
+
+def _s(n, d):
+    return ("sbuf", [128, n], d)
+
+
+SCRATCH = {
+    "ps": ("psum", [128, 4096], "float32"),
+    "xin": _s(1024, "bfloat16"), "xt": _s(1024, "bfloat16"), "ut": _s(512, "bfloat16"), "vt": _s(512, "bfloat16"),
+    "uq": _s(128, F8), "uqs": _s(128, "uint8"), "ur0": _s(128, F8), "ur0s": _s(128, "uint8"),
+    "upk": _s(16, F8), "upks": _s(16, "uint8"), "uland": _s(16, F8), "ulands": _s(16, "uint8"),
+    "ur1": _s(128, F8), "ur1s": _s(128, "uint8"), "ur2": _s(128, F8), "ur2s": _s(128, "uint8"),
+    "vq": _s(128, F8), "vqs": _s(128, "uint8"), "wq": _s(512, F8), "wqs": _s(512, "uint8"),
+    "et": _s(2048, "bfloat16"), "ones": _s(512, "bfloat16"), "eq": _s(512, F8), "eqs": _s(512, "uint8"),
+    "g1": _s(512, "bfloat16"), "g2": _s(512, "bfloat16"), "gq": _s(128, F8), "gqs": _s(128, "uint8"),
+    "ft": _s(2816, "bfloat16"), "fc": _s(704, F8), "fcs": _s(704, "uint8"),
+    "xq": _s(256, F8), "xqs": _s(256, "uint8"), "zq": _s(256, F8), "zqs": _s(256, "uint8"),
+    "qa": _s(128 * R, F8), "qas": _s(128 * R, "uint8"), "aland": _s(128 * R, F8), "alands": _s(128 * R, "uint8"),
+    "xp": _s(1024, "bfloat16"), "vh": _s(1280, "bfloat16"), "gg": _s(1024, "bfloat16"),
+    "zt": _s(1024, "bfloat16"), "za": _s(1024, "bfloat16"), "zb": _s(1024, "bfloat16"), "at": _s(512, "bfloat16"),
+    "d1": _s(256, "float32"), "hs": _s(256, "float32"), "ssend": _s(16 * R, "float32"), "sland": _s(32 * R, "float32"),
+    "nes": _s(256, "bfloat16"), "base": _s(16, "float32"), "acc": _s(16, "float32"), "r1": _s(16, "float32"),
+    "cm": _s(256, "bfloat16"), "ce": _s(256, "bfloat16"), "sg": _s(2048, "bfloat16"), "jk": _s(2048, "bfloat16"),
+    "cmp": _s(2048, "bfloat16"), "scn": _s(2048, "bfloat16"), "pc": _s(2560, "bfloat16"),
+    "rk": _s(16, "float32"), "roff": _s(16, "uint16"),
+    "ob": _s(288, "bfloat16"), "tb": _s(544, "bfloat16"), "tw": _s(544, "bfloat16"), "lw": _s(16, "float32"),
+    "lf": _s(16, "float32"), "ol": _s(16, "uint16"), "ll": _s(16, "uint16"),
+    "pt": _s(288, "bfloat16"), "pp": _s(288, "bfloat16"), "pm": _s(14, "float32"),
+    "fsend": _s(16 * R, "bfloat16"), "fland": _s(32 * R, "bfloat16"),
+    "kx": _s(128, "float32"), "kr": _s(128, "float32"), "ko": _s(16, "float32"),
+    "xl": _s(8, "uint16"), "kl": _s(2, "uint16"), "lj": _s(8, "int32"),
+    "pa": _s(8, "float32"), "pb": _s(8, "float32"), "ksum": _s(8, "float32"), "pl": _s(8, "float32"),
+    "poff": _s(8, "uint16"), "wb": _s(336, "bfloat16"), "nf": _s(256, "bfloat16"), "cu": _s(288, "bfloat16"),
+    "i1": _s(256, "int32"), "i2": _s(256, "int32"), "negm": _s(256, "float32"), "hold": _s(256, "float32"),
+    "m01": _s(256, "bfloat16"), "alt": _s(512, "bfloat16"),
+    "seg": _s(512, "bfloat16"), "cc": _s(16, "float32"), "jd": _s(256, "bfloat16"),
+    "pi": _s(8, "int32"), "pf": _s(8, "float32"), "li": _s(16, "int32"),
+    "tl": _s(2, "uint16"), "cl": _s(2, "uint16"), "el": _s(16, "uint16"), "rl": _s(8, "uint16"),
+    "keyc": _s(128, "float32"), "qown": _s(16, "float32"), "ids": _s(128, "bfloat16"), "qrow": _s(128, "float32"),
+    "tbl": _s(320, "float32"), "lsb": _s(384, "float32"), "fq": _s(128, "float32"), "yb": _s(256, "float32"),
+}
+NCS, NDS = 100, 24
+SEMAPHORES = (["c%d" % i for i in range(NCS)] + ["d%d" % i for i in range(NDS)] + ["lsent", "au"]
+              + ["%s%d" % (k, t) for k in ("sa", "sb", "aa", "af") for t in range(R)])
+
+
+def split_engines(topo, src, d1, d2):
+    e1, e2 = topo.engines(src, d1), topo.engines(src, d2)
+    if len(e1) == len(e2):
+        h = len(e1) // 2
+        e1, e2 = e1[:h], e2[h:]
+    elif len(e1) > len(e2):
+        e1 = [e for e in e1 if e not in e2]
+    else:
+        e2 = [e for e in e2 if e not in e1]
+    return [(sum(1 << e for e in es), len(es)) for es in (e1, e2)]
+
+
+def rank_program(g, core, T, topo):
+    rank = T.rank_of(core)
+    if rank is None:
+        return
+    n = len(T.cores)
+    cores = T.cores
+    Q = {"g": g, "v": g.vector, "s": g.scalar, "t": g.tensor, "y": g.sync}
+
+    ops = []
+    known = {k: 0 for k in Q}
+    log = {}
+    exts = {}
+
+    def bits(a):
+        if a[0] == "ps":
+            return sum(1 << k for k in range(a[1] // 512, (a[2] - 1) // 512 + 1))
+        if a[3] == 1:
+            return ((1 << (a[2] - a[1])) - 1) << a[1]
+        return sum(1 << k for k in range(a[1], a[2], a[3]))
+
+    def ext(sem, count):
+        if sem not in exts:
+            exts[sem] = len(ops)
+            ops.append({"ext": (sem, count), "k": 1 << len(ops), "q": None})
+        return exts[sem]
+
+    def op(q, fn, rd, wr, after=(), dma=False, group=None):
+        me = len(ops)
+        deps = set(after)
+        for a, w in [(a, False) for a in rd] + [(a, True) for a in wr]:
+            m = bits(a)
+            for (o, om, ow, oq) in log.get(a[0], []):
+                if om & m and (w or ow or (a[0] == "ps" and oq != q)) and o != group:
+                    deps.add(o)
+        waits = []
+        for o in sorted(deps, reverse=True):
+            if not known[q] >> o & 1:
+                waits.append(o)
+                known[q] |= ops[o]["k"]
+                ops[o]["sig"] = True
+        k = known[q] | 1 << me | (0 if group is None else ops[group]["k"])
+        ops.append({"q": q, "fn": fn, "waits": waits, "ki": known[q], "k": k, "dma": dma})
+        for a, w in [(a, False) for a in rd] + [(a, True) for a in wr]:
+            m = bits(a)
+            if w:
+                log[a[0]] = [e for e in log.get(a[0], []) if e[1] & ~m]
+            log.setdefault(a[0], []).append((me, m, w, q))
+        return me
+
+    def A(name, a, b, s=1):
+        return (name, a, b, s)
+
+    def ap(a):
+        return T[a[0]][:, a[1]:a[2]] if a[3] == 1 else T[a[0]][:, a[1]:a[2]:a[3]]
+
+    def isap(a):
+        return isinstance(a, tuple)
+
+    def src(a, off):
+        return ap(a) if off is None else ap(a).indirect(ap(off))
+
+    def vts(out, in0, s1, s2, o0, o1=None, off=None, after=()):
+        rd = [in0] + [s for s in (s1, s2, off) if isap(s)]
+        f = lambda s: ap(s) if isap(s) else s
+        if o1 is None:
+            return op("v", lambda: g.vector.tensor_scalar(ap(out), src(in0, off), f(s1), None, o0), rd, [out], after)
+        return op("v", lambda: g.vector.tensor_scalar(ap(out), src(in0, off), f(s1), f(s2), o0, o1), rd, [out], after)
+
+    def vtt(out, in0, in1, o, off=None, after=()):
+        return op("v", lambda: g.vector.tensor_tensor(ap(out), src(in0, off), ap(in1), o),
+                  [in0, in1] + ([off] if off else []), [out], after)
+
+    def vcopy(out, in_):
+        return op("v", lambda: g.vector.tensor_copy(ap(out), ap(in_)), [in_], [out])
+
+    def vscatter(win, off, in_):
+        return op("v", lambda: g.vector.tensor_copy(ap(win).indirect(ap(off)), ap(in_)), [in_, off], [win])
+
+    def vscan(out, d0, d1, o0, o1, init=None):
+        return op("v", lambda: g.vector.tensor_tensor_scan(ap(out), ap(d0), ap(d1), ap(init) if init else 0.0, o0, o1),
+                  [d0, d1] + ([init] if init else []), [out])
+
+    def vsum(out, d):
+        return vscan(out, d, d, ALU.add, ALU.max)
+
+    def vseg(out, d, mask="seg"):
+        return vscan(out, A(mask, 0, out[2] - out[1]), d, ALU.mult, ALU.add)
+
+    def vtr(out, in_):
+        return op("v", lambda: g.vector.transpose(ap(out), ap(in_)), [in_], [out])
+
+    def vset(out, c):
+        return op("v", lambda: g.vector.memset(ap(out), c), [], [out])
+
+    def quant(c, a, b, tile, e0):
+        t, o, s = A(tile, e0, e0 + 4 * (b - a)), A(c, a, b), A(c + "s", a, b)
+        return op("v", lambda: g.vector.quantize_mx(ap(o), ap(s), ap(t)), [t], [o, s])
+
+    def act(out, in_, func, bias=None, scale=None, acc=None, off=None, after=()):
+        rd = [in_] + [s for s in (bias, off) if isap(s)]
+        kw = {}
+        if bias is not None:
+            kw["bias"] = bias
+        if scale is not None:
+            kw["scale"] = scale
+
+        def fn():
+            k = {a: (ap(b) if isap(b) else b) for a, b in kw.items()}
+            if acc is not None:
+                k["accum_out"] = ap(acc)
+            return g.scalar.activation(ap(out), src(in_, off), func, **k)
+        return op("s", fn, rd, [out] + ([acc] if acc else []), after)
+
+    def scaled(q, out, in_, c, off=None):
+        if q == "v":
+            return vts(out, in_, c, None, ALU.mult, off=off)
+        return act(out, in_, ACT.Copy, scale=c, off=off)
+
+    def zero(a):
+        return scaled("s", a, A("ones", 0, len(range(a[1], a[2], a[3]))), 0.0)
+
+    def pick(dst, win, w, off, after=()):
+        m = 16 * (off[2] - off[1])
+        o, i = A(dst, 0, m), A(win, 0, w)
+        op("v", lambda: g.vector.tensor_copy(ap(o).bitcast(dt.uint32), ap(i).bitcast(dt.uint32).indirect(ap(off))),
+           [i, off], [o], after)
+        o2, i2 = A(dst + "s", 0, m), A(win + "s", 0, w)
+        op("s", lambda: g.scalar.activation(ap(o2), ap(i2).indirect(ap(off)), ACT.Copy), [i2, off], [o2], after)
+
+    def mm(bank, w, w0, x, x0, m, after=(), start=True, stop=True, group=None):
+        o = A("ps", 512 * bank, 512 * bank + m)
+        r = [A(w, w0, w0 + 128), A(w + "s", w0, w0 + 128), A(x, x0, x0 + m), A(x + "s", x0, x0 + m)]
+        return op("t", lambda: g.tensor.matmul_mx(ap(o), ap(r[0]), ap(r[1]), ap(r[2]), ap(r[3]), start, stop),
+                  r, [o], after, group=group)
+
+    def iota(out, pattern, base, cm, whole=False):
+        if whole:
+            return op("g", lambda: g.iota(ap(out), pattern, base, cm), [], [out])
+        return op("g", lambda: g.iota(ap(out), pattern, base, cm, allow_small_or_imprecise_dtypes=True), [], [out])
+
+    def select(out, in_, pattern, cmp, base, cm):
+        return op("g", lambda: g.affine_select(ap(out), ap(in_), pattern, cmp, 0.0, base, cm), [in_], [out])
+
+    def dma(q, fn, rd, wr, after=()):
+        return op(q, fn, rd, wr, after, dma=True)
+
+    sent = [0]
+
+    def send(sbuf, dsts, codes, sems):
+        ms = split_engines(topo, core, cores[dsts[0][0]], cores[dsts[1][0]])
+
+        def fn():
+            f = (lambda a: ap(a).bitcast(dt.uint8)) if codes else ap
+            tr = []
+            for (rk_, place), (mask, cnt), sem in zip(dsts, ms, sems):
+                ad = topo.addr(cores[rk_])
+                tr.append(RemoteDMATransfer(dst_ids=[DstId(rid=ad[0], pnc=ad[1])], dma_engine_mask=mask,
+                                            remote_sem=T.sem[sem], src=f(sbuf), dst=f(place)))
+            g.remote_dma_fused(tr, local_sem=T.sem.lsent)
+        sent[0] += ms[0][1] + ms[1][1]
+        return op("g", fn, [sbuf], [])
+
+    def send1(sbuf, rk_, place, codes, sem, engines):
+        def fn():
+            f = (lambda a: ap(a).bitcast(dt.uint8)) if codes else ap
+            ad = topo.addr(cores[rk_])
+            g.remote_dma(f(place), f(sbuf), T.sem[sem], T.sem.lsent, ad[1], ad[0], sum(1 << e for e in engines))
+        sent[0] += len(engines)
+        return fn
+
+    def fwd(r):
+        return [(r + 1) % n, (r + 2) % n]
+
+    def back(r):
+        return [(r - 1) % n, (r - 2) % n]
+
+    def count(s, dsts):
+        return split_engines(topo, cores[s], cores[dsts[0]], cores[dsts[1]])[dsts.index(rank)][1]
+
+    def slot(s, r):
+        return sorted(back(r)).index(s)
+
+    def handed(s):
+        a, b = [topo.chip(cores[r]) for r in fwd(s)]
+        return a == b != topo.chip(cores[s])
+
+    def inner(r):
+        far = [e for e in range(n) if topo.chip(cores[e]) != topo.chip(cores[r])][0]
+        return [e for e in topo.engines(cores[r], cores[(r + 1) % n]) if e not in topo.engines(cores[r], cores[far])]
+
+    def codes_count(s):
+        if not handed(s):
+            return count(s, fwd(s))
+        r = fwd(s)[0]
+        return len(topo.engines(cores[s], cores[r])) if r == rank else len(inner(r))
+
+    ncodes = sum(codes_count(s) for s in back(rank))
+    nfwd = sum(count(s, fwd(s)) for s in back(rank))
+    nback = [count(e, back(e)) for e in fwd(rank)]
+
+    dma("s", lambda: g.scalar.dma_start(T.ut[:], T.u[:]), [], [A("ut", 0, 512)])
+    xin = [dma("y", lambda h=h: g.sync.dma_start(T.xin[:, 512 * h:512 * h + 512], T.x[:, 512 * h:512 * h + 512]),
+               [], [A("xin", 512 * h, 512 * h + 512)]) for h in range(2)]
+    dma("y", lambda: g.sync.dma_start(T.wq[:].bitcast(dt.uint8), T.wc[:]), [], [A("wq", 0, 512)], xin)
+    dma("y", lambda: g.sync.dma_start(T.wqs[:], T.ws[:]), [], [A("wqs", 0, 512)])
+    dma("y", lambda: g.sync.dma_start(T.vt[:], T.v[:]), [], [A("vt", 0, 512)])
+
+    FT = [0, 1024, 1792, 2304, 2816]
+    iota(A("li", 0, 16), [[1, 16]], 0, 0, True)
+    iota(A("pi", 0, 1), [[0, 1]], 0, 1, True)
+    iota(A("i1", 0, 256), [[0, 16], [1, 16]], 128, -1, True)
+    vset(A("ones", 0, 512), 1.0)
+    select(A("g1", 0, 512), A("ones", 0, 512), [[16, 8], [0, 64]], ALU.is_ge, 15, -1)
+    select(A("g2", 0, 512), A("g1", 0, 512), [[-16, 8], [0, 64]], ALU.is_ge, 0, 1)
+    vset(A("hold", 0, 256), 0.0)
+    vset(A("seg", 0, 512), 1.0)
+    vset(A("hold", 0, 256, 16), -5 * BIG)
+    vset(A("seg", 0, 512, 16), 0.0)
+    vts(A("rl", 0, 8), A("li", 0, 8), 16.0, None, ALU.mult)
+    vcopy(A("el", 0, 16), A("li", 0, 16))
+    vts(A("pi", 2, 3), A("pi", 0, 1), 15, None, ALU.bitwise_and)
+    vts(A("pi", 4, 5), A("pi", 0, 1), 4, None, ALU.logical_shift_right)
+    vts(A("i2", 0, 256), A("i1", 0, 256), 15, None, ALU.bitwise_and)
+    vts(A("cl", 0, 1), A("pi", 2, 3), 16.0, 112.0, ALU.mult, ALU.min)
+    vtt(A("pi", 5, 6), A("pi", 4, 5), A("pi", 0, 1), ALU.add)
+    vts(A("negm", 0, 256), A("i2", 0, 256), 0.0, -BIG, ALU.not_equal, ALU.mult)
+    for a, e in ((0, 208), (1, 144), (2, 80), (3, 16)):
+        zero(A("ft", FT[a] + 4 * e, FT[a + 1]))
+
+    quant("uq", 0, 128, "ut", 0)
+    pick("ur0", "uq", 128, A("rl", 0, 8))
+    pick("upk", "uq", 128, A("cl", 0, 1))
+    act(A("m01", 0, 256), A("negm", 0, 256), ACT.Relu, bias=1.0, scale=10.0 / BIG)
+    for a in (A("ob", 0, 16), A("ob", 272, 288), A("at", 256, 512), A("cu", 0, 16), A("cu", 272, 288),
+              A("pc", 15, 256, 16), A("pc", 2319, 2560, 16), A("acc", 0, 1)):
+        zero(a)
+    for h in range(2):
+        quant("xq", 128 * h, 128 * h + 128, "xin", 512 * h)
+    send(A("upk", 0, 8), [(s, A("uland", 8 * j, 8 * j + 8)) for j, s in enumerate(back(rank))], True, ["au", "au"])
+    send(A("upks", 0, 8), [(s, A("ulands", 8 * j, 8 * j + 8)) for j, s in enumerate(back(rank))], False, ["au", "au"])
+
+    def turn(dst, row, which):
+        if which == 0:
+            vtr(A(dst, 0, 256), A(row, 16, 272))
+        else:
+            vtr(A(dst, 256, 544), A(row, 0, 288))
+
+    def flags(c):
+        a, e = (0, 16 - c) if c > 12 else (1 + (12 - c) // 4, (12 - c) % 4)
+        return A("ft", FT[a] + e, FT[a] + 64 * c, 4)
+
+    SU, VS, KS = K["su"], K["vs"], K["ks"]
+    at16 = lambda c: 8 * c * (c - 1)
+    outs = []
+
+    for t in range(R):
+        first, last = t == 0, t == R - 1
+        xs = 1.0 if first else 0.03125
+
+        mm(0, "ur0", 0, "xq", 0, 256)
+        mm(1, "ur0", 0, "xq", 0, 256)
+        if first:
+            vts(A("pi", 6, 7), A("pi", 5, 6), 1, None, ALU.bitwise_and)
+            vts(A("pf", 0, 1), A("pi", 2, 3), 16.0, None, ALU.mult)
+            vts(A("pf", 2, 3), A("pi", 2, 3), -1.0, 15.0, ALU.mult, ALU.add)
+            vts(A("tl", 0, 1), A("pi", 6, 7), 272.0, A("pf", 0, 1), ALU.mult, ALU.add)
+        vtt(A("d1", 0, 256), A("ps", 0, 256), A("negm", 0, 256), ALU.add)
+        if first:
+            vts(A("cc", 0, 16), A("li", 0, 16), 16.0, A("pf", 2, 3), ALU.mult, ALU.add)
+        vscan(A("hs", 0, 256), A("hold", 0, 256), A("d1", 0, 256), ALU.add, ALU.max)
+        own = lambda c: A("hs", 16 * c + 15, 16 * c + 16)
+        act(A("ssend", 16 * t, 16 * t + 16), A("hs", 15, 256, 16), ACT.Copy)
+        send(A("ssend", 16 * t, 16 * t + 16),
+             [(s, A("sland", 32 * t + 16 * j, 32 * t + 16 * j + 16)) for j, s in enumerate(back(rank))],
+             False, ["sa%d" % t, "sb%d" % t])
+        if first:
+            iota(A("jd", 0, 256), [[1, 256]], 0, 0)
+            for b in range(4):
+                select(A("et", 512 * b, 512 * b + 512), A("ones", 0, 512), [[8, 128], [1, 4]], ALU.is_equal, -b, -8)
+        if t == 1:
+            iota(A("qrow", 0, 128), [[1, 128]], 0, 0)
+            iota(A("tbl", 0, 128), [[1, 128]], 256, 0)
+
+        def on_scalar(cs):
+            for c in cs:
+                act(A("sg", at16(c), at16(c) + 16 * c), A("ps", 512, 512 + 16 * c), ACT.Sign, bias=own(c), scale=-1.0)
+            for c in cs:
+                act(flags(c), A("sg", at16(c), at16(c) + 16 * c), ACT.Relu, acc=A("acc", c, c + 1))
+
+        def on_vector(cs):
+            for c in cs:
+                vts(flags(c), A("ps", 0, 16 * c), own(c), None, ALU.is_lt)
+
+        on_scalar(range(SU, 4, -1))
+        on_scalar(range(4, 0, -1))
+        vtt(A("ft", 0, 1024, 4), A("ps", 0, 256), A("hs", 0, 256), ALU.is_le)
+        on_vector([15, 14, 13, 12])
+        quant("fc", 0, 256, "ft", FT[0])
+        if first:
+            quant("gq", 0, 128, "g2", 0)
+        grp = mm(3, "gq", 0, "fc", 0, 256, stop=False)
+        on_vector(range(11, SU, -1))
+        vseg(A("nes", 0, 256), A("ft", 0, 1024, 4))
+        quant("fc", 256, 448, "ft", FT[1])
+        grp = mm(3, "gq", 0, "fc", 256, 192, start=False, stop=False, group=grp)
+        vtt(A("base", 0, 16), A("cc", 0, 16), A("nes", 15, 256, 16), ALU.subtract)
+        quant("fc", 448, 576, "ft", FT[2])
+        grp = mm(3, "gq", 0, "fc", 448, 128, start=False, stop=False, group=grp)
+        quant("fc", 576, 704, "ft", FT[3])
+        mm(3, "gq", 0, "fc", 576, 128, start=False, group=grp)
+        for c in range(VS - 1, SU, -1):
+            act(A("jk", at16(c), at16(c) + 16 * c), flags(c), ACT.Copy, acc=A("acc", c, c + 1))
+        ends = lambda c: 256 * (c - VS) + 256
+        for c in range(15, VS, -1):
+            vsum(A("scn", ends(c) - 16 * c, ends(c)), flags(c))
+        vtt(A("cm", 0, 256), A("ps", 1536, 1792), A("m01", 0, 256), ALU.mult)
+        if VS < 16:
+            vsum(A("scn", ends(VS) - 16 * VS, ends(VS)), flags(VS))
+        vseg(A("ce", 0, 256), A("cm", 0, 256))
+        if VS < 16:
+            vtt(A("r1", VS, 16), A("base", VS, 16), A("scn", 255, ends(15), 256), ALU.subtract)
+        vtt(A("r1", 0, VS), A("base", 0, VS), A("acc", 0, VS), ALU.subtract)
+        vtt(A("rk", 0, 16), A("r1", 0, 16), A("ce", 15, 256, 16), ALU.add)
+        vcopy(A("roff", 0, 16), A("rk", 0, 16))
+        if first:
+            for b in range(4):
+                act(A("xp", 256 * b, 256 * b + 256), A("xin", b, 1024, 4), ACT.Copy)
+        vscatter(A("ob", 16, 272), A("roff", 0, 16), A("jd", 0, 256))
+        if first:
+            au = ext("au", 2 * sum(nback))
+            pick("ur1", "uland", 16, A("el", 0, 8), [au])
+        turn("tb", "ob", 0)
+        turn("tb", "ob", 1)
+        vts(A("ol", 0, 16), A("tb", 0, 544), 0.0, None, ALU.add, off=A("tl", 0, 1))
+        if first:
+            pick("ur2", "uland", 16, A("el", 8, 16), [au])
+
+        for b in (0, 2, 1, 3):
+            scaled("v" if b < 2 else "s", A("at", b, 256, 4), A("xp", 256 * b, 256 * b + 256), xs, A("ol", 0, 4))
+        quant("qa", 128 * t, 128 * t + 128, "at", 0)
+        mm(1, "ur1", 0, "qa", 128 * t, 128)
+        mm(0, "ur2", 0, "qa", 128 * t, 128)
+        land = lambda name, s, r: A(name, 128 * t + 64 * slot(s, r), 128 * t + 64 * slot(s, r) + 64)
+        for name, to, codes in (("qa", "aland", True), ("qas", "alands", False)):
+            a = A(name, 128 * t, 128 * t + 64)
+            if handed(rank):
+                r = fwd(rank)[0]
+                op("g", send1(a, r, land(to, rank, r), codes, "aa%d" % t, topo.engines(core, cores[r])), [a], [])
+            else:
+                send(a, [(r, land(to, rank, r)) for r in fwd(rank)], codes, ["aa%d" % t] * 2)
+        vset(A("wb", 0, 336), 256.0)
+
+        e1, e2 = ext("sa%d" % t, nback[0]), ext("sb%d" % t, nback[1])
+        for c in range(16):
+            act(A("cmp", c, 1024, 16), A("ps", 512, 576), ACT.Sign, bias=A("sland", 32 * t + c, 32 * t + c + 1),
+                scale=-1.0, after=[e1])
+        for c in range(16):
+            vts(A("cmp", 1024 + c, 2048, 16), A("ps", 0, 64), A("sland", 32 * t + 16 + c, 32 * t + 17 + c), None,
+                ALU.is_lt, after=[e2])
+        pieces = [(0, 512), (512, 768), (768, 1024)]
+        for a, b in pieces:
+            act(A("cmp", a, b), A("cmp", a, b), ACT.Relu)
+        for a, b in [(1024, 1536), (1536, 2048)] + pieces:
+            vseg(A("pc", 256 + a, 256 + b), A("cmp", a, b))
+        vtr(A("pt", 0, 128), A("pc", 256 + 15, 2304, 16))
+        vtr(A("pt", 128, 288), A("pc", 15, 2560, 16))
+        vseg(A("pp", 0, 288), A("pt", 0, 288))
+        vtt(A("pm", 0, 14), A("pp", 15, 224, 16), A("pp", 79, 288, 16), ALU.max)
+        vts(A("fsend", 16 * t, 16 * t + 14), A("pm", 0, 14), 64.0, 128.0, ALU.max, ALU.mult)
+        place = lambda r: 32 * t + 14 * slot(rank, r)
+        send(A("fsend", 16 * t, 16 * t + 14), [(r, A("fland", place(r), place(r) + 14)) for r in fwd(rank)], False,
+             ["af%d" % t] * 2)
+
+        if first:
+            iota(A("lj", 0, 8), [[14, 2], [1, 4]], 0, 0, True)
+            iota(A("fq", 0, 128), [[32, 4], [0, 32]], 0, 0)
+        aa = ext("aa%d" % t, 2 * ncodes)
+        s = back(rank)[0]
+        if handed(s):
+            r = fwd(s)[1]
+            for name, codes in (("aland", True), ("alands", False)):
+                op("g", send1(land(name, s, rank), r, land(name, s, r), codes, "aa%d" % t, inner(rank)), [], [], [aa])
+        if first:
+            iota(A("ids", 0, 128), [[1, 128]], -127, 0)
+            iota(A("alt", 0, 256), [[0, 128], [1, 2]], 0, 0)
+            iota(A("alt", 256, 512), [[0, 128], [-1, 2]], 1, 0)
+            quant("eq", 0, 512, "et", 0)
+        for b in range(4):
+            mm(4 + b, "eq", 128 * b, "aland", 128 * t, 128, [aa])
+        for b in (2, 0, 3, 1):
+            scaled("v" if b < 2 else "s", A("vh", 320 * b + 128, 320 * b + 320), A("xp", 256 * b, 256 * b + 256),
+                   16.0 * xs, A("ol", 4, 16))
+        if first:
+            vts(A("pi", 1, 2), A("pi", 0, 1), 31, None, ALU.bitwise_and)
+            vcopy(A("pf", 1, 2), A("pi", 2, 3))
+            vts(A("pi", 3, 4), A("pi", 0, 1), 3, None, ALU.bitwise_and)
+            vts(A("pi", 7, 8), A("pi", 0, 1), 4, None, ALU.bitwise_and)
+            vcopy(A("pf", 5, 6), A("pi", 1, 2))
+            vts(A("qown", 0, 16), A("li", 0, 16), 16.0, A("pf", 1, 2), ALU.mult, ALU.add)
+            vcopy(A("pf", 3, 4), A("pi", 3, 4))
+            vcopy(A("xl", 0, 8), A("lj", 0, 8))
+            vts(A("keyc", 0, 128), A("fq", 0, 128), A("pf", 5, 6), None, ALU.add)
+            vts(A("pf", 4, 5), A("pi", 7, 8), 3.5, A("pf", 3, 4), ALU.mult, ALU.add)
+            vts(A("kl", 0, 1), A("pi", 6, 7), 9.0, A("pf", 4, 5), ALU.mult, ALU.add)
+        if t == 1:
+            quant("vq", 0, 128, "vt", 0)
+        if last:
+            act(A("tbl", 128, 320), A("ob", 80, 272), ACT.Copy)
+
+        af = ext("af%d" % t, nfwd)
+        came = A("fland", 32 * t, 32 * t + 28)
+        vtt(A("kx", 0, 128), came, A("keyc", 0, 128), ALU.add, off=A("xl", 0, 8), after=[af])
+        vtt(A("ko", 0, 16), came, A("qown", 0, 16), ALU.add, off=A("kl", 0, 1), after=[af])
+        vtr(A("kr", 0, 128), A("kx", 0, 128))
+        kown = lambda c: A("ko", c, c + 1)
+        for c in range(KS):
+            act(A("jk", 128 * c, 128 * c + 128), A("kr", 0, 128), ACT.Sign, bias=kown(c), scale=-1.0,
+                acc=A("ksum", c, c + 1))
+        for b in range(4):
+            act(A("vh", 320 * b, 320 * b + 128), A("ps", 2048 + 512 * b, 2048 + 512 * b + 128), ACT.Copy, scale=16.0)
+        for c in range(KS, 8):
+            vts(A("cmp", 128 * c, 128 * c + 128), A("kr", 0, 128), kown(c), 2.0, ALU.is_lt, ALU.mult)
+        vtt(A("pa", 0, 8), A("ko", 0, 8), A("qown", 0, 8), ALU.subtract)
+        for c in range(KS, 8):
+            vsum(A("scn", 128 * c, 128 * c + 128), A("cmp", 128 * c, 128 * c + 128))
+            if c == KS:
+                vts(A("pb", 0, 8), A("pa", 0, 8), 0.015625, 510.0, ALU.mult, ALU.min)
+        vtt(A("pl", KS, 8), A("scn", 128 * KS + 127, 1024, 128), A("pb", KS, 8), ALU.add)
+        vtt(A("pl", 0, KS), A("ksum", 0, KS), A("pb", 0, KS), ALU.add)
+        vts(A("poff", KS, 8), A("pl", KS, 8), -126.0, 0.5, ALU.add, ALU.mult)
+        vts(A("poff", 0, KS), A("pl", 0, KS), 1.0, 0.5, ALU.add, ALU.mult)
+        vscatter(A("wb", 16, 336), A("poff", 0, 8), A("ids", 0, 128))
+        vts(A("nf", 0, 256), A("wb", 16, 272), 255.0, None, ALU.is_gt)
+        turn("tw", "wb", 0)
+        vsum(A("cu", 16, 272), A("nf", 0, 256))
+        turn("tw", "wb", 1)
+        act(A("lw", 0, 16), A("tw", 0, 544), ACT.Copy, off=A("tl", 0, 1))
+        turn("tb", "cu", 0)
+        turn("tb", "cu", 1)
+        vtt(A("lf", 0, 16), A("tb", 0, 544), A("lw", 0, 16), ALU.min, off=A("tl", 0, 1))
+        vts(A("ll", 0, 16), A("lf", 0, 16), 127.0, None, ALU.add)
+
+        for word in K["blend"].split():
+            kind, h, b, q = word[0], int(word[1]), int(word[2]), word[3]
+            o = 256 * b
+            bank = 4 + b if h == 0 else (4 if b == 3 else b)
+            z32 = A("za", o + 1, o + 256, 2) if h == 0 else A("zb", o, o + 256, 2)
+            if kind == "g":
+                scaled(q, A("gg", o, o + 256), A("vh", 320 * b, 320 * b + 320), 1.0, A("ll", 0, 16))
+            elif kind == "a":
+                vseg(A("za", o, o + 256), A("gg", o, o + 256), "alt")
+            elif kind == "b":
+                vscan(A("zb", o, o + 256), A("alt", 256, 512), A("gg", o, o + 256), ALU.mult, ALU.add, A("gg", o, o + 1))
+            elif kind == "o":
+                scaled(q, A("zt", b, 512, 4), A("za", o + 1, o + 256, 2), 0.03125)
+            elif kind == "e":
+                scaled(q, A("zt", 512 + b, 1024, 4), A("zb", o, o + 256, 2), 0.03125)
+            elif kind == "q":
+                quant("zq", 128 * h, 128 * h + 128, "zt", 512 * h)
+            elif kind == "m":
+                mm(bank, "wq", 128 * b, "zq", 128 * h, 128)
+            elif kind == "p":
+                vtt(A("xp", o + 1 - h, o + 256, 2), A("ps", 512 * bank, 512 * bank + 128), z32, ALU.add)
+            elif kind == "x":
+                scaled(q, A("xt", 4 * (1 - h) + b, 1024, 8), A("xp", o + 1 - h, o + 256, 2), 0.03125)
+        quant("xq", 0, 256, "xt", 0)
+
+    mm(3, "vq", 0, "xq", 0, 128)
+    mm(2, "vq", 0, "xq", 128, 128)
+    outs.append(dma("y", lambda: g.sync.dma_start(T.oc[:], T.xq[:].bitcast(dt.uint8)), [A("xq", 0, 256)], []))
+    act(A("lsb", 0, 256), A("tbl", 0, 320), ACT.Copy, off=A("ll", 0, 16))
+    vtt(A("fq", 0, 128), A("kr", 0, 128), A("qrow", 0, 128), ALU.subtract)
+    for k in range(4):
+        outs.append(dma("y", lambda k=k: g.sync.dma_start(T.osc[4 * k:4 * k + 4, :], T.xqs[32 * k:32 * k + 4, :]),
+                        [A("xqs", 0, 256)], []))
+    scaled("v", A("yb", 0, 128), A("ps", 1536, 1664), 1.0)
+    scaled("s", A("yb", 128, 256), A("ps", 1024, 1152), 1.0)
+    vts(A("lsb", 256, 384), A("fq", 0, 128), 0.0078125, -64.0, ALU.mult, ALU.add)
+    outs.append(dma("y", lambda: g.sync.dma_start(T.y[:, 0:128], T.yb[:, 0:128]), [A("yb", 0, 128)], []))
+    outs.append(dma("s", lambda: g.scalar.dma_start(T.y[:, 128:256], T.yb[:, 128:256]), [A("yb", 128, 256)], []))
+    outs.append(dma("y", lambda: g.sync.dma_start(T.ls[:], T.lsb[0:128:16, :]), [A("lsb", 0, 384)], []))
+    op("g", lambda: g.wait_ge(T.sem.lsent, sent[0]), [], [], outs)
+
+    pools = {False: [["c%d" % i, 0, None] for i in range(NCS)], True: [["d%d" % i, 0, None] for i in range(NDS)]}
+    for i, o in enumerate(ops):
+        if o["q"] is None:
+            o["at"] = o["ext"]
+            continue
+        for w in o["waits"]:
+            Q[o["q"]].wait_ge(T.sem[ops[w]["at"][0]], ops[w]["at"][1])
+        ins = o["fn"]()
+        if o.get("sig"):
+            s = [p for p in pools[o["dma"]] if p[2] is None or o["ki"] >> p[2] & 1][0]
+            inc = 16 if o["dma"] else 1
+            s[1] += inc
+            s[2] = i
+            ins.then_inc(T.sem[s[0]], inc)
+            o["at"] = (s[0], s[1])

@@ -6,13 +6,13 @@ ACT = ActivationFunctionType
 R = 3
 BIG = 1.0e29
 F8 = "float8_e4m3fn_x4"
+UP, DOWN, TINY = 2.0 ** 21, 2.0 ** -51, 2.0 ** -20
 K = {
     "su": 9,
     "vs": 14,
     "ks": 5,
-    "blend": "g20s g22v g21s b22v a22v e22v b20v g23s a21v b21v o21v a20v o22s a23v o20s b23v e20s o23v e23v e21s "
-             "q00v q10v m01t m00t p01v m02t p00v m11t x01s m10t p02v x00s m13t p11v m03t x02s p10v m12t x11s p03v "
-             "x10s p13v x03s p12v x13s x12v",
+    "gv": 80,
+    "sv": 96,
 }
 
 
@@ -32,26 +32,28 @@ SCRATCH = {
     "ft": _s(2816, "bfloat16"), "fc": _s(704, F8), "fcs": _s(704, "uint8"),
     "xq": _s(256, F8), "xqs": _s(256, "uint8"), "zq": _s(256, F8), "zqs": _s(256, "uint8"),
     "qa": _s(128 * R, F8), "qas": _s(128 * R, "uint8"), "aland": _s(128 * R, F8), "alands": _s(128 * R, "uint8"),
-    "xp": _s(1024, "bfloat16"), "vh": _s(1280, "bfloat16"), "gg": _s(1024, "bfloat16"),
-    "zt": _s(1024, "bfloat16"), "za": _s(1024, "bfloat16"), "zb": _s(1024, "bfloat16"), "at": _s(512, "bfloat16"),
+    "x32": _s(1024, "bfloat16"), "vh": _s(1280, "bfloat16"), "gg": _s(1024, "bfloat16"),
+    "zt": _s(1024, "bfloat16"), "z32": _s(1024, "bfloat16"), "at": _s(512, "bfloat16"),
     "d1": _s(256, "float32"), "hs": _s(256, "float32"), "ssend": _s(16 * R, "float32"), "sland": _s(32 * R, "float32"),
-    "nes": _s(256, "bfloat16"), "base": _s(16, "float32"), "acc": _s(16, "float32"), "r1": _s(16, "float32"),
-    "cm": _s(256, "bfloat16"), "ce": _s(256, "bfloat16"), "sg": _s(2048, "bfloat16"), "jk": _s(2048, "bfloat16"),
+    "nes": _s(256, "bfloat16"), "base": _s(16, "float32"), "acc": _s(16, "float32"),
+    "lat": _s(256, "float32"), "la": _s(256, "bfloat16"), "lb": _s(256, "bfloat16"), "ce": _s(256, "float32"),
+    "sg": _s(2048, "bfloat16"), "jk": _s(2048, "bfloat16"),
     "cmp": _s(2048, "bfloat16"), "scn": _s(2048, "bfloat16"), "pc": _s(2560, "bfloat16"),
-    "rk": _s(16, "float32"), "roff": _s(16, "uint16"),
-    "ob": _s(288, "bfloat16"), "tb": _s(544, "bfloat16"), "tw": _s(544, "bfloat16"), "lw": _s(16, "float32"),
-    "lf": _s(16, "float32"), "ol": _s(16, "uint16"), "ll": _s(16, "uint16"),
+    "roff": _s(16, "uint16"), "ob": _s(256, "bfloat16"), "oh": _s(256, "bfloat16"), "ol": _s(64, "uint16"),
+    "m4": _s(256, "bfloat16"), "m16": _s(256, "bfloat16"), "c4": _s(12, "float32"),
+    "wh": _s(256, "bfloat16"), "ch": _s(256, "bfloat16"), "lw": _s(64, "float32"), "lf": _s(64, "float32"),
+    "ll": _s(64, "uint16"), "wi": _s(256, "bfloat16"), "ci": _s(256, "bfloat16"), "lx": _s(16, "float32"),
+    "lg": _s(16, "float32"), "lk": _s(16, "uint16"),
     "pt": _s(288, "bfloat16"), "pp": _s(288, "bfloat16"), "pm": _s(14, "float32"),
     "fsend": _s(16 * R, "bfloat16"), "fland": _s(32 * R, "bfloat16"),
-    "kx": _s(128, "float32"), "kr": _s(128, "float32"), "ko": _s(16, "float32"),
+    "kx": _s(128, "float32"), "kr": _s(130, "float32"), "ko": _s(16, "float32"),
     "xl": _s(8, "uint16"), "kl": _s(2, "uint16"), "lj": _s(8, "int32"),
-    "pa": _s(8, "float32"), "pb": _s(8, "float32"), "ksum": _s(8, "float32"), "pl": _s(8, "float32"),
-    "poff": _s(8, "uint16"), "wb": _s(336, "bfloat16"), "nf": _s(256, "bfloat16"), "cu": _s(288, "bfloat16"),
-    "i1": _s(256, "int32"), "i2": _s(256, "int32"), "negm": _s(256, "float32"), "hold": _s(256, "float32"),
-    "m01": _s(256, "bfloat16"), "alt": _s(512, "bfloat16"),
+    "pa": _s(16, "float32"), "pb": _s(16, "float32"), "ksum": _s(8, "float32"),
+    "poff": _s(8, "uint16"), "wb": _s(320, "bfloat16"), "cu": _s(256, "bfloat16"),
+    "negm": _s(256, "float32"), "hold": _s(256, "float32"), "r16": _s(256, "bfloat16"),
     "seg": _s(512, "bfloat16"), "cc": _s(16, "float32"), "jd": _s(256, "bfloat16"),
-    "pi": _s(8, "int32"), "pf": _s(8, "float32"), "li": _s(16, "int32"),
-    "tl": _s(2, "uint16"), "cl": _s(2, "uint16"), "el": _s(16, "uint16"), "rl": _s(8, "uint16"),
+    "pi": _s(16, "int32"), "pf": _s(24, "float32"), "li": _s(16, "int32"),
+    "cl": _s(2, "uint16"), "el": _s(16, "uint16"), "rl": _s(8, "uint16"),
     "keyc": _s(128, "float32"), "qown": _s(16, "float32"), "ids": _s(128, "bfloat16"), "qrow": _s(128, "float32"),
     "tbl": _s(320, "float32"), "lsb": _s(384, "float32"), "fq": _s(128, "float32"), "yb": _s(256, "float32"),
 }
@@ -150,15 +152,19 @@ def rank_program(g, core, T, topo):
     def vscatter(win, off, in_):
         return op("v", lambda: g.vector.tensor_copy(ap(win).indirect(ap(off)), ap(in_)), [in_, off], [win])
 
-    def vscan(out, d0, d1, o0, o1, init=None):
-        return op("v", lambda: g.vector.tensor_tensor_scan(ap(out), ap(d0), ap(d1), ap(init) if init else 0.0, o0, o1),
-                  [d0, d1] + ([init] if init else []), [out])
+    def vscan(out, d0, d1, o0, o1, init=0.0):
+        return op("v", lambda: g.vector.tensor_tensor_scan(ap(out), ap(d0), ap(d1), ap(init) if isap(init) else init,
+                                                           o0, o1),
+                  [d0, d1] + ([init] if isap(init) else []), [out])
 
-    def vsum(out, d):
-        return vscan(out, d, d, ALU.add, ALU.max)
+    def vsum(out, d, init=0.0):
+        return vscan(out, d, d, ALU.add, ALU.max, init)
 
-    def vseg(out, d, mask="seg"):
-        return vscan(out, A(mask, 0, out[2] - out[1]), d, ALU.mult, ALU.add)
+    def vseg(out, d):
+        return vscan(out, A("seg", 0, out[2] - out[1]), d, ALU.mult, ALU.add)
+
+    def vhold(out, row, mask):
+        return vscan(out, row, A(mask, 0, out[2] - out[1]), ALU.max, ALU.mult)
 
     def vtr(out, in_):
         return op("v", lambda: g.vector.transpose(ap(out), ap(in_)), [in_], [out])
@@ -171,7 +177,7 @@ def rank_program(g, core, T, topo):
         return op("v", lambda: g.vector.quantize_mx(ap(o), ap(s), ap(t)), [t], [o, s])
 
     def act(out, in_, func, bias=None, scale=None, acc=None, off=None, after=()):
-        rd = [in_] + [s for s in (bias, off) if isap(s)]
+        rd = [in_] + [s for s in (bias, scale, off) if isap(s)]
         kw = {}
         if bias is not None:
             kw["bias"] = bias
@@ -275,89 +281,77 @@ def rank_program(g, core, T, topo):
     dma("s", lambda: g.scalar.dma_start(T.ut[:], T.u[:]), [], [A("ut", 0, 512)])
     xin = [dma("y", lambda h=h: g.sync.dma_start(T.xin[:, 512 * h:512 * h + 512], T.x[:, 512 * h:512 * h + 512]),
                [], [A("xin", 512 * h, 512 * h + 512)]) for h in range(2)]
-    dma("y", lambda: g.sync.dma_start(T.wq[:].bitcast(dt.uint8), T.wc[:]), [], [A("wq", 0, 512)], xin)
-    dma("y", lambda: g.sync.dma_start(T.wqs[:], T.ws[:]), [], [A("wqs", 0, 512)])
-    dma("y", lambda: g.sync.dma_start(T.vt[:], T.v[:]), [], [A("vt", 0, 512)])
 
-    FT = [0, 1024, 1792, 2304, 2816]
+    FT = [0, 1024, 1792, 2304, 2560]
+    pi = lambda k, m=1: A("pi", k, k + m)
+    pf = lambda k, m=1: A("pf", k, k + m)
+    iota(pi(0, 2), [[12, 2]], 0, 1, True)
     iota(A("li", 0, 16), [[1, 16]], 0, 0, True)
-    iota(A("pi", 0, 1), [[0, 1]], 0, 1, True)
-    iota(A("i1", 0, 256), [[0, 16], [1, 16]], 128, -1, True)
+    iota(A("g1", 0, 512), [[1, 8], [0, 64]], 0, 0)
     vset(A("ones", 0, 512), 1.0)
-    select(A("g1", 0, 512), A("ones", 0, 512), [[16, 8], [0, 64]], ALU.is_ge, 15, -1)
-    select(A("g2", 0, 512), A("g1", 0, 512), [[-16, 8], [0, 64]], ALU.is_ge, 0, 1)
-    vset(A("hold", 0, 256), 0.0)
     vset(A("seg", 0, 512), 1.0)
-    vset(A("hold", 0, 256, 16), -5 * BIG)
+    vts(pi(4, 2), pi(0, 2), 15, None, ALU.bitwise_and)
     vset(A("seg", 0, 512, 16), 0.0)
+    vts(pi(6), pi(0), 4, None, ALU.logical_shift_right)
     vts(A("rl", 0, 8), A("li", 0, 8), 16.0, None, ALU.mult)
+    vset(A("hold", 0, 256), 0.0)
+    vts(pi(8, 2), pi(4, 2), 2, None, ALU.logical_shift_right)
+    vts(pf(0), pi(4), 1.0, None, ALU.add)
+    vseg(A("r16", 0, 256), A("ones", 0, 256))
+    vset(A("hold", 0, 256, 16), -5 * BIG)
+    vts(A("cl", 0, 1), pi(4), 16.0, 112.0, ALU.mult, ALU.min)
+    vcopy(pf(1), pi(4))
+    vcopy(pf(2, 2), pi(8, 2))
+    vts(A("negm", 0, 256), A("r16", 0, 256), pf(0), -BIG, ALU.not_equal, ALU.mult)
+    vcopy(pf(4), pi(6))
     vcopy(A("el", 0, 16), A("li", 0, 16))
-    vts(A("pi", 2, 3), A("pi", 0, 1), 15, None, ALU.bitwise_and)
-    vts(A("pi", 4, 5), A("pi", 0, 1), 4, None, ALU.logical_shift_right)
-    vts(A("i2", 0, 256), A("i1", 0, 256), 15, None, ALU.bitwise_and)
-    vts(A("cl", 0, 1), A("pi", 2, 3), 16.0, 112.0, ALU.mult, ALU.min)
-    vtt(A("pi", 5, 6), A("pi", 4, 5), A("pi", 0, 1), ALU.add)
-    vts(A("negm", 0, 256), A("i2", 0, 256), 0.0, -BIG, ALU.not_equal, ALU.mult)
-    for a, e in ((0, 208), (1, 144), (2, 80), (3, 16)):
+    vts(pi(10), pi(0), 3, None, ALU.bitwise_and)
+    vts(A("la", 0, 256), A("r16", 0, 256), pf(0), -1024.0, ALU.is_equal, ALU.mult)
+    vts(A("lb", 0, 256), A("r16", 0, 256), pf(1), 2048.0, ALU.is_equal, ALU.mult)
+    for a, e in ((0, 208), (1, 144), (2, 80)):
         zero(A("ft", FT[a] + 4 * e, FT[a + 1]))
+    zero(A("ft", FT[3] + 64, FT[4] + 256))
+    for b in range(4):
+        zero(A("et", 512 * b, 512 * b + 512))
 
     quant("uq", 0, 128, "ut", 0)
     pick("ur0", "uq", 128, A("rl", 0, 8))
+    quant("xq", 0, 128, "xin", 0)
     pick("upk", "uq", 128, A("cl", 0, 1))
-    act(A("m01", 0, 256), A("negm", 0, 256), ACT.Relu, bias=1.0, scale=10.0 / BIG)
-    for a in (A("ob", 0, 16), A("ob", 272, 288), A("at", 256, 512), A("cu", 0, 16), A("cu", 272, 288),
-              A("pc", 15, 256, 16), A("pc", 2319, 2560, 16), A("acc", 0, 1)):
+    quant("xq", 128, 256, "xin", 512)
+    for a in (A("at", 256, 512), A("pc", 15, 256, 16), A("pc", 2319, 2560, 16), A("acc", 0, 1)):
         zero(a)
-    for h in range(2):
-        quant("xq", 128 * h, 128 * h + 128, "xin", 512 * h)
     send(A("upk", 0, 8), [(s, A("uland", 8 * j, 8 * j + 8)) for j, s in enumerate(back(rank))], True, ["au", "au"])
     send(A("upks", 0, 8), [(s, A("ulands", 8 * j, 8 * j + 8)) for j, s in enumerate(back(rank))], False, ["au", "au"])
-
-    def turn(dst, row, which):
-        if which == 0:
-            vtr(A(dst, 0, 256), A(row, 16, 272))
-        else:
-            vtr(A(dst, 256, 544), A(row, 0, 288))
 
     def flags(c):
         a, e = (0, 16 - c) if c > 12 else (1 + (12 - c) // 4, (12 - c) % 4)
         return A("ft", FT[a] + e, FT[a] + 64 * c, 4)
 
-    SU, VS, KS = K["su"], K["vs"], K["ks"]
+    SU, VS, KS, GV, SV = K["su"], K["vs"], K["ks"], K["gv"], K["sv"]
     at16 = lambda c: 8 * c * (c - 1)
     outs = []
 
     for t in range(R):
         first, last = t == 0, t == R - 1
-        xs = 1.0 if first else 0.03125
+        X = A("xin" if first else "xt", 0, 1024)
 
         mm(0, "ur0", 0, "xq", 0, 256)
         mm(1, "ur0", 0, "xq", 0, 256)
         if first:
-            vts(A("pi", 6, 7), A("pi", 5, 6), 1, None, ALU.bitwise_and)
-            vts(A("pf", 0, 1), A("pi", 2, 3), 16.0, None, ALU.mult)
-            vts(A("pf", 2, 3), A("pi", 2, 3), -1.0, 15.0, ALU.mult, ALU.add)
-            vts(A("tl", 0, 1), A("pi", 6, 7), 272.0, A("pf", 0, 1), ALU.mult, ALU.add)
-        vtt(A("d1", 0, 256), A("ps", 0, 256), A("negm", 0, 256), ALU.add)
-        if first:
-            vts(A("cc", 0, 16), A("li", 0, 16), 16.0, A("pf", 2, 3), ALU.mult, ALU.add)
-        vscan(A("hs", 0, 256), A("hold", 0, 256), A("d1", 0, 256), ALU.add, ALU.max)
+            vtt(A("lat", 0, 256), A("la", 0, 256), A("lb", 0, 256), ALU.add)
+        cut = 16 * SU + 16
+        for a, b in ((0, cut), (cut, 256)):
+            vtt(A("d1", a, b), A("ps", a, b), A("negm", a, b), ALU.add)
+        for a, b in ((0, cut), (cut, 256)):
+            vscan(A("hs", a, b), A("hold", a, b), A("d1", a, b), ALU.add, ALU.max)
         own = lambda c: A("hs", 16 * c + 15, 16 * c + 16)
-        act(A("ssend", 16 * t, 16 * t + 16), A("hs", 15, 256, 16), ACT.Copy)
-        send(A("ssend", 16 * t, 16 * t + 16),
-             [(s, A("sland", 32 * t + 16 * j, 32 * t + 16 * j + 16)) for j, s in enumerate(back(rank))],
-             False, ["sa%d" % t, "sb%d" % t])
-        if first:
-            iota(A("jd", 0, 256), [[1, 256]], 0, 0)
-            for b in range(4):
-                select(A("et", 512 * b, 512 * b + 512), A("ones", 0, 512), [[8, 128], [1, 4]], ALU.is_equal, -b, -8)
-        if t == 1:
-            iota(A("qrow", 0, 128), [[1, 128]], 0, 0)
-            iota(A("tbl", 0, 128), [[1, 128]], 256, 0)
 
-        def on_scalar(cs):
+        def signs(cs):
             for c in cs:
                 act(A("sg", at16(c), at16(c) + 16 * c), A("ps", 512, 512 + 16 * c), ACT.Sign, bias=own(c), scale=-1.0)
+
+        def sums(cs):
             for c in cs:
                 act(flags(c), A("sg", at16(c), at16(c) + 16 * c), ACT.Relu, acc=A("acc", c, c + 1))
 
@@ -365,52 +359,82 @@ def rank_program(g, core, T, topo):
             for c in cs:
                 vts(flags(c), A("ps", 0, 16 * c), own(c), None, ALU.is_lt)
 
-        on_scalar(range(SU, 4, -1))
-        on_scalar(range(4, 0, -1))
+        signs(range(SU, 4, -1))
+        act(A("ssend", 16 * t, 16 * t + 16), A("hs", 15, 256, 16), ACT.Copy)
+        send(A("ssend", 16 * t, 16 * t + 16),
+             [(s, A("sland", 32 * t + 16 * j, 32 * t + 16 * j + 16)) for j, s in enumerate(back(rank))],
+             False, ["sa%d" % t, "sb%d" % t])
+        if first:
+            for b in range(4):
+                select(A("et", 512 * b + b, 512 * b + 512, 4), A("ones", 0, 128), [[1, 128]], ALU.is_equal, 0, -1)
+        if t == 1:
+            iota(A("qrow", 0, 128), [[1, 128]], 0, 0)
+            iota(A("tbl", 0, 128), [[1, 128]], 256, 0)
+        sums(range(SU, 4, -1))
+        signs(range(4, 0, -1))
+        sums(range(4, 0, -1))
+        if first:
+            vts(A("g2", 0, 512), A("g1", 0, 512), pf(4), None, ALU.is_equal)
         vtt(A("ft", 0, 1024, 4), A("ps", 0, 256), A("hs", 0, 256), ALU.is_le)
         on_vector([15, 14, 13, 12])
-        quant("fc", 0, 256, "ft", FT[0])
         if first:
             quant("gq", 0, 128, "g2", 0)
+        quant("fc", 0, 256, "ft", FT[0])
         grp = mm(3, "gq", 0, "fc", 0, 256, stop=False)
         on_vector(range(11, SU, -1))
+        if first:
+            vts(pf(5), pf(1), -1.0, 15.0, ALU.mult, ALU.add)
+            vts(pf(6), pf(1), 0.0, 2048.0, ALU.is_equal, ALU.mult)
+            vts(pf(7), pf(1), 15.0, -1024.0, ALU.is_equal, ALU.mult)
         vseg(A("nes", 0, 256), A("ft", 0, 1024, 4))
+        if first:
+            vts(pf(8), pf(5), pf(6), pf(7), ALU.add, ALU.add)
+            vts(pf(9), pf(6), -1.0, 1024.0, ALU.mult, ALU.add)
+            vsum(A("jd", 0, 256), A("ones", 0, 256))
+            vts(A("cc", 0, 16), A("li", 0, 16), 16.0, pf(8), ALU.mult, ALU.add)
         quant("fc", 256, 448, "ft", FT[1])
         grp = mm(3, "gq", 0, "fc", 256, 192, start=False, stop=False, group=grp)
         vtt(A("base", 0, 16), A("cc", 0, 16), A("nes", 15, 256, 16), ALU.subtract)
-        quant("fc", 448, 576, "ft", FT[2])
+        quant("fc", 448, 704 if first else 640, "ft", FT[2])
         grp = mm(3, "gq", 0, "fc", 448, 128, start=False, stop=False, group=grp)
-        quant("fc", 576, 704, "ft", FT[3])
         mm(3, "gq", 0, "fc", 576, 128, start=False, group=grp)
         for c in range(VS - 1, SU, -1):
             act(A("jk", at16(c), at16(c) + 16 * c), flags(c), ACT.Copy, acc=A("acc", c, c + 1))
         ends = lambda c: 256 * (c - VS) + 256
-        for c in range(15, VS, -1):
+        for c in range(15, VS - 1, -1):
             vsum(A("scn", ends(c) - 16 * c, ends(c)), flags(c))
-        vtt(A("cm", 0, 256), A("ps", 1536, 1792), A("m01", 0, 256), ALU.mult)
-        if VS < 16:
-            vsum(A("scn", ends(VS) - 16 * VS, ends(VS)), flags(VS))
-        vseg(A("ce", 0, 256), A("cm", 0, 256))
-        if VS < 16:
-            vtt(A("r1", VS, 16), A("base", VS, 16), A("scn", 255, ends(15), 256), ALU.subtract)
-        vtt(A("r1", 0, VS), A("base", 0, VS), A("acc", 0, VS), ALU.subtract)
-        vtt(A("rk", 0, 16), A("r1", 0, 16), A("ce", 15, 256, 16), ALU.add)
-        vcopy(A("roff", 0, 16), A("rk", 0, 16))
         if first:
-            for b in range(4):
-                act(A("xp", 256 * b, 256 * b + 256), A("xin", b, 1024, 4), ACT.Copy)
-        vscatter(A("ob", 16, 272), A("roff", 0, 16), A("jd", 0, 256))
+            vts(A("c4", 0, 4), A("li", 0, 4), pf(2), UP, ALU.is_equal, ALU.mult)
+            vts(A("c4", 4, 8), A("li", 0, 4), pf(3), DOWN, ALU.not_equal, ALU.max)
+            vts(pf(10), pf(2), 0.0, 4.0 / (UP * DOWN), ALU.is_equal, ALU.mult)
+            vts(pf(12), pi(10), -4.0, None, ALU.add)
+            vtt(A("c4", 8, 12), A("c4", 0, 4), A("c4", 4, 8), ALU.max)
+            vts(pf(11), pf(10), 4.0 / UP, None, ALU.max)
+            for j in range(4):
+                act(A("m4", j, 256, 4), A("ones", 0, 64), ACT.Copy, scale=A("c4", 8 + j, 9 + j))
+        if VS < 16:
+            vtt(A("lat", 16 * VS + 15, 256, 16), A("base", VS, 16), A("scn", 255, ends(15), 256), ALU.subtract)
+        vtt(A("lat", 15, 16 * VS, 16), A("base", 0, VS), A("acc", 0, VS), ALU.subtract)
+        vscan(A("ce", 0, 256), A("ps", 1536, 1792), A("lat", 0, 256), ALU.min, ALU.add, 4096.0)
+        vts(A("roff", 0, 16), A("ce", 15, 256, 16), pf(9), None, ALU.add)
+        if first:
+            dma("y", lambda: g.sync.dma_start(T.wq[:].bitcast(dt.uint8), T.wc[:]), [A("ce", 0, 1)], [A("wq", 0, 512)])
+            dma("y", lambda: g.sync.dma_start(T.wqs[:], T.ws[:]), [], [A("wqs", 0, 512)])
+        if t == 1:
+            dma("y", lambda: g.sync.dma_start(T.vt[:], T.v[:]), [A("ce", 0, 1)], [A("vt", 0, 512)])
+        vscatter(A("ob", 0, 256), A("roff", 0, 16), A("jd", 0, 256))
         if first:
             au = ext("au", 2 * sum(nback))
             pick("ur1", "uland", 16, A("el", 0, 8), [au])
-        turn("tb", "ob", 0)
-        turn("tb", "ob", 1)
-        vts(A("ol", 0, 16), A("tb", 0, 544), 0.0, None, ALU.add, off=A("tl", 0, 1))
+
+        vhold(A("oh", 0, 64), A("ob", 0, 64), "m4")
         if first:
             pick("ur2", "uland", 16, A("el", 8, 16), [au])
-
-        for b in (0, 2, 1, 3):
-            scaled("v" if b < 2 else "s", A("at", b, 256, 4), A("xp", 256 * b, 256 * b + 256), xs, A("ol", 0, 4))
+        vts(A("ol", 0, 16), A("oh", 3, 64, 4), pf(11), pf(12), ALU.mult, ALU.add)
+        vhold(A("oh", 64, 256), A("ob", 64, 256), "m4")
+        scaled("s", A("at", 128, 256), X, 1.0, A("ol", 8, 16))
+        scaled("v", A("at", 0, 128), X, 1.0, A("ol", 0, 8))
+        vts(A("ol", 16, 64), A("oh", 67, 256, 4), pf(11), pf(12), ALU.mult, ALU.add)
         quant("qa", 128 * t, 128 * t + 128, "at", 0)
         mm(1, "ur1", 0, "qa", 128 * t, 128)
         mm(0, "ur2", 0, "qa", 128 * t, 128)
@@ -422,7 +446,7 @@ def rank_program(g, core, T, topo):
                 op("g", send1(a, r, land(to, rank, r), codes, "aa%d" % t, topo.engines(core, cores[r])), [a], [])
             else:
                 send(a, [(r, land(to, rank, r)) for r in fwd(rank)], codes, ["aa%d" % t] * 2)
-        vset(A("wb", 0, 336), 256.0)
+        vset(A("wb", 0, 320), 1.0)
 
         e1, e2 = ext("sa%d" % t, nback[0]), ext("sb%d" % t, nback[1])
         for c in range(16):
@@ -440,7 +464,7 @@ def rank_program(g, core, T, topo):
         vtr(A("pt", 128, 288), A("pc", 15, 2560, 16))
         vseg(A("pp", 0, 288), A("pt", 0, 288))
         vtt(A("pm", 0, 14), A("pp", 15, 224, 16), A("pp", 79, 288, 16), ALU.max)
-        vts(A("fsend", 16 * t, 16 * t + 14), A("pm", 0, 14), 64.0, 128.0, ALU.max, ALU.mult)
+        vts(A("fsend", 16 * t, 16 * t + 14), A("pm", 0, 14), 64.0, -192.0, ALU.max, ALU.add)
         place = lambda r: 32 * t + 14 * slot(rank, r)
         send(A("fsend", 16 * t, 16 * t + 14), [(r, A("fland", place(r), place(r) + 14)) for r in fwd(rank)], False,
              ["af%d" % t] * 2)
@@ -454,105 +478,121 @@ def rank_program(g, core, T, topo):
             r = fwd(s)[1]
             for name, codes in (("aland", True), ("alands", False)):
                 op("g", send1(land(name, s, rank), r, land(name, s, r), codes, "aa%d" % t, inner(rank)), [], [], [aa])
+        scaled("s", A("vh", 512 + 4 * SV, 1280), X, 0.5, A("ol", 16 + SV // 4, 64))
         if first:
-            iota(A("ids", 0, 128), [[1, 128]], -127, 0)
-            iota(A("alt", 0, 256), [[0, 128], [1, 2]], 0, 0)
-            iota(A("alt", 256, 512), [[0, 128], [-1, 2]], 1, 0)
             quant("eq", 0, 512, "et", 0)
+            vts(pi(11), pi(0), 31, None, ALU.bitwise_and)
+            vtt(pi(12), pi(6), pi(0), ALU.add)
+            vts(pi(13), pi(0), 4, None, ALU.bitwise_and)
+            vts(pf(19), pf(1), 0.0078125, None, ALU.mult)
+            vcopy(pf(13), pi(11))
+            vts(pi(14), pi(12), 1, None, ALU.bitwise_and)
+            vcopy(A("xl", 0, 8), A("lj", 0, 8))
+            vts(pf(14), pi(13), 3.5, pf(12), ALU.mult, ALU.add)
+            vts(A("keyc", 0, 128), A("fq", 0, 128), pf(13), 0.0078125, ALU.add, ALU.mult)
+            vset(A("kr", 128, 130), -1024.0)
+            vts(A("qown", 0, 16), A("li", 0, 16), 0.125, pf(19), ALU.mult, ALU.add)
+            vts(pf(15), pi(14), 9.0, 4.0, ALU.mult, ALU.add)
+            vts(pf(16), pf(2), 0.0, -128.0 * UP, ALU.not_equal, ALU.mult)
+            vts(pf(18), pf(12), 512.0, None, ALU.add)
+            vts(A("kl", 0, 1), pf(15), pf(14), None, ALU.add)
+            vts(pf(17), pf(16), -128.0 * UP * DOWN, None, ALU.min)
+            scaled("s", A("ids", 0, 128), A("jd", 0, 128), TINY)
         for b in range(4):
             mm(4 + b, "eq", 128 * b, "aland", 128 * t, 128, [aa])
-        for b in (2, 0, 3, 1):
-            scaled("v" if b < 2 else "s", A("vh", 320 * b + 128, 320 * b + 320), A("xp", 256 * b, 256 * b + 256),
-                   16.0 * xs, A("ol", 4, 16))
-        if first:
-            vts(A("pi", 1, 2), A("pi", 0, 1), 31, None, ALU.bitwise_and)
-            vcopy(A("pf", 1, 2), A("pi", 2, 3))
-            vts(A("pi", 3, 4), A("pi", 0, 1), 3, None, ALU.bitwise_and)
-            vts(A("pi", 7, 8), A("pi", 0, 1), 4, None, ALU.bitwise_and)
-            vcopy(A("pf", 5, 6), A("pi", 1, 2))
-            vts(A("qown", 0, 16), A("li", 0, 16), 16.0, A("pf", 1, 2), ALU.mult, ALU.add)
-            vcopy(A("pf", 3, 4), A("pi", 3, 4))
-            vcopy(A("xl", 0, 8), A("lj", 0, 8))
-            vts(A("keyc", 0, 128), A("fq", 0, 128), A("pf", 5, 6), None, ALU.add)
-            vts(A("pf", 4, 5), A("pi", 7, 8), 3.5, A("pf", 3, 4), ALU.mult, ALU.add)
-            vts(A("kl", 0, 1), A("pi", 6, 7), 9.0, A("pf", 4, 5), ALU.mult, ALU.add)
+        scaled("v", A("vh", 512, 512 + 4 * SV), X, 0.5, A("ol", 16, 16 + SV // 4))
         if t == 1:
             quant("vq", 0, 128, "vt", 0)
+            vts(pf(19), pf(1), 0.0, 16.0, ALU.is_equal, ALU.mult)
+            vts(A("la", 0, 256), A("r16", 0, 256), pf(0), UP, ALU.is_equal, ALU.mult)
+            vts(pf(21), pf(1), 0.0, -128.0 * UP, ALU.not_equal, ALU.mult)
+            vts(pf(20), pf(19), pf(1), None, ALU.add)
+            vts(pf(23), pf(19), 1.0 / (16.0 * UP * DOWN), 1.0 / UP, ALU.mult, ALU.max)
+            vts(pf(22), pf(21), -128.0 * UP * DOWN, None, ALU.min)
+            vts(A("lb", 0, 256), A("r16", 0, 256), pf(20), DOWN, ALU.not_equal, ALU.max)
+            vtt(A("m16", 0, 256), A("la", 0, 256), A("lb", 0, 256), ALU.max)
+            act(A("fq", 0, 128), A("qrow", 0, 128), ACT.Identity, bias=128.0, scale=-0.0078125)
         if last:
-            act(A("tbl", 128, 320), A("ob", 80, 272), ACT.Copy)
+            act(A("tbl", 128, 320), A("ob", 64, 256), ACT.Identity, bias=-1.0)
 
         af = ext("af%d" % t, nfwd)
         came = A("fland", 32 * t, 32 * t + 28)
         vtt(A("kx", 0, 128), came, A("keyc", 0, 128), ALU.add, off=A("xl", 0, 8), after=[af])
         vtt(A("ko", 0, 16), came, A("qown", 0, 16), ALU.add, off=A("kl", 0, 1), after=[af])
+        vts(A("pb", 0, 16), came, 63.0, None, ALU.min, off=A("kl", 0, 1))
         vtr(A("kr", 0, 128), A("kx", 0, 128))
+        vts(A("pa", 0, 16), came, 63.0, 192.0, ALU.min, ALU.add, off=A("kl", 0, 1))
         kown = lambda c: A("ko", c, c + 1)
         for c in range(KS):
-            act(A("jk", 128 * c, 128 * c + 128), A("kr", 0, 128), ACT.Sign, bias=kown(c), scale=-1.0,
+            act(A("jk", 256 * c, 256 * c + 129), A("kr", 0, 129), ACT.Sign, bias=kown(c), scale=-1.0,
                 acc=A("ksum", c, c + 1))
+        for c in range(KS, 8):
+            vts(A("cmp", 128 * c, 128 * c + 128), A("kr", 0, 128), kown(c), None, ALU.is_lt)
+        placed = lambda c: vts(A("poff", c, c + 1), A("ksum", c, c + 1), 0.5, A("pa", c, c + 1), ALU.mult, ALU.add)
+        for c in range(KS, 8):
+            vscan(A("scn", 128 * c, 128 * c + 128), A("cmp", 128 * c, 128 * c + 128), A("ones", 0, 128),
+                  ALU.add, ALU.mult, A("pb", c, c + 1))
+        for c in range(KS - 1):
+            placed(c)
+        vts(A("poff", KS, 8), A("scn", 128 * KS + 127, 1024, 128), 129.0, None, ALU.add)
+        placed(KS - 1)
+        vscatter(A("wb", 0, 320), A("poff", 0, 8), A("ids", 0, 128))
         for b in range(4):
-            act(A("vh", 320 * b, 320 * b + 128), A("ps", 2048 + 512 * b, 2048 + 512 * b + 128), ACT.Copy, scale=16.0)
-        for c in range(KS, 8):
-            vts(A("cmp", 128 * c, 128 * c + 128), A("kr", 0, 128), kown(c), 2.0, ALU.is_lt, ALU.mult)
-        vtt(A("pa", 0, 8), A("ko", 0, 8), A("qown", 0, 8), ALU.subtract)
-        for c in range(KS, 8):
-            vsum(A("scn", 128 * c, 128 * c + 128), A("cmp", 128 * c, 128 * c + 128))
-            if c == KS:
-                vts(A("pb", 0, 8), A("pa", 0, 8), 0.015625, 510.0, ALU.mult, ALU.min)
-        vtt(A("pl", KS, 8), A("scn", 128 * KS + 127, 1024, 128), A("pb", KS, 8), ALU.add)
-        vtt(A("pl", 0, KS), A("ksum", 0, KS), A("pb", 0, KS), ALU.add)
-        vts(A("poff", KS, 8), A("pl", KS, 8), -126.0, 0.5, ALU.add, ALU.mult)
-        vts(A("poff", 0, KS), A("pl", 0, KS), 1.0, 0.5, ALU.add, ALU.mult)
-        vscatter(A("wb", 16, 336), A("poff", 0, 8), A("ids", 0, 128))
-        vts(A("nf", 0, 256), A("wb", 16, 272), 255.0, None, ALU.is_gt)
-        turn("tw", "wb", 0)
-        vsum(A("cu", 16, 272), A("nf", 0, 256))
-        turn("tw", "wb", 1)
-        act(A("lw", 0, 16), A("tw", 0, 544), ACT.Copy, off=A("tl", 0, 1))
-        turn("tb", "cu", 0)
-        turn("tb", "cu", 1)
-        vtt(A("lf", 0, 16), A("tb", 0, 544), A("lw", 0, 16), ALU.min, off=A("tl", 0, 1))
-        vts(A("ll", 0, 16), A("lf", 0, 16), 127.0, None, ALU.add)
+            act(A("vh", b, 512, 4), A("ps", 2048 + 512 * b, 2048 + 512 * b + 128), ACT.Copy, scale=0.5)
+        vsum(A("cu", 0, 256), A("wb", 0, 256))
+        vhold(A("wh", 0, 256), A("wb", 0, 256), "m4")
+        vhold(A("ch", 0, 256), A("cu", 0, 256), "m4")
+        vts(A("lw", 0, 64), A("wh", 3, 256, 4), 1.0 / TINY, pf(17), ALU.mult, ALU.add)
+        vtt(A("lf", 0, 64), A("ch", 3, 256, 4), A("lw", 0, 64), ALU.min)
+        vts(A("ll", 0, 64), A("lf", 0, 64), pf(11), pf(18), ALU.mult, ALU.add)
 
-        for word in K["blend"].split():
-            kind, h, b, q = word[0], int(word[1]), int(word[2]), word[3]
-            o = 256 * b
-            bank = 4 + b if h == 0 else (4 if b == 3 else b)
-            z32 = A("za", o + 1, o + 256, 2) if h == 0 else A("zb", o, o + 256, 2)
-            if kind == "g":
-                scaled(q, A("gg", o, o + 256), A("vh", 320 * b, 320 * b + 320), 1.0, A("ll", 0, 16))
-            elif kind == "a":
-                vseg(A("za", o, o + 256), A("gg", o, o + 256), "alt")
-            elif kind == "b":
-                vscan(A("zb", o, o + 256), A("alt", 256, 512), A("gg", o, o + 256), ALU.mult, ALU.add, A("gg", o, o + 1))
-            elif kind == "o":
-                scaled(q, A("zt", b, 512, 4), A("za", o + 1, o + 256, 2), 0.03125)
-            elif kind == "e":
-                scaled(q, A("zt", 512 + b, 1024, 4), A("zb", o, o + 256, 2), 0.03125)
-            elif kind == "q":
-                quant("zq", 128 * h, 128 * h + 128, "zt", 512 * h)
-            elif kind == "m":
-                mm(bank, "wq", 128 * b, "zq", 128 * h, 128)
-            elif kind == "p":
-                vtt(A("xp", o + 1 - h, o + 256, 2), A("ps", 512 * bank, 512 * bank + 128), z32, ALU.add)
-            elif kind == "x":
-                scaled(q, A("xt", 4 * (1 - h) + b, 1024, 8), A("xp", o + 1 - h, o + 256, 2), 0.03125)
-        quant("xq", 0, 256, "xt", 0)
+        V = A("vh", 0, 1280)
+        scaled("s", A("gg", 4 * GV, 512), V, 1.0, A("ll", GV // 4, 32))
+        scaled("v", A("gg", 0, 4 * GV), V, 1.0, A("ll", 0, GV // 4))
+        scaled("s", A("gg", 512, 1024), V, 1.0, A("ll", 32, 64))
+        if last:
+            vhold(A("wi", 0, 256), A("wb", 0, 256), "m16")
+        vtt(A("zt", 0, 4), A("gg", 0, 4), A("gg", 0, 4), ALU.add)
+        vtt(A("zt", 4, 512), A("gg", 4, 512), A("gg", 0, 508), ALU.add)
+        if last:
+            vhold(A("ci", 0, 256), A("cu", 0, 256), "m16")
+        bank = lambda h, b: 4 * (1 - h) + b
+        for h in range(2):
+            a, b = ((512, 768), (768, 1024))[h]
+            vtt(A("zt", a, b), A("gg", a, b), A("gg", a - 4, b - 4), ALU.add)
+            quant("zq", 128 * h, 128 * h + 128, "zt", 512 * h)
+            for b in range(4):
+                mm(bank(h, b), "wq", 128 * b, "zq", 128 * h, 128)
+            scaled("s", A("z32", 512 * h, 512 * h + 512), A("zt", 512 * h, 512 * h + 512), 32.0)
+        plane = lambda name, h, b: A(name, 512 * h + b, 512 * h + 512, 4)
+        for h in range(2):
+            for b in range(4):
+                vtt(plane("x32", h, b), A("ps", 512 * bank(h, b), 512 * bank(h, b) + 128), plane("z32", h, b), ALU.add)
+                if h == 1 and b < 1:
+                    scaled("s", plane("xt", h, b), plane("x32", h, b), 0.03125)
+            if h == 0:
+                scaled("s", A("xt", 0, 512), A("x32", 0, 512), 0.03125)
+        for b in range(1, 4):
+            scaled("v", plane("xt", 1, b), plane("x32", 1, b), 0.03125)
+        quant("xq", 0, 128, "xt", 0)
+        if last:
+            mm(4, "vq", 0, "xq", 0, 128)
+        quant("xq", 128, 256, "xt", 512)
 
-    mm(3, "vq", 0, "xq", 0, 128)
-    mm(2, "vq", 0, "xq", 128, 128)
+    mm(5, "vq", 0, "xq", 128, 128)
     outs.append(dma("y", lambda: g.sync.dma_start(T.oc[:], T.xq[:].bitcast(dt.uint8)), [A("xq", 0, 256)], []))
-    act(A("lsb", 0, 256), A("tbl", 0, 320), ACT.Copy, off=A("ll", 0, 16))
-    vtt(A("fq", 0, 128), A("kr", 0, 128), A("qrow", 0, 128), ALU.subtract)
+    act(A("lx", 0, 16), A("wi", 15, 256, 16), ACT.Identity, bias=pf(22), scale=1.0 / TINY)
+    scaled("s", A("yb", 0, 128), A("ps", 2048, 2176), 1.0)
+    vtt(A("lg", 0, 16), A("ci", 15, 256, 16), A("lx", 0, 16), ALU.min)
+    vtt(A("lsb", 256, 384), A("kr", 0, 128), A("fq", 0, 128), ALU.add)
+    vts(A("lk", 0, 16), A("lg", 0, 16), pf(23), 127.0, ALU.mult, ALU.add)
+    scaled("v", A("yb", 128, 256), A("ps", 2560, 2688), 1.0)
+    act(A("lsb", 0, 256), A("tbl", 0, 320), ACT.Copy, off=A("lk", 0, 16))
     for k in range(4):
         outs.append(dma("y", lambda k=k: g.sync.dma_start(T.osc[4 * k:4 * k + 4, :], T.xqs[32 * k:32 * k + 4, :]),
                         [A("xqs", 0, 256)], []))
-    scaled("v", A("yb", 0, 128), A("ps", 1536, 1664), 1.0)
-    scaled("s", A("yb", 128, 256), A("ps", 1024, 1152), 1.0)
-    vts(A("lsb", 256, 384), A("fq", 0, 128), 0.0078125, -64.0, ALU.mult, ALU.add)
-    outs.append(dma("y", lambda: g.sync.dma_start(T.y[:, 0:128], T.yb[:, 0:128]), [A("yb", 0, 128)], []))
-    outs.append(dma("s", lambda: g.scalar.dma_start(T.y[:, 128:256], T.yb[:, 128:256]), [A("yb", 128, 256)], []))
-    outs.append(dma("y", lambda: g.sync.dma_start(T.ls[:], T.lsb[0:128:16, :]), [A("lsb", 0, 384)], []))
+    outs.append(dma("y", lambda: g.sync.dma_start(T.y[:], T.yb[:]), [A("yb", 0, 256)], []))
+    outs.append(dma("s", lambda: g.scalar.dma_start(T.ls[:], T.lsb[0:128:16, :]), [A("lsb", 0, 384)], []))
     op("g", lambda: g.wait_ge(T.sem.lsent, sent[0]), [], [], outs)
 
     pools = {False: [["c%d" % i, 0, None] for i in range(NCS)], True: [["d%d" % i, 0, None] for i in range(NDS)]}

@@ -7,12 +7,19 @@ R = 3
 BIG = 1.0e29
 F8 = "float8_e4m3fn_x4"
 UP, DOWN, TINY = 2.0 ** 21, 2.0 ** -51, 2.0 ** -20
+CYCLE, FIX, GATHER, SCATTER, WAKE, CALL = 0.9, 60, 1.35, 3.2, 255, 800
 K = {
-    "su": 9,
-    "vs": 14,
+    "blocks": ("sssssvv", "ssssvvvv", "sssssvv"),
+    "quants": ((0, 192), (256, 384), (384, 512), (512, 640), (640, 768)),
+    "ps": 12,
     "ks": 5,
-    "gv": 80,
     "sv": 96,
+    "gather": "v0 s64 v128 s160",
+    "xc": "ssssssvv",
+    "shakes": 2600,
+    "hand": False,
+    "add": 0,
+    "near": 255,
 }
 
 
@@ -24,35 +31,36 @@ SCRATCH = {
     "ps": ("psum", [128, 4096], "float32"),
     "xin": _s(1024, "bfloat16"), "xt": _s(1024, "bfloat16"), "ut": _s(512, "bfloat16"), "vt": _s(512, "bfloat16"),
     "uq": _s(128, F8), "uqs": _s(128, "uint8"), "ur0": _s(128, F8), "ur0s": _s(128, "uint8"),
-    "upk": _s(16, F8), "upks": _s(16, "uint8"), "uland": _s(16, F8), "ulands": _s(16, "uint8"),
+    "upk": _s(32, F8), "upks": _s(32, "uint8"), "uland": _s(64, F8), "ulands": _s(64, "uint8"),
     "ur1": _s(128, F8), "ur1s": _s(128, "uint8"), "ur2": _s(128, F8), "ur2s": _s(128, "uint8"),
     "vq": _s(128, F8), "vqs": _s(128, "uint8"), "wq": _s(512, F8), "wqs": _s(512, "uint8"),
     "et": _s(2048, "bfloat16"), "ones": _s(512, "bfloat16"), "eq": _s(512, F8), "eqs": _s(512, "uint8"),
-    "g1": _s(512, "bfloat16"), "g2": _s(512, "bfloat16"), "gq": _s(128, F8), "gqs": _s(128, "uint8"),
-    "ft": _s(2816, "bfloat16"), "fc": _s(704, F8), "fcs": _s(704, "uint8"),
+    "g1": _s(512, "bfloat16"), "g2": _s(1024, "bfloat16"), "gq": _s(256, F8), "gqs": _s(256, "uint8"),
+    "ft": _s(3072, "bfloat16"), "fc": _s(768, F8), "fcs": _s(768, "uint8"),
     "xq": _s(256, F8), "xqs": _s(256, "uint8"), "zq": _s(256, F8), "zqs": _s(256, "uint8"),
     "qa": _s(128 * R, F8), "qas": _s(128 * R, "uint8"), "aland": _s(128 * R, F8), "alands": _s(128 * R, "uint8"),
     "x32": _s(1024, "bfloat16"), "vh": _s(1280, "bfloat16"), "gg": _s(1024, "bfloat16"),
     "zt": _s(1024, "bfloat16"), "z32": _s(1024, "bfloat16"), "at": _s(512, "bfloat16"),
     "d1": _s(256, "float32"), "hs": _s(256, "float32"), "ssend": _s(16 * R, "float32"), "sland": _s(32 * R, "float32"),
-    "nes": _s(256, "bfloat16"), "base": _s(16, "float32"), "acc": _s(16, "float32"),
+    "lj": _s(8, "int32"), "fl": _s(2, "uint16"),
+    "nes": _s(256, "bfloat16"), "base": _s(16, "float32"), "bas2": _s(8, "float32"), "acc": _s(32, "float32"),
     "lat": _s(256, "float32"), "la": _s(256, "bfloat16"), "lb": _s(256, "bfloat16"), "ce": _s(256, "float32"),
-    "sg": _s(2048, "bfloat16"), "jk": _s(2048, "bfloat16"),
-    "cmp": _s(2048, "bfloat16"), "scn": _s(2048, "bfloat16"), "pc": _s(2560, "bfloat16"),
+    "sg": _s(4096, "bfloat16"), "sp": _s(1024, "bfloat16"), "jk": _s(2048, "bfloat16"),
+    "cmp": _s(2048, "bfloat16"), "scn": _s(4096, "bfloat16"), "pc": _s(3072, "bfloat16"),
     "roff": _s(16, "uint16"), "ob": _s(256, "bfloat16"), "oh": _s(256, "bfloat16"), "ol": _s(64, "uint16"),
     "m4": _s(256, "bfloat16"), "m16": _s(256, "bfloat16"), "c4": _s(12, "float32"),
     "wh": _s(256, "bfloat16"), "ch": _s(256, "bfloat16"), "lw": _s(64, "float32"), "lf": _s(64, "float32"),
-    "ll": _s(64, "uint16"), "wi": _s(256, "bfloat16"), "ci": _s(256, "bfloat16"), "lx": _s(16, "float32"),
-    "lg": _s(16, "float32"), "lk": _s(16, "uint16"),
-    "pt": _s(288, "bfloat16"), "pp": _s(288, "bfloat16"), "pm": _s(14, "float32"),
-    "fsend": _s(16 * R, "bfloat16"), "fland": _s(32 * R, "bfloat16"),
+    "ll": _s(64, "uint16"), "wi": _s(256, "bfloat16"), "ci": _s(256, "bfloat16"), "lx": _s(32, "float32"),
+    "lk": _s(16, "uint16"),
+    "pt": _s(320, "bfloat16"), "pp": _s(320, "bfloat16"), "pm": _s(16, "float32"),
+    "fsend": _s(16 * R, "bfloat16"), "fland": _s(16 * R, "bfloat16"),
     "kx": _s(128, "float32"), "kr": _s(130, "float32"), "ko": _s(16, "float32"),
-    "xl": _s(8, "uint16"), "kl": _s(2, "uint16"), "lj": _s(8, "int32"),
+    "xl": _s(8, "uint16"), "kl": _s(2, "uint16"),
     "pa": _s(16, "float32"), "pb": _s(16, "float32"), "ksum": _s(8, "float32"),
     "poff": _s(8, "uint16"), "wb": _s(320, "bfloat16"), "cu": _s(256, "bfloat16"),
     "negm": _s(256, "float32"), "hold": _s(256, "float32"), "r16": _s(256, "bfloat16"),
     "seg": _s(512, "bfloat16"), "cc": _s(16, "float32"), "jd": _s(256, "bfloat16"),
-    "pi": _s(16, "int32"), "pf": _s(24, "float32"), "li": _s(16, "int32"),
+    "pi": _s(24, "int32"), "pf": _s(48, "float32"), "li": _s(16, "int32"),
     "cl": _s(2, "uint16"), "el": _s(16, "uint16"), "rl": _s(8, "uint16"),
     "keyc": _s(128, "float32"), "qown": _s(16, "float32"), "ids": _s(128, "bfloat16"), "qrow": _s(128, "float32"),
     "tbl": _s(320, "float32"), "lsb": _s(384, "float32"), "fq": _s(128, "float32"), "yb": _s(256, "float32"),
@@ -60,6 +68,7 @@ SCRATCH = {
 NCS, NDS = 100, 24
 SEMAPHORES = (["c%d" % i for i in range(NCS)] + ["d%d" % i for i in range(NDS)] + ["lsent", "au"]
               + ["%s%d" % (k, t) for k in ("sa", "sb", "aa", "af") for t in range(R)])
+LAID = {}
 
 
 def split_engines(topo, src, d1, d2):
@@ -71,7 +80,15 @@ def split_engines(topo, src, d1, d2):
         e1 = [e for e in e1 if e not in e2]
     else:
         e2 = [e for e in e2 if e not in e1]
-    return [(sum(1 << e for e in es), len(es)) for es in (e1, e2)]
+    return [e1, e2]
+
+
+def deal(engines, k):
+    shares = [engines]
+    while len(shares) < k:
+        a = shares.pop(0)
+        shares += [a[:len(a) // 2], a[len(a) // 2:]]
+    return shares
 
 
 def rank_program(g, core, T, topo):
@@ -83,9 +100,10 @@ def rank_program(g, core, T, topo):
     Q = {"g": g, "v": g.vector, "s": g.scalar, "t": g.tensor, "y": g.sync}
 
     ops = []
-    known = {k: 0 for k in Q}
     log = {}
     exts = {}
+    tip = {}
+    gate = []
 
     def bits(a):
         if a[0] == "ps":
@@ -94,34 +112,40 @@ def rank_program(g, core, T, topo):
             return ((1 << (a[2] - a[1])) - 1) << a[1]
         return sum(1 << k for k in range(a[1], a[2], a[3]))
 
-    def ext(sem, count):
+    def ext(sem, count, mine, late):
         if sem not in exts:
             exts[sem] = len(ops)
-            ops.append({"ext": (sem, count), "k": 1 << len(ops), "q": None})
+            ops.append({"ext": (sem, count), "q": None, "deps": set(), "behind": {mine}, "busy": 0, "late": late})
         return exts[sem]
 
-    def op(q, fn, rd, wr, after=(), dma=False, group=None):
+    def op(q, fn, rd, wr, busy, after=(), dma=False, group=None, late=0):
         me = len(ops)
         deps = set(after)
+        behind = {tip[q]} if q in tip and q in "gty" else set()
         for a, w in [(a, False) for a in rd] + [(a, True) for a in wr]:
             m = bits(a)
             for (o, om, ow, oq) in log.get(a[0], []):
                 if om & m and (w or ow or (a[0] == "ps" and oq != q)) and o != group:
                     deps.add(o)
-        waits = []
-        for o in sorted(deps, reverse=True):
-            if not known[q] >> o & 1:
-                waits.append(o)
-                known[q] |= ops[o]["k"]
-                ops[o]["sig"] = True
-        k = known[q] | 1 << me | (0 if group is None else ops[group]["k"])
-        ops.append({"q": q, "fn": fn, "waits": waits, "ki": known[q], "k": k, "dma": dma})
+        behind |= set(gate)
+        tip[q] = me
+        ops.append({"q": q, "fn": fn, "deps": deps, "behind": behind, "busy": busy, "late": late, "dma": dma,
+                    "group": group})
         for a, w in [(a, False) for a in rd] + [(a, True) for a in wr]:
             m = bits(a)
             if w:
                 log[a[0]] = [e for e in log.get(a[0], []) if e[1] & ~m]
             log.setdefault(a[0], []).append((me, m, w, q))
         return me
+
+    def size(a):
+        return len(range(a[1], a[2], a[3]))
+
+    def cost(out, *ins, off=None, halves=True):
+        if off is not None:
+            return FIX + GATHER * size(out)
+        narrow = halves and all(SCRATCH[a[0]][2] in ("bfloat16", "uint16") for a in (out,) + ins)
+        return K["add"] + max(FIX - K["add"], CYCLE * size(out) * (0.5 if narrow else 1.0))
 
     def A(name, a, b, s=1):
         return (name, a, b, s)
@@ -138,24 +162,25 @@ def rank_program(g, core, T, topo):
     def vts(out, in0, s1, s2, o0, o1=None, off=None, after=()):
         rd = [in0] + [s for s in (s1, s2, off) if isap(s)]
         f = lambda s: ap(s) if isap(s) else s
-        if o1 is None:
-            return op("v", lambda: g.vector.tensor_scalar(ap(out), src(in0, off), f(s1), None, o0), rd, [out], after)
-        return op("v", lambda: g.vector.tensor_scalar(ap(out), src(in0, off), f(s1), f(s2), o0, o1), rd, [out], after)
+        more = () if o1 is None else (o1,)
+        return op("v", lambda: g.vector.tensor_scalar(ap(out), src(in0, off), f(s1), None if o1 is None else f(s2),
+                                                      o0, *more), rd, [out], cost(out, in0, off=off), after)
 
     def vtt(out, in0, in1, o, off=None, after=()):
         return op("v", lambda: g.vector.tensor_tensor(ap(out), src(in0, off), ap(in1), o),
-                  [in0, in1] + ([off] if off else []), [out], after)
+                  [in0, in1] + ([off] if off else []), [out], cost(out, off=off, halves=False), after)
 
     def vcopy(out, in_):
-        return op("v", lambda: g.vector.tensor_copy(ap(out), ap(in_)), [in_], [out])
+        return op("v", lambda: g.vector.tensor_copy(ap(out), ap(in_)), [in_], [out], cost(out, in_))
 
     def vscatter(win, off, in_):
-        return op("v", lambda: g.vector.tensor_copy(ap(win).indirect(ap(off)), ap(in_)), [in_, off], [win])
+        return op("v", lambda: g.vector.tensor_copy(ap(win).indirect(ap(off)), ap(in_)), [in_, off], [win],
+                  FIX + SCATTER * size(in_))
 
     def vscan(out, d0, d1, o0, o1, init=0.0):
         return op("v", lambda: g.vector.tensor_tensor_scan(ap(out), ap(d0), ap(d1), ap(init) if isap(init) else init,
                                                            o0, o1),
-                  [d0, d1] + ([init] if isap(init) else []), [out])
+                  [d0, d1] + ([init] if isap(init) else []), [out], cost(out, d0, d1))
 
     def vsum(out, d, init=0.0):
         return vscan(out, d, d, ALU.add, ALU.max, init)
@@ -166,15 +191,15 @@ def rank_program(g, core, T, topo):
     def vhold(out, row, mask):
         return vscan(out, row, A(mask, 0, out[2] - out[1]), ALU.max, ALU.mult)
 
-    def vtr(out, in_):
-        return op("v", lambda: g.vector.transpose(ap(out), ap(in_)), [in_], [out])
+    def vtr(out, in_, after=()):
+        return op("v", lambda: g.vector.transpose(ap(out), ap(in_)), [in_], [out], cost(out, in_), after)
 
     def vset(out, c):
-        return op("v", lambda: g.vector.memset(ap(out), c), [], [out])
+        return op("v", lambda: g.vector.memset(ap(out), c), [], [out], cost(out))
 
     def quant(c, a, b, tile, e0):
         t, o, s = A(tile, e0, e0 + 4 * (b - a)), A(c, a, b), A(c + "s", a, b)
-        return op("v", lambda: g.vector.quantize_mx(ap(o), ap(s), ap(t)), [t], [o, s])
+        return op("v", lambda: g.vector.quantize_mx(ap(o), ap(s), ap(t)), [t], [o, s], 0.29 * CYCLE * size(t))
 
     def act(out, in_, func, bias=None, scale=None, acc=None, off=None, after=()):
         rd = [in_] + [s for s in (bias, scale, off) if isap(s)]
@@ -189,7 +214,8 @@ def rank_program(g, core, T, topo):
             if acc is not None:
                 k["accum_out"] = ap(acc)
             return g.scalar.activation(ap(out), src(in_, off), func, **k)
-        return op("s", fn, rd, [out] + ([acc] if acc else []), after)
+        return op("s", fn, rd, [out] + ([acc] if acc else []),
+                  cost(out, off=off, halves=False) + (20 if acc or off else 0), after)
 
     def scaled(q, out, in_, c, off=None):
         if q == "v":
@@ -197,56 +223,49 @@ def rank_program(g, core, T, topo):
         return act(out, in_, ACT.Copy, scale=c, off=off)
 
     def zero(a):
-        return scaled("s", a, A("ones", 0, len(range(a[1], a[2], a[3]))), 0.0)
+        return scaled("s", a, A("ones", 0, size(a)), 0.0)
 
-    def pick(dst, win, w, off, after=()):
+    def pick(dst, win, w, off, after=(), w0=0):
         m = 16 * (off[2] - off[1])
-        o, i = A(dst, 0, m), A(win, 0, w)
+        o, i = A(dst, 0, m), A(win, w0, w0 + w)
         op("v", lambda: g.vector.tensor_copy(ap(o).bitcast(dt.uint32), ap(i).bitcast(dt.uint32).indirect(ap(off))),
-           [i, off], [o], after)
-        o2, i2 = A(dst + "s", 0, m), A(win + "s", 0, w)
-        op("s", lambda: g.scalar.activation(ap(o2), ap(i2).indirect(ap(off)), ACT.Copy), [i2, off], [o2], after)
+           [i, off], [o], cost(o, off=off), after)
+        o2, i2 = A(dst + "s", 0, m), A(win + "s", w0, w0 + w)
+        op("s", lambda: g.scalar.activation(ap(o2), ap(i2).indirect(ap(off)), ACT.Copy), [i2, off], [o2],
+           cost(o, off=off), after)
 
     def mm(bank, w, w0, x, x0, m, after=(), start=True, stop=True, group=None):
         o = A("ps", 512 * bank, 512 * bank + m)
         r = [A(w, w0, w0 + 128), A(w + "s", w0, w0 + 128), A(x, x0, x0 + m), A(x + "s", x0, x0 + m)]
         return op("t", lambda: g.tensor.matmul_mx(ap(o), ap(r[0]), ap(r[1]), ap(r[2]), ap(r[3]), start, stop),
-                  r, [o], after, group=group)
+                  r, [o], 0.85 * CYCLE * (m + 16), after, group=group)
 
     def iota(out, pattern, base, cm, whole=False):
         if whole:
-            return op("g", lambda: g.iota(ap(out), pattern, base, cm), [], [out])
-        return op("g", lambda: g.iota(ap(out), pattern, base, cm, allow_small_or_imprecise_dtypes=True), [], [out])
+            return op("g", lambda: g.iota(ap(out), pattern, base, cm), [], [out], 130 + 2 * CYCLE * size(out))
+        return op("g", lambda: g.iota(ap(out), pattern, base, cm, allow_small_or_imprecise_dtypes=True), [], [out],
+                  130 + 2 * CYCLE * size(out))
 
-    def select(out, in_, pattern, cmp, base, cm):
-        return op("g", lambda: g.affine_select(ap(out), ap(in_), pattern, cmp, 0.0, base, cm), [in_], [out])
-
-    def dma(q, fn, rd, wr, after=()):
-        return op(q, fn, rd, wr, after, dma=True)
+    def dma(q, fn, rd, wr, late=2000):
+        return op(q, fn, rd, wr, 50, dma=True, late=late)
 
     sent = [0]
 
-    def send(sbuf, dsts, codes, sems):
-        ms = split_engines(topo, core, cores[dsts[0][0]], cores[dsts[1][0]])
-
+    def send(ways, after=()):
         def fn():
-            f = (lambda a: ap(a).bitcast(dt.uint8)) if codes else ap
+            f = lambda a: ap(a).bitcast(dt.uint8) if SCRATCH[a[0]][2] == F8 else ap(a)
             tr = []
-            for (rk_, place), (mask, cnt), sem in zip(dsts, ms, sems):
-                ad = topo.addr(cores[rk_])
-                tr.append(RemoteDMATransfer(dst_ids=[DstId(rid=ad[0], pnc=ad[1])], dma_engine_mask=mask,
-                                            remote_sem=T.sem[sem], src=f(sbuf), dst=f(place)))
+            for r, engines, sem, pieces in ways:
+                ad = topo.addr(cores[r])
+                for (a, b), es in zip(pieces, deal(engines, len(pieces))):
+                    tr.append(RemoteDMATransfer(dst_ids=[DstId(rid=ad[0], pnc=ad[1])], remote_sem=T.sem[sem],
+                                                dma_engine_mask=sum(1 << e for e in es), src=f(a), dst=f(b)))
             g.remote_dma_fused(tr, local_sem=T.sem.lsent)
-        sent[0] += ms[0][1] + ms[1][1]
-        return op("g", fn, [sbuf], [])
+        sent[0] += sum(len(w[1]) for w in ways)
+        return op("g", fn, [] if after else [a for w in ways for a, b in w[3]], [], CALL, after)
 
-    def send1(sbuf, rk_, place, codes, sem, engines):
-        def fn():
-            f = (lambda a: ap(a).bitcast(dt.uint8)) if codes else ap
-            ad = topo.addr(cores[rk_])
-            g.remote_dma(f(place), f(sbuf), T.sem[sem], T.sem.lsent, ad[1], ad[0], sum(1 << e for e in engines))
-        sent[0] += len(engines)
-        return fn
+    def both(s, dsts):
+        return split_engines(topo, cores[s], cores[dsts[0]], cores[dsts[1]])
 
     def fwd(r):
         return [(r + 1) % n, (r + 2) % n]
@@ -255,358 +274,446 @@ def rank_program(g, core, T, topo):
         return [(r - 1) % n, (r - 2) % n]
 
     def count(s, dsts):
-        return split_engines(topo, cores[s], cores[dsts[0]], cores[dsts[1]])[dsts.index(rank)][1]
+        return len(both(s, dsts)[dsts.index(rank)])
 
     def slot(s, r):
         return sorted(back(r)).index(s)
 
     def handed(s):
         a, b = [topo.chip(cores[r]) for r in fwd(s)]
-        return a == b != topo.chip(cores[s])
-
-    def inner(r):
-        far = [e for e in range(n) if topo.chip(cores[e]) != topo.chip(cores[r])][0]
-        return [e for e in topo.engines(cores[r], cores[(r + 1) % n]) if e not in topo.engines(cores[r], cores[far])]
+        return K["hand"] and a == b != topo.chip(cores[s])
 
     def codes_count(s):
         if not handed(s):
             return count(s, fwd(s))
         r = fwd(s)[0]
-        return len(topo.engines(cores[s], cores[r])) if r == rank else len(inner(r))
+        return len(topo.engines(cores[s if r == rank else r], core))
 
     ncodes = sum(codes_count(s) for s in back(rank))
     nfwd = sum(count(s, fwd(s)) for s in back(rank))
     nback = [count(e, back(e)) for e in fwd(rank)]
 
-    dma("s", lambda: g.scalar.dma_start(T.ut[:], T.u[:]), [], [A("ut", 0, 512)])
-    xin = [dma("y", lambda h=h: g.sync.dma_start(T.xin[:, 512 * h:512 * h + 512], T.x[:, 512 * h:512 * h + 512]),
-               [], [A("xin", 512 * h, 512 * h + 512)]) for h in range(2)]
+    dma("s", lambda: g.scalar.dma_start(T.ut[:], T.u[:]), [], [A("ut", 0, 512)], 1900)
+    for h in range(2):
+        dma("y", lambda h=h: g.sync.dma_start(T.xin[:, 512 * h:512 * h + 512], T.x[:, 512 * h:512 * h + 512]),
+            [], [A("xin", 512 * h, 512 * h + 512)], 2800 + 900 * h)
 
-    FT = [0, 1024, 1792, 2304, 2560]
+    FT = [0, 128, 256, 384, 512, 640, 768]
     pi = lambda k, m=1: A("pi", k, k + m)
     pf = lambda k, m=1: A("pf", k, k + m)
+    row = lambda name: A(name, 0, 256)
     iota(pi(0, 2), [[12, 2]], 0, 1, True)
     iota(A("li", 0, 16), [[1, 16]], 0, 0, True)
+    iota(row("r16"), [[0, 16], [1, 16]], 1, 0)
     iota(A("g1", 0, 512), [[1, 8], [0, 64]], 0, 0)
+    iota(row("jd"), [[1, 256]], 1, 0)
     vset(A("ones", 0, 512), 1.0)
-    vset(A("seg", 0, 512), 1.0)
     vts(pi(4, 2), pi(0, 2), 15, None, ALU.bitwise_and)
-    vset(A("seg", 0, 512, 16), 0.0)
     vts(pi(6), pi(0), 4, None, ALU.logical_shift_right)
-    vts(A("rl", 0, 8), A("li", 0, 8), 16.0, None, ALU.mult)
-    vset(A("hold", 0, 256), 0.0)
-    vts(pi(8, 2), pi(4, 2), 2, None, ALU.logical_shift_right)
     vts(pf(0), pi(4), 1.0, None, ALU.add)
-    vseg(A("r16", 0, 256), A("ones", 0, 256))
-    vset(A("hold", 0, 256, 16), -5 * BIG)
-    vts(A("cl", 0, 1), pi(4), 16.0, 112.0, ALU.mult, ALU.min)
     vcopy(pf(1), pi(4))
-    vcopy(pf(2, 2), pi(8, 2))
-    vts(A("negm", 0, 256), A("r16", 0, 256), pf(0), -BIG, ALU.not_equal, ALU.mult)
     vcopy(pf(4), pi(6))
-    vcopy(A("el", 0, 16), A("li", 0, 16))
-    vts(pi(10), pi(0), 3, None, ALU.bitwise_and)
-    vts(A("la", 0, 256), A("r16", 0, 256), pf(0), -1024.0, ALU.is_equal, ALU.mult)
-    vts(A("lb", 0, 256), A("r16", 0, 256), pf(1), 2048.0, ALU.is_equal, ALU.mult)
-    for a, e in ((0, 208), (1, 144), (2, 80)):
-        zero(A("ft", FT[a] + 4 * e, FT[a + 1]))
-    zero(A("ft", FT[3] + 64, FT[4] + 256))
-    for b in range(4):
-        zero(A("et", 512 * b, 512 * b + 512))
+    vts(A("rl", 0, 8), A("li", 0, 8), 16.0, None, ALU.mult)
+    vts(A("cl", 0, 2), pi(4, 2), 16.0, 112.0, ALU.mult, ALU.min)
+    for a in (0, 256):
+        act(A("seg", a, a + 256), row("r16"), ACT.Sign, bias=-1.0)
+    act(row("hold"), row("seg"), ACT.Identity, bias=-5 * BIG, scale=5 * BIG)
+    vts(row("negm"), row("r16"), pf(0), -BIG, ALU.not_equal, ALU.mult)
+    vts(A("g2", 0, 512), A("g1", 0, 512), pf(4), None, ALU.is_equal)
+    vts(A("g2", 512, 1024), A("g1", 0, 512), pf(4), -1.0, ALU.is_equal, ALU.mult)
+    quant("gq", 0, 128, "g2", 0)
+    quant("gq", 128, 256, "g2", 512)
+    vts(row("la"), row("r16"), pf(0), -1024.0, ALU.is_equal, ALU.mult)
+    vts(row("lb"), row("r16"), pf(1), 2048.0, ALU.is_equal, ALU.mult)
+    vtt(row("lat"), row("la"), row("lb"), ALU.add)
+    vts(pf(5), pf(1), -1.0, 15.0, ALU.mult, ALU.add)
+    vts(pf(6), pf(1), 0.0, 2048.0, ALU.is_equal, ALU.mult)
+    vts(pf(7), pf(1), 15.0, -1024.0, ALU.is_equal, ALU.mult)
+    vts(pf(8), pf(5), pf(6), pf(7), ALU.add, ALU.add)
+    act(pf(9), pf(6), ACT.Identity, bias=1024.0, scale=-1.0)
+    vts(A("cc", 0, 16), A("li", 0, 16), 16.0, pf(8), ALU.mult, ALU.add)
+    for a in (0, 4):
+        zero(A("ft", 4 * (FT[a] + 80), 4 * FT[a + 1]))
+        zero(A("ft", 4 * (FT[a + 1] + 16), 4 * FT[a + 2]))
+    zero(A("acc", 0, 25, 24))
+
+    def for_lists():
+        vts(pi(8, 2), pi(4, 2), 2, None, ALU.logical_shift_right)
+        vts(pi(10), pi(0), 3, None, ALU.bitwise_and)
+        vcopy(pf(2, 2), pi(8, 2))
+        vcopy(A("el", 0, 8), A("li", 0, 8))
+        vts(A("c4", 0, 4), A("li", 0, 4), pf(2), UP, ALU.is_equal, ALU.mult)
+        vts(A("c4", 4, 8), A("li", 0, 4), pf(3), DOWN, ALU.not_equal, ALU.max)
+        vtt(A("c4", 8, 12), A("c4", 0, 4), A("c4", 4, 8), ALU.max)
+        for j in range(4):
+            act(A("m4", j, 256, 4), A("ones", 0, 64), ACT.Copy, scale=A("c4", 8 + j, 9 + j))
+        vts(pf(10), pf(2), 0.0, 4.0 / (UP * DOWN), ALU.is_equal, ALU.mult)
+        vts(pf(11), pf(10), 4.0 / UP, None, ALU.max)
+        vts(pf(12), pi(10), -4.0, None, ALU.add)
+        for a in (A("at", 256, 512), A("pc", 15, 256, 16), A("pc", 1295, 1792, 16), A("pc", 2831, 3072, 16)):
+            zero(a)
+
+    def for_proposals():
+        vtt(pi(12), pi(6), pi(0), ALU.add)
+        vts(pi(13), pi(0), 4, None, ALU.bitwise_and)
+        vts(pi(14), pi(12), 1, None, ALU.bitwise_and)
+        vcopy(pf(15), pi(14))
+        vts(pf(25), pi(13), -20.0, 80.0, ALU.mult, ALU.add)
+        vts(pf(26), pf(25), pf(15), 15.0, ALU.mult, ALU.add)
+        vts(A("fl", 0, 1), pi(10), 16.0, pf(26), ALU.mult, ALU.add)
+        for b in range(4):
+            zero(A("et", 512 * b, 512 * b + 512))
+
+    def for_queue():
+        vts(pf(27), pi(0), 1.0, None, ALU.add)
+        for b in range(4):
+            vts(A("et", 512 * b + b, 512 * b + 512, 4), A("jd", 0, 128), pf(27), None, ALU.is_equal)
+        quant("eq", 0, 512, "et", 0)
+        vts(pi(11), pi(0), 31, None, ALU.bitwise_and)
+        vcopy(pf(13), pi(11))
+        act(pf(14), pf(12), ACT.Identity, bias=4.0)
+        act(pf(18), pf(12), ACT.Identity, bias=512.0)
+        scaled("s", pf(19), pf(1), 0.0078125)
+        vcopy(A("xl", 0, 8), A("lj", 0, 8))
+        vts(A("kl", 0, 1), pi(13), 2.0, pf(14), ALU.mult, ALU.add)
+        vts(A("keyc", 0, 128), A("fq", 0, 128), pf(13), 0.0078125, ALU.add, ALU.mult)
+        vts(A("qown", 0, 16), A("li", 0, 16), 0.125, pf(19), ALU.mult, ALU.add)
+        scaled("s", A("kr", 128, 130), A("ones", 0, 2), -1024.0)
+        scaled("s", A("ids", 0, 128), A("jd", 0, 128), TINY)
+        vts(pf(16), pf(2), 0.0, -128.0 * UP, ALU.not_equal, ALU.mult)
+        vts(pf(17), pf(16), -128.0 * UP * DOWN, None, ALU.min)
+
+    def for_ls():
+        quant("vq", 0, 128, "vt", 0)
+        vts(pf(24), pf(1), 0.0, 16.0, ALU.is_equal, ALU.mult)
+        vts(pf(20), pf(24), pf(1), None, ALU.add)
+        vts(pf(21), pf(1), 0.0, -128.0 * UP, ALU.not_equal, ALU.mult)
+        vts(pf(22), pf(21), -128.0 * UP * DOWN, None, ALU.min)
+        vts(pf(23), pf(24), 1.0 / (16.0 * UP * DOWN), 1.0 / UP, ALU.mult, ALU.max)
+        vts(row("la"), row("r16"), pf(0), UP, ALU.is_equal, ALU.mult)
+        vts(row("lb"), row("r16"), pf(20), DOWN, ALU.not_equal, ALU.max)
+        vtt(row("m16"), row("la"), row("lb"), ALU.max)
+        act(A("tbl", 0, 128), A("jd", 0, 128), ACT.Identity, bias=255.0)
+        act(A("qrow", 0, 128), A("jd", 0, 128), ACT.Identity, bias=-63.9921875, scale=-0.0078125)
+
+    def once(now, make):
+        if now:
+            gate.append(len(ops) - 1)
+            make()
+            gate.pop()
 
     quant("uq", 0, 128, "ut", 0)
     pick("ur0", "uq", 128, A("rl", 0, 8))
-    quant("xq", 0, 128, "xin", 0)
-    pick("upk", "uq", 128, A("cl", 0, 1))
-    quant("xq", 128, 256, "xin", 512)
-    for a in (A("at", 256, 512), A("pc", 15, 256, 16), A("pc", 2319, 2560, 16), A("acc", 0, 1)):
-        zero(a)
-    send(A("upk", 0, 8), [(s, A("uland", 8 * j, 8 * j + 8)) for j, s in enumerate(back(rank))], True, ["au", "au"])
-    send(A("upks", 0, 8), [(s, A("ulands", 8 * j, 8 * j + 8)) for j, s in enumerate(back(rank))], False, ["au", "au"])
+    pick("upk", "uq", 128, A("cl", 0, 2))
+    mine = send([(s, es, "au", [(A("upk", 0, 8), A("uland", 32 * j, 32 * j + 8)),
+                                (A("upks", 0, 32), A("ulands", 32 * j, 32 * j + 32))])
+                 for j, (s, es) in enumerate(zip(back(rank), both(rank, back(rank))))])
+    au = ext("au", sum(nback), mine, 5500)
+    iota(A("lj", 0, 8), [[8, 2], [1, 4]], 4, 0, True)
+    iota(A("fq", 0, 128), [[32, 4], [0, 32]], 0, 0)
 
-    def flags(c):
-        a, e = (0, 16 - c) if c > 12 else (1 + (12 - c) // 4, (12 - c) % 4)
-        return A("ft", FT[a] + e, FT[a] + 64 * c, 4)
+    def scores(h, tile):
+        quant("xq", 128 * h, 128 * h + 128, tile, 512 * h)
+        for k in range(2):
+            mm(4 * (1 - h) + k, "ur0", 0, "xq", 128 * h, 128)
 
-    SU, VS, KS, GV, SV = K["su"], K["vs"], K["ks"], K["gv"], K["sv"]
-    at16 = lambda c: 8 * c * (c - 1)
+    KS, SV = K["ks"], K["sv"]
     outs = []
+    for h in range(2):
+        scores(h, "xin")
 
     for t in range(R):
         first, last = t == 0, t == R - 1
         X = A("xin" if first else "xt", 0, 1024)
 
-        mm(0, "ur0", 0, "xq", 0, 256)
-        mm(1, "ur0", 0, "xq", 0, 256)
-        if first:
-            vtt(A("lat", 0, 256), A("la", 0, 256), A("lb", 0, 256), ALU.add)
-        cut = 16 * SU + 16
-        for a, b in ((0, cut), (cut, 256)):
-            vtt(A("d1", a, b), A("ps", a, b), A("negm", a, b), ALU.add)
-        for a, b in ((0, cut), (cut, 256)):
+        for h in range(2):
+            a, b, o = 128 * h, 128 * h + 128, 2048 * (1 - h)
+            vtt(A("d1", a, b), A("ps", o, o + 128), A("negm", a, b), ALU.add)
             vscan(A("hs", a, b), A("hold", a, b), A("d1", a, b), ALU.add, ALU.max)
         own = lambda c: A("hs", 16 * c + 15, 16 * c + 16)
-
-        def signs(cs):
-            for c in cs:
-                act(A("sg", at16(c), at16(c) + 16 * c), A("ps", 512, 512 + 16 * c), ACT.Sign, bias=own(c), scale=-1.0)
-
-        def sums(cs):
-            for c in cs:
-                act(flags(c), A("sg", at16(c), at16(c) + 16 * c), ACT.Relu, acc=A("acc", c, c + 1))
-
-        def on_vector(cs):
-            for c in cs:
-                vts(flags(c), A("ps", 0, 16 * c), own(c), None, ALU.is_lt)
-
-        signs(range(SU, 4, -1))
         act(A("ssend", 16 * t, 16 * t + 16), A("hs", 15, 256, 16), ACT.Copy)
-        send(A("ssend", 16 * t, 16 * t + 16),
-             [(s, A("sland", 32 * t + 16 * j, 32 * t + 16 * j + 16)) for j, s in enumerate(back(rank))],
-             False, ["sa%d" % t, "sb%d" % t])
-        if first:
-            for b in range(4):
-                select(A("et", 512 * b + b, 512 * b + 512, 4), A("ones", 0, 128), [[1, 128]], ALU.is_equal, 0, -1)
-        if t == 1:
-            iota(A("qrow", 0, 128), [[1, 128]], 0, 0)
-            iota(A("tbl", 0, 128), [[1, 128]], 256, 0)
-        sums(range(SU, 4, -1))
-        signs(range(4, 0, -1))
-        sums(range(4, 0, -1))
-        if first:
-            vts(A("g2", 0, 512), A("g1", 0, 512), pf(4), None, ALU.is_equal)
-        vtt(A("ft", 0, 1024, 4), A("ps", 0, 256), A("hs", 0, 256), ALU.is_le)
-        on_vector([15, 14, 13, 12])
-        if first:
-            quant("gq", 0, 128, "g2", 0)
-        quant("fc", 0, 256, "ft", FT[0])
-        grp = mm(3, "gq", 0, "fc", 0, 256, stop=False)
-        on_vector(range(11, SU, -1))
-        if first:
-            vts(pf(5), pf(1), -1.0, 15.0, ALU.mult, ALU.add)
-            vts(pf(6), pf(1), 0.0, 2048.0, ALU.is_equal, ALU.mult)
-            vts(pf(7), pf(1), 15.0, -1024.0, ALU.is_equal, ALU.mult)
-        vseg(A("nes", 0, 256), A("ft", 0, 1024, 4))
-        if first:
-            vts(pf(8), pf(5), pf(6), pf(7), ALU.add, ALU.add)
-            vts(pf(9), pf(6), -1.0, 1024.0, ALU.mult, ALU.add)
-            vsum(A("jd", 0, 256), A("ones", 0, 256))
-            vts(A("cc", 0, 16), A("li", 0, 16), 16.0, pf(8), ALU.mult, ALU.add)
-        quant("fc", 256, 448, "ft", FT[1])
-        grp = mm(3, "gq", 0, "fc", 256, 192, start=False, stop=False, group=grp)
-        vtt(A("base", 0, 16), A("cc", 0, 16), A("nes", 15, 256, 16), ALU.subtract)
-        quant("fc", 448, 704 if first else 640, "ft", FT[2])
-        grp = mm(3, "gq", 0, "fc", 448, 128, start=False, stop=False, group=grp)
-        mm(3, "gq", 0, "fc", 576, 128, start=False, group=grp)
-        for c in range(VS - 1, SU, -1):
-            act(A("jk", at16(c), at16(c) + 16 * c), flags(c), ACT.Copy, acc=A("acc", c, c + 1))
-        ends = lambda c: 256 * (c - VS) + 256
-        for c in range(15, VS - 1, -1):
-            vsum(A("scn", ends(c) - 16 * c, ends(c)), flags(c))
-        if first:
-            vts(A("c4", 0, 4), A("li", 0, 4), pf(2), UP, ALU.is_equal, ALU.mult)
-            vts(A("c4", 4, 8), A("li", 0, 4), pf(3), DOWN, ALU.not_equal, ALU.max)
-            vts(pf(10), pf(2), 0.0, 4.0 / (UP * DOWN), ALU.is_equal, ALU.mult)
-            vts(pf(12), pi(10), -4.0, None, ALU.add)
-            vtt(A("c4", 8, 12), A("c4", 0, 4), A("c4", 4, 8), ALU.max)
-            vts(pf(11), pf(10), 4.0 / UP, None, ALU.max)
-            for j in range(4):
-                act(A("m4", j, 256, 4), A("ones", 0, 64), ACT.Copy, scale=A("c4", 8 + j, 9 + j))
-        if VS < 16:
-            vtt(A("lat", 16 * VS + 15, 256, 16), A("base", VS, 16), A("scn", 255, ends(15), 256), ALU.subtract)
-        vtt(A("lat", 15, 16 * VS, 16), A("base", 0, VS), A("acc", 0, VS), ALU.subtract)
-        vscan(A("ce", 0, 256), A("ps", 1536, 1792), A("lat", 0, 256), ALU.min, ALU.add, 4096.0)
-        vts(A("roff", 0, 16), A("ce", 15, 256, 16), pf(9), None, ALU.add)
+        mine = send([(s, es, "s%s%d" % ("ab"[j], t),
+                      [(A("ssend", 16 * t, 16 * t + 16), A("sland", 32 * t + 16 * j, 32 * t + 16 * j + 16))])
+                     for j, (s, es) in enumerate(zip(back(rank), both(rank, back(rank))))])
+        e1, e2 = ext("sa%d" % t, nback[0], mine, 3800), ext("sb%d" % t, nback[1], mine, 3800)
+
+        for h in range(2):
+            a, b, o = 128 * h, 128 * h + 128, 2048 * (1 - h)
+            diag = A("ft", 4 * FT[4 * h], 4 * FT[4 * h + 1], 4)
+            vtt(diag, A("ps", o, o + 128), A("hs", a, b), ALU.is_le)
+            vseg(A("nes", a, b), diag)
+            vtt(A("base", 8 * h, 8 * h + 8), A("cc", 8 * h, 8 * h + 8), A("nes", a + 15, b, 16), ALU.subtract)
+        sums = {(0, 0): ("acc", 0, 1), (2, 8): ("acc", 24, 1)}
+        for part, blocks in enumerate((range(7, 0, -1), range(7, -1, -1), range(15, 8, -1))):
+            for c in blocks:
+                how, across = K["blocks"][part][c - blocks[-1]], part == 1
+                m, k = (128, c) if across else (16 * (c % 8), 8 - c % 8)
+                e, o, at = 4 * FT[2 * part + k // 4], 2048 * (part == 0) + 512 * (how == "s"), 8 * part + c
+                flags, seen, sign = A("ft", e + k % 4, e + 4 * m, 4), A("ps", o, o + m), A("sg", 128 * at, 128 * at + m)
+                if how == "s":
+                    sums[part, c] = ("acc", at, 1)
+                    act(sign, seen, ACT.Sign, bias=own(c), scale=-1.0)
+                    act(flags, sign, ACT.Relu, scale=-1.0 if across else 1.0, acc=A("acc", at, at + 1))
+                else:
+                    sums[part, c] = ("scn", 128 * at + 127, 128)
+                    vts(flags, seen, own(c), None, ALU.is_gt if across else ALU.is_lt)
+                    vsum(A("scn", 128 * at + 128 - m, 128 * at + 128), flags)
+
+        def along(out, step, base, part, c0):
+            a = c0
+            for c in range(c0 + 1, c0 + 9):
+                if c == c0 + 8 or sums[part, c][0] != sums[part, a][0]:
+                    name, at, by = sums[part, a]
+                    vtt(A(out, step * a + step - 1, step * c, step), A(base, a, c),
+                        A(name, at, at + by * (c - a - 1) + 1, by), ALU.add if part == 1 else ALU.subtract)
+                    a = c
+
+        for a, b in K["quants"]:
+            quant("fc", a, b + (64 if first and b % 128 else 0), "ft", 4 * a)
+        once(first, for_lists)
+        along("bas2", 1, "base", 0, 0)
+        along("lat", 16, "bas2", 1, 0)
+        along("lat", 16, "base", 2, 8)
+        for h, tiles in enumerate((FT[:2], FT[2:6])):
+            grp = None
+            for a in tiles:
+                grp = mm(2 + h, "gq", 128 * (a in FT[2:4]), "fc", a, 128, start=a == tiles[0], stop=a == tiles[-1],
+                         group=grp)
+            a, b, o = 128 * h, 128 * h + 128, 1024 + 512 * h
+            vscan(A("ce", a, b), A("ps", o, o + 128), A("lat", a, b), ALU.min, ALU.add, 4096.0)
+            vts(A("roff", 8 * h, 8 * h + 8), A("ce", a + 15, b, 16), pf(9), None, ALU.add)
+            vscatter(row("ob"), A("roff", 8 * h, 8 * h + 8), A("jd", a, b))
         if first:
             dma("y", lambda: g.sync.dma_start(T.wq[:].bitcast(dt.uint8), T.wc[:]), [A("ce", 0, 1)], [A("wq", 0, 512)])
             dma("y", lambda: g.sync.dma_start(T.wqs[:], T.ws[:]), [], [A("wqs", 0, 512)])
         if t == 1:
             dma("y", lambda: g.sync.dma_start(T.vt[:], T.v[:]), [A("ce", 0, 1)], [A("vt", 0, 512)])
-        vscatter(A("ob", 0, 256), A("roff", 0, 16), A("jd", 0, 256))
+        once(first, for_proposals)
         if first:
-            au = ext("au", 2 * sum(nback))
-            pick("ur1", "uland", 16, A("el", 0, 8), [au])
+            pick("ur1", "uland", 8, A("el", 0, 8), [au])
+            pick("ur2", "uland", 8, A("el", 0, 8), [au], 32)
 
-        vhold(A("oh", 0, 64), A("ob", 0, 64), "m4")
-        if first:
-            pick("ur2", "uland", 16, A("el", 8, 16), [au])
-        vts(A("ol", 0, 16), A("oh", 3, 64, 4), pf(11), pf(12), ALU.mult, ALU.add)
-        vhold(A("oh", 64, 256), A("ob", 64, 256), "m4")
+        for a, b in ((0, 64), (64, 256)):
+            vhold(A("oh", a, b), A("ob", a, b), "m4")
+            vts(A("ol", a // 4, b // 4), A("oh", a + 3, b, 4), pf(11), pf(12), ALU.mult, ALU.add)
         scaled("s", A("at", 128, 256), X, 1.0, A("ol", 8, 16))
         scaled("v", A("at", 0, 128), X, 1.0, A("ol", 0, 8))
-        vts(A("ol", 16, 64), A("oh", 67, 256, 4), pf(11), pf(12), ALU.mult, ALU.add)
         quant("qa", 128 * t, 128 * t + 128, "at", 0)
-        mm(1, "ur1", 0, "qa", 128 * t, 128)
         mm(0, "ur2", 0, "qa", 128 * t, 128)
-        land = lambda name, s, r: A(name, 128 * t + 64 * slot(s, r), 128 * t + 64 * slot(s, r) + 64)
-        for name, to, codes in (("qa", "aland", True), ("qas", "alands", False)):
-            a = A(name, 128 * t, 128 * t + 64)
-            if handed(rank):
-                r = fwd(rank)[0]
-                op("g", send1(a, r, land(to, rank, r), codes, "aa%d" % t, topo.engines(core, cores[r])), [a], [])
+        mm(1, "ur1", 0, "qa", 128 * t, 128)
+        mm(2, "ur1", 0, "qa", 128 * t, 128)
+        land = lambda s, r: 128 * t + 64 * slot(s, r)
+        piece = lambda name, e, a, b: [(A(name + e, a, a + 64), A("aland" + e, b, b + 64))]
+        ways = list(zip(fwd(rank), both(rank, fwd(rank))))
+        if handed(rank):
+            ways = [(fwd(rank)[0], topo.engines(core, cores[fwd(rank)[0]]))]
+        for e in ("", "s"):
+            codes = send([(r, es, "aa%d" % t, piece("qa", e, 128 * t, land(rank, r))) for r, es in ways])
+
+        for c in range(32):
+            flag, score = A("cmp", 1024 * (c // 16) + c % 16, 1024 * (c // 16) + 1024, 16), A("sland", 32 * t + c, 32 * t + c + 1)
+            if c < K["ps"]:
+                act(A("sp", 64 * c, 64 * c + 64), A("ps", 512, 576), ACT.Sign, bias=score, scale=-1.0, after=[e1])
+                act(flag, A("sp", 64 * c, 64 * c + 64), ACT.Relu)
             else:
-                send(a, [(r, land(to, rank, r)) for r in fwd(rank)], codes, ["aa%d" % t] * 2)
-        vset(A("wb", 0, 320), 1.0)
+                o = 1024 * (c < 16)
+                vts(flag, A("ps", o, o + 64), score, None, ALU.is_lt, after=[e1 if c < 16 else e2])
+        for e in range(2):
+            for a in (0, 512):
+                vseg(A("pc", 1536 * e + 256 + a, 1536 * e + 768 + a), A("cmp", 1024 * e + a, 1024 * e + 512 + a))
+        for e in range(2):
+            vtr(A("pt", 160 * e, 160 * e + 64), A("pc", 1536 * e + 271, 1536 * e + 1280, 16))
+            vtr(A("pt", 160 * e + 64, 160 * e + 160), A("pc", 1536 * e + 15, 1536 * e + 1536, 16))
+            vseg(A("pp", 160 * e, 160 * e + 160), A("pt", 160 * e, 160 * e + 160))
+        vts(A("pm", 0, 16), A("pp", 160, 320), 64.0, None, ALU.max, off=A("fl", 0, 1))
+        vtt(A("fsend", 16 * t, 16 * t + 16), A("pp", 0, 160), A("pm", 0, 16), ALU.max, off=A("fl", 0, 1))
+        once(first, for_queue)
+        once(t == 1, for_ls)
+        place = lambda r: 16 * t + 8 * slot(rank, r)
+        mine = send([(r, es, "af%d" % t, [(A("fsend", 16 * t, 16 * t + 8), A("fland", place(r), place(r) + 8))])
+                     for r, es in zip(fwd(rank), both(rank, fwd(rank)))])
+        af = ext("af%d" % t, nfwd, mine, 1500)
 
-        e1, e2 = ext("sa%d" % t, nback[0]), ext("sb%d" % t, nback[1])
-        for c in range(16):
-            act(A("cmp", c, 1024, 16), A("ps", 512, 576), ACT.Sign, bias=A("sland", 32 * t + c, 32 * t + c + 1),
-                scale=-1.0, after=[e1])
-        for c in range(16):
-            vts(A("cmp", 1024 + c, 2048, 16), A("ps", 0, 64), A("sland", 32 * t + 16 + c, 32 * t + 17 + c), None,
-                ALU.is_lt, after=[e2])
-        pieces = [(0, 512), (512, 768), (768, 1024)]
-        for a, b in pieces:
-            act(A("cmp", a, b), A("cmp", a, b), ACT.Relu)
-        for a, b in [(1024, 1536), (1536, 2048)] + pieces:
-            vseg(A("pc", 256 + a, 256 + b), A("cmp", a, b))
-        vtr(A("pt", 0, 128), A("pc", 256 + 15, 2304, 16))
-        vtr(A("pt", 128, 288), A("pc", 15, 2560, 16))
-        vseg(A("pp", 0, 288), A("pt", 0, 288))
-        vtt(A("pm", 0, 14), A("pp", 15, 224, 16), A("pp", 79, 288, 16), ALU.max)
-        vts(A("fsend", 16 * t, 16 * t + 14), A("pm", 0, 14), 64.0, -192.0, ALU.max, ALU.add)
-        place = lambda r: 32 * t + 14 * slot(rank, r)
-        send(A("fsend", 16 * t, 16 * t + 14), [(r, A("fland", place(r), place(r) + 14)) for r in fwd(rank)], False,
-             ["af%d" % t] * 2)
-
-        if first:
-            iota(A("lj", 0, 8), [[14, 2], [1, 4]], 0, 0, True)
-            iota(A("fq", 0, 128), [[32, 4], [0, 32]], 0, 0)
-        aa = ext("aa%d" % t, 2 * ncodes)
         s = back(rank)[0]
+        aa = ext("aa%d" % t, 2 * ncodes, *((codes, 5000) if handed(s) or not K["hand"] else (mine, 4000)))
         if handed(s):
             r = fwd(s)[1]
-            for name, codes in (("aland", True), ("alands", False)):
-                op("g", send1(land(name, s, rank), r, land(name, s, r), codes, "aa%d" % t, inner(rank)), [], [], [aa])
+            for e in ("", "s"):
+                send([(r, topo.engines(core, cores[r]), "aa%d" % t, piece("aland", e, land(s, rank), land(s, r)))], [aa])
+        vset(A("wb", 0, 320), 1.0)
         scaled("s", A("vh", 512 + 4 * SV, 1280), X, 0.5, A("ol", 16 + SV // 4, 64))
-        if first:
-            quant("eq", 0, 512, "et", 0)
-            vts(pi(11), pi(0), 31, None, ALU.bitwise_and)
-            vtt(pi(12), pi(6), pi(0), ALU.add)
-            vts(pi(13), pi(0), 4, None, ALU.bitwise_and)
-            vts(pf(19), pf(1), 0.0078125, None, ALU.mult)
-            vcopy(pf(13), pi(11))
-            vts(pi(14), pi(12), 1, None, ALU.bitwise_and)
-            vcopy(A("xl", 0, 8), A("lj", 0, 8))
-            vts(pf(14), pi(13), 3.5, pf(12), ALU.mult, ALU.add)
-            vts(A("keyc", 0, 128), A("fq", 0, 128), pf(13), 0.0078125, ALU.add, ALU.mult)
-            vset(A("kr", 128, 130), -1024.0)
-            vts(A("qown", 0, 16), A("li", 0, 16), 0.125, pf(19), ALU.mult, ALU.add)
-            vts(pf(15), pi(14), 9.0, 4.0, ALU.mult, ALU.add)
-            vts(pf(16), pf(2), 0.0, -128.0 * UP, ALU.not_equal, ALU.mult)
-            vts(pf(18), pf(12), 512.0, None, ALU.add)
-            vts(A("kl", 0, 1), pf(15), pf(14), None, ALU.add)
-            vts(pf(17), pf(16), -128.0 * UP * DOWN, None, ALU.min)
-            scaled("s", A("ids", 0, 128), A("jd", 0, 128), TINY)
+        scaled("v", A("vh", 512, 512 + 4 * SV), X, 0.5, A("ol", 16, 16 + SV // 4))
         for b in range(4):
             mm(4 + b, "eq", 128 * b, "aland", 128 * t, 128, [aa])
-        scaled("v", A("vh", 512, 512 + 4 * SV), X, 0.5, A("ol", 16, 16 + SV // 4))
-        if t == 1:
-            quant("vq", 0, 128, "vt", 0)
-            vts(pf(19), pf(1), 0.0, 16.0, ALU.is_equal, ALU.mult)
-            vts(A("la", 0, 256), A("r16", 0, 256), pf(0), UP, ALU.is_equal, ALU.mult)
-            vts(pf(21), pf(1), 0.0, -128.0 * UP, ALU.not_equal, ALU.mult)
-            vts(pf(20), pf(19), pf(1), None, ALU.add)
-            vts(pf(23), pf(19), 1.0 / (16.0 * UP * DOWN), 1.0 / UP, ALU.mult, ALU.max)
-            vts(pf(22), pf(21), -128.0 * UP * DOWN, None, ALU.min)
-            vts(A("lb", 0, 256), A("r16", 0, 256), pf(20), DOWN, ALU.not_equal, ALU.max)
-            vtt(A("m16", 0, 256), A("la", 0, 256), A("lb", 0, 256), ALU.max)
-            act(A("fq", 0, 128), A("qrow", 0, 128), ACT.Identity, bias=128.0, scale=-0.0078125)
+            act(A("vh", b, 512, 4), A("ps", 2048 + 512 * b, 2048 + 512 * b + 128), ACT.Copy, scale=0.5)
         if last:
             act(A("tbl", 128, 320), A("ob", 64, 256), ACT.Identity, bias=-1.0)
 
-        af = ext("af%d" % t, nfwd)
-        came = A("fland", 32 * t, 32 * t + 28)
+        came = A("fland", 16 * t, 16 * t + 16)
         vtt(A("kx", 0, 128), came, A("keyc", 0, 128), ALU.add, off=A("xl", 0, 8), after=[af])
         vtt(A("ko", 0, 16), came, A("qown", 0, 16), ALU.add, off=A("kl", 0, 1), after=[af])
-        vts(A("pb", 0, 16), came, 63.0, None, ALU.min, off=A("kl", 0, 1))
+        vts(A("pb", 0, 16), came, 255.0, -192.0, ALU.min, ALU.add, off=A("kl", 0, 1), after=[af])
+        vts(A("pa", 0, 16), came, 255.0, None, ALU.min, off=A("kl", 0, 1), after=[af])
         vtr(A("kr", 0, 128), A("kx", 0, 128))
-        vts(A("pa", 0, 16), came, 63.0, 192.0, ALU.min, ALU.add, off=A("kl", 0, 1))
-        kown = lambda c: A("ko", c, c + 1)
-        for c in range(KS):
-            act(A("jk", 256 * c, 256 * c + 129), A("kr", 0, 129), ACT.Sign, bias=kown(c), scale=-1.0,
-                acc=A("ksum", c, c + 1))
-        for c in range(KS, 8):
-            vts(A("cmp", 128 * c, 128 * c + 128), A("kr", 0, 128), kown(c), None, ALU.is_lt)
-        placed = lambda c: vts(A("poff", c, c + 1), A("ksum", c, c + 1), 0.5, A("pa", c, c + 1), ALU.mult, ALU.add)
-        for c in range(KS, 8):
-            vscan(A("scn", 128 * c, 128 * c + 128), A("cmp", 128 * c, 128 * c + 128), A("ones", 0, 128),
-                  ALU.add, ALU.mult, A("pb", c, c + 1))
-        for c in range(KS - 1):
-            placed(c)
+        for c in range(8):
+            part = A("cmp", 128 * c, 128 * c + 128)
+            if c < KS:
+                act(A("jk", 256 * c, 256 * c + 129), A("kr", 0, 129), ACT.Sign, bias=A("ko", c, c + 1), scale=-1.0,
+                    acc=A("ksum", c, c + 1))
+                vts(A("poff", c, c + 1), A("ksum", c, c + 1), 0.5, A("pa", c, c + 1), ALU.mult, ALU.add)
+            else:
+                vts(part, A("kr", 0, 128), A("ko", c, c + 1), None, ALU.is_lt)
+                vscan(A("scn", 128 * c, 128 * c + 128), part, A("ones", 0, 128), ALU.add, ALU.mult, A("pb", c, c + 1))
         vts(A("poff", KS, 8), A("scn", 128 * KS + 127, 1024, 128), 129.0, None, ALU.add)
-        placed(KS - 1)
         vscatter(A("wb", 0, 320), A("poff", 0, 8), A("ids", 0, 128))
-        for b in range(4):
-            act(A("vh", b, 512, 4), A("ps", 2048 + 512 * b, 2048 + 512 * b + 128), ACT.Copy, scale=0.5)
-        vsum(A("cu", 0, 256), A("wb", 0, 256))
-        vhold(A("wh", 0, 256), A("wb", 0, 256), "m4")
-        vhold(A("ch", 0, 256), A("cu", 0, 256), "m4")
+        vsum(row("cu"), row("wb"))
+        vhold(row("wh"), row("wb"), "m4")
+        vhold(row("ch"), row("cu"), "m4")
         vts(A("lw", 0, 64), A("wh", 3, 256, 4), 1.0 / TINY, pf(17), ALU.mult, ALU.add)
         vtt(A("lf", 0, 64), A("ch", 3, 256, 4), A("lw", 0, 64), ALU.min)
         vts(A("ll", 0, 64), A("lf", 0, 64), pf(11), pf(18), ALU.mult, ALU.add)
+        if last:
+            vhold(row("wi"), row("wb"), "m16")
+            vhold(row("ci"), row("cu"), "m16")
+            act(A("lx", 0, 16), A("wi", 15, 256, 16), ACT.Identity, bias=pf(22), scale=1.0 / TINY)
+            vtt(A("lx", 16, 32), A("ci", 15, 256, 16), A("lx", 0, 16), ALU.min)
+            vts(A("lk", 0, 16), A("lx", 16, 32), pf(23), 127.0, ALU.mult, ALU.add)
+            act(A("lsb", 0, 256), A("tbl", 0, 320), ACT.Copy, off=A("lk", 0, 16))
+            vtt(A("lsb", 256, 384), A("kr", 0, 128), A("qrow", 0, 128), ALU.add)
+            outs.append(dma("s", lambda: g.scalar.dma_start(T.ls[:], T.lsb[0:128:16, :]), [A("lsb", 0, 384)], []))
 
         V = A("vh", 0, 1280)
-        scaled("s", A("gg", 4 * GV, 512), V, 1.0, A("ll", GV // 4, 32))
-        scaled("v", A("gg", 0, 4 * GV), V, 1.0, A("ll", 0, GV // 4))
-        scaled("s", A("gg", 512, 1024), V, 1.0, A("ll", 32, 64))
-        if last:
-            vhold(A("wi", 0, 256), A("wb", 0, 256), "m16")
+        cuts = [int(w[1:]) for w in K["gather"].split()] + [256]
+        for w, a, b in zip(K["gather"].split(), cuts, cuts[1:]):
+            scaled(w[0], A("gg", 4 * a, 4 * b), V, 1.0, A("ll", a // 4, b // 4))
         vtt(A("zt", 0, 4), A("gg", 0, 4), A("gg", 0, 4), ALU.add)
-        vtt(A("zt", 4, 512), A("gg", 4, 512), A("gg", 0, 508), ALU.add)
-        if last:
-            vhold(A("ci", 0, 256), A("cu", 0, 256), "m16")
-        bank = lambda h, b: 4 * (1 - h) + b
-        for h in range(2):
-            a, b = ((512, 768), (768, 1024))[h]
+        for a, b in ((4, 512), (512, 768), (768, 1024)):
             vtt(A("zt", a, b), A("gg", a, b), A("gg", a - 4, b - 4), ALU.add)
+        bank = lambda h, b: 4 * (1 - h) + b
+        plane = lambda name, h, b: A(name, 512 * h + b, 512 * h + 512, 4)
+        for h in range(2):
             quant("zq", 128 * h, 128 * h + 128, "zt", 512 * h)
+            scaled("s", A("z32", 512 * h, 512 * h + 512), A("zt", 512 * h, 512 * h + 512), 32.0)
             for b in range(4):
                 mm(bank(h, b), "wq", 128 * b, "zq", 128 * h, 128)
-            scaled("s", A("z32", 512 * h, 512 * h + 512), A("zt", 512 * h, 512 * h + 512), 32.0)
-        plane = lambda name, h, b: A(name, 512 * h + b, 512 * h + 512, 4)
         for h in range(2):
             for b in range(4):
                 vtt(plane("x32", h, b), A("ps", 512 * bank(h, b), 512 * bank(h, b) + 128), plane("z32", h, b), ALU.add)
-                if h == 1 and b < 1:
-                    scaled("s", plane("xt", h, b), plane("x32", h, b), 0.03125)
+                scaled(K["xc"][4 * h + b], plane("xt", h, b), plane("x32", h, b), 0.03125)
+            if not last:
+                scores(h, "xt")
+                continue
+            a, b = 128 * h, 128 * h + 128
+            quant("xq", a, b, "xt", 4 * a)
+            mm(4 + h, "vq", 0, "xq", a, 128)
+            scaled("sv"[h], A("yb", a, b), A("ps", 2048 + 512 * h, 2048 + 512 * h + 128), 1.0)
+            outs.append(dma("y", lambda a=a, b=b: g.sync.dma_start(T.oc[:, 4 * a:4 * b], T.xq[:, a:b].bitcast(dt.uint8)),
+                            [A("xq", a, b)], [], 3000 - 600 * h))
             if h == 0:
-                scaled("s", A("xt", 0, 512), A("x32", 0, 512), 0.03125)
-        for b in range(1, 4):
-            scaled("v", plane("xt", 1, b), plane("x32", 1, b), 0.03125)
-        quant("xq", 0, 128, "xt", 0)
-        if last:
-            mm(4, "vq", 0, "xq", 0, 128)
-        quant("xq", 128, 256, "xt", 512)
-
-    mm(5, "vq", 0, "xq", 128, 128)
-    outs.append(dma("y", lambda: g.sync.dma_start(T.oc[:], T.xq[:].bitcast(dt.uint8)), [A("xq", 0, 256)], []))
-    act(A("lx", 0, 16), A("wi", 15, 256, 16), ACT.Identity, bias=pf(22), scale=1.0 / TINY)
-    scaled("s", A("yb", 0, 128), A("ps", 2048, 2176), 1.0)
-    vtt(A("lg", 0, 16), A("ci", 15, 256, 16), A("lx", 0, 16), ALU.min)
-    vtt(A("lsb", 256, 384), A("kr", 0, 128), A("fq", 0, 128), ALU.add)
-    vts(A("lk", 0, 16), A("lg", 0, 16), pf(23), 127.0, ALU.mult, ALU.add)
-    scaled("v", A("yb", 128, 256), A("ps", 2560, 2688), 1.0)
-    act(A("lsb", 0, 256), A("tbl", 0, 320), ACT.Copy, off=A("lk", 0, 16))
+                outs.append(dma("s", lambda: g.scalar.dma_start(T.y[:, 0:128], T.yb[:, 0:128]), [A("yb", 0, 128)], [],
+                                2500))
     for k in range(4):
-        outs.append(dma("y", lambda k=k: g.sync.dma_start(T.osc[4 * k:4 * k + 4, :], T.xqs[32 * k:32 * k + 4, :]),
+        outs.append(dma("sy"[k % 2], lambda k=k: Q["sy"[k % 2]].dma_start(T.osc[4 * k:4 * k + 4, :],
+                                                                         T.xqs[32 * k:32 * k + 4, :]),
                         [A("xqs", 0, 256)], []))
-    outs.append(dma("y", lambda: g.sync.dma_start(T.y[:], T.yb[:]), [A("yb", 0, 256)], []))
-    outs.append(dma("s", lambda: g.scalar.dma_start(T.ls[:], T.lsb[0:128:16, :]), [A("lsb", 0, 384)], []))
-    op("g", lambda: g.wait_ge(T.sem.lsent, sent[0]), [], [], outs)
+    outs.append(dma("y", lambda: g.sync.dma_start(T.y[:, 128:256], T.yb[:, 128:256]), [A("yb", 128, 256)], []))
+    op("g", lambda: g.wait_ge(T.sem.lsent, sent[0]), [], [], 0, outs)
 
-    pools = {False: [["c%d" % i, 0, None] for i in range(NCS)], True: [["d%d" % i, 0, None] for i in range(NDS)]}
-    for i, o in enumerate(ops):
+    N = len(ops)
+    pre = [[(d, (K["near"] if ops[d]["q"] == o["q"] else WAKE) + ops[d]["late"]) for d in o["deps"]]
+           + [(d, 0) for d in o["behind"]] for o in ops]
+    post = [[] for o in ops]
+    for i in range(N):
+        for d, w in pre[i]:
+            post[d].append((i, w))
+    busy, queue = [o["busy"] for o in ops], [o["q"] for o in ops]
+
+    def lay(before, after, key):
+        end, taken = [0] * N, {k: [] for k in Q}
+        open_ = [len(b) for b in before]
+        can = sorted([(key[i], i) for i in range(N) if not open_[i]], reverse=True)
+        while can:
+            i = can.pop()[1]
+            at = max([0] + [end[d] + w for d, w in before[i]])
+            if queue[i] is not None:
+                spans = taken[queue[i]]
+                k = len(spans)
+                while k and spans[k - 1][1] > at:
+                    k -= 1
+                while k < len(spans) and spans[k][0] < at + busy[i]:
+                    at = max(at, spans[k][1])
+                    k += 1
+                spans.insert(k, (at, at + busy[i]))
+            end[i] = at + busy[i]
+            for j, w in after[i]:
+                open_[j] -= 1
+                if not open_[j]:
+                    can.append((key[j], j))
+            can.sort(reverse=True)
+        return end
+
+    def relay(key):
+        end = lay(pre, post, key)
+        way = lay(post, pre, [-e for e in end])
+        return lay(pre, post, [-w for w in way])
+
+    kind = handed(rank)
+    if kind not in LAID:
+        way = [0] * N
+        for i in range(N - 1, -1, -1):
+            way[i] = busy[i] + max([0] + [w + way[j] for j, w in post[i]])
+        end = relay([-w for w in way])
+        seed = [1]
+
+        def some(a, b):
+            seed[0] = seed[0] * 48271 % 2147483647
+            return a + (b - a) * seed[0] / 2147483647
+
+        for _ in range(K["shakes"]):
+            mid, span = some(0, max(end)), some(500, 4000)
+            new = relay([end[i] - busy[i] + (some(-400, 400) if abs(end[i] - mid) < span else 0) for i in range(N)])
+            if max(new) <= max(end):
+                end = new
+        LAID[kind] = end
+    end = LAID[kind]
+    order = sorted(range(N), key=lambda i: (end[i] - busy[i], end[i], i))
+
+    known = {k: 0 for k in Q}
+    place_of = {i: k for k, i in enumerate(order)}
+    bunches = []
+    for i in order:
+        o = ops[i]
+        o["k"] = 1 << i
         if o["q"] is None:
-            o["at"] = o["ext"]
+            o["bunch"] = {"at": o["ext"], "k": o["k"]}
             continue
-        for w in o["waits"]:
-            Q[o["q"]].wait_ge(T.sem[ops[w]["at"][0]], ops[w]["at"][1])
-        ins = o["fn"]()
-        if o.get("sig"):
-            s = [p for p in pools[o["dma"]] if p[2] is None or o["ki"] >> p[2] & 1][0]
-            inc = 16 if o["dma"] else 1
-            s[1] += inc
-            s[2] = i
-            ins.then_inc(T.sem[s[0]], inc)
-            o["at"] = (s[0], s[1])
+        o["waits"], fresh = [], {}
+        for d in sorted(o["deps"], key=lambda d: -place_of[d]):
+            if not known[o["q"]] >> d & 1:
+                if "bunch" not in ops[d]:
+                    if ops[d]["dma"] not in fresh:
+                        fresh[ops[d]["dma"]] = {"calls": [], "k": 0, "dma": ops[d]["dma"]}
+                        bunches.append(fresh[ops[d]["dma"]])
+                    ops[d]["bunch"] = fresh[ops[d]["dma"]]
+                    ops[d]["bunch"]["calls"].append(d)
+                    ops[d]["bunch"]["k"] |= ops[d]["k"]
+                if not any(b is ops[d]["bunch"] for b in o["waits"]):
+                    o["waits"].append(ops[d]["bunch"])
+                known[o["q"]] |= ops[d]["bunch"]["k"]
+        o["ki"] = known[o["q"]]
+        o["k"] |= o["ki"] | (0 if o["group"] is None else ops[o["group"]]["k"])
+    pools = {False: [["c%d" % i, 0, 0] for i in range(NCS)], True: [["d%d" % i, 0, 0] for i in range(NDS)]}
+    for b in sorted(bunches, key=lambda b: min(place_of[d] for d in b["calls"])):
+        s = [p for p in pools[b["dma"]] if all(ops[d]["ki"] & p[2] == p[2] for d in b["calls"])][0]
+        s[1] += len(b["calls"]) * (16 if b["dma"] else 1)
+        s[2] = sum(1 << d for d in b["calls"])
+        b["at"] = (s[0], s[1])
+
+    for i in order:
+        o = ops[i]
+        if o["q"] is not None:
+            for b in o["waits"]:
+                Q[o["q"]].wait_ge(T.sem[b["at"][0]], b["at"][1])
+            ins = o["fn"]()
+            if "bunch" in o:
+                ins.then_inc(T.sem[o["bunch"]["at"][0]], 16 if o["dma"] else 1)

from concourse.bass import DstId, RemoteDMATransfer
from concourse.mybir import dt, AluOpType, ActivationFunctionType

ALU = AluOpType
ACT = ActivationFunctionType
R = 3
BIG = 1.0e29
F8 = "float8_e4m3fn_x4"
UP, DOWN, TINY = 2.0 ** 21, 2.0 ** -51, 2.0 ** -20
CYCLE, FIX, GATHER, SCATTER, WAKE, CALL = 0.9, 60, 1.35, 3.2, 255, 800
K = {
    "blocks": ("sssssvv", "ssssvvvv", "sssssvv"),
    "quants": ((0, 192), (256, 384), (384, 512), (512, 640), (640, 768)),
    "ps": 12,
    "ks": 5,
    "sv": 96,
    "gather": "v0 s64 v128 s160",
    "xc": "ssssssvv",
    "shakes": 2600,
    "hand": False,
    "add": 0,
    "near": 255,
}


def _s(n, d):
    return ("sbuf", [128, n], d)


SCRATCH = {
    "ps": ("psum", [128, 4096], "float32"),
    "xin": _s(1024, "bfloat16"), "xt": _s(1024, "bfloat16"), "ut": _s(512, "bfloat16"), "vt": _s(512, "bfloat16"),
    "uq": _s(128, F8), "uqs": _s(128, "uint8"), "ur0": _s(128, F8), "ur0s": _s(128, "uint8"),
    "upk": _s(32, F8), "upks": _s(32, "uint8"), "uland": _s(64, F8), "ulands": _s(64, "uint8"),
    "ur1": _s(128, F8), "ur1s": _s(128, "uint8"), "ur2": _s(128, F8), "ur2s": _s(128, "uint8"),
    "vq": _s(128, F8), "vqs": _s(128, "uint8"), "wq": _s(512, F8), "wqs": _s(512, "uint8"),
    "et": _s(2048, "bfloat16"), "ones": _s(512, "bfloat16"), "eq": _s(512, F8), "eqs": _s(512, "uint8"),
    "g1": _s(512, "bfloat16"), "g2": _s(1024, "bfloat16"), "gq": _s(256, F8), "gqs": _s(256, "uint8"),
    "ft": _s(3072, "bfloat16"), "fc": _s(768, F8), "fcs": _s(768, "uint8"),
    "xq": _s(256, F8), "xqs": _s(256, "uint8"), "zq": _s(256, F8), "zqs": _s(256, "uint8"),
    "qa": _s(128 * R, F8), "qas": _s(128 * R, "uint8"), "aland": _s(128 * R, F8), "alands": _s(128 * R, "uint8"),
    "x32": _s(1024, "bfloat16"), "vh": _s(1280, "bfloat16"), "gg": _s(1024, "bfloat16"),
    "zt": _s(1024, "bfloat16"), "z32": _s(1024, "bfloat16"), "at": _s(512, "bfloat16"),
    "d1": _s(256, "float32"), "hs": _s(256, "float32"), "ssend": _s(16 * R, "float32"), "sland": _s(32 * R, "float32"),
    "lj": _s(8, "int32"), "fl": _s(2, "uint16"),
    "nes": _s(256, "bfloat16"), "base": _s(16, "float32"), "bas2": _s(8, "float32"), "acc": _s(32, "float32"),
    "lat": _s(256, "float32"), "la": _s(256, "bfloat16"), "lb": _s(256, "bfloat16"), "ce": _s(256, "float32"),
    "sg": _s(4096, "bfloat16"), "sp": _s(1024, "bfloat16"), "jk": _s(2048, "bfloat16"),
    "cmp": _s(2048, "bfloat16"), "scn": _s(4096, "bfloat16"), "pc": _s(3072, "bfloat16"),
    "roff": _s(16, "uint16"), "ob": _s(256, "bfloat16"), "oh": _s(256, "bfloat16"), "ol": _s(64, "uint16"),
    "m4": _s(256, "bfloat16"), "m16": _s(256, "bfloat16"), "c4": _s(12, "float32"),
    "wh": _s(256, "bfloat16"), "ch": _s(256, "bfloat16"), "lw": _s(64, "float32"), "lf": _s(64, "float32"),
    "ll": _s(64, "uint16"), "wi": _s(256, "bfloat16"), "ci": _s(256, "bfloat16"), "lx": _s(32, "float32"),
    "lk": _s(16, "uint16"),
    "pt": _s(320, "bfloat16"), "pp": _s(320, "bfloat16"), "pm": _s(16, "float32"),
    "fsend": _s(16 * R, "bfloat16"), "fland": _s(16 * R, "bfloat16"),
    "kx": _s(128, "float32"), "kr": _s(130, "float32"), "ko": _s(16, "float32"),
    "xl": _s(8, "uint16"), "kl": _s(2, "uint16"),
    "pa": _s(16, "float32"), "pb": _s(16, "float32"), "ksum": _s(8, "float32"),
    "poff": _s(8, "uint16"), "wb": _s(320, "bfloat16"), "cu": _s(256, "bfloat16"),
    "negm": _s(256, "float32"), "hold": _s(256, "float32"), "r16": _s(256, "bfloat16"),
    "seg": _s(512, "bfloat16"), "cc": _s(16, "float32"), "jd": _s(256, "bfloat16"),
    "pi": _s(24, "int32"), "pf": _s(48, "float32"), "li": _s(16, "int32"),
    "cl": _s(2, "uint16"), "el": _s(16, "uint16"), "rl": _s(8, "uint16"),
    "keyc": _s(128, "float32"), "qown": _s(16, "float32"), "ids": _s(128, "bfloat16"), "qrow": _s(128, "float32"),
    "tbl": _s(320, "float32"), "lsb": _s(384, "float32"), "fq": _s(128, "float32"), "yb": _s(256, "float32"),
}
NCS, NDS = 100, 24
SEMAPHORES = (["c%d" % i for i in range(NCS)] + ["d%d" % i for i in range(NDS)] + ["lsent", "au"]
              + ["%s%d" % (k, t) for k in ("sa", "sb", "aa", "af") for t in range(R)])
LAID = {}


def split_engines(topo, src, d1, d2):
    e1, e2 = topo.engines(src, d1), topo.engines(src, d2)
    if len(e1) == len(e2):
        h = len(e1) // 2
        e1, e2 = e1[:h], e2[h:]
    elif len(e1) > len(e2):
        e1 = [e for e in e1 if e not in e2]
    else:
        e2 = [e for e in e2 if e not in e1]
    return [e1, e2]


def deal(engines, k):
    shares = [engines]
    while len(shares) < k:
        a = shares.pop(0)
        shares += [a[:len(a) // 2], a[len(a) // 2:]]
    return shares


def rank_program(g, core, T, topo):
    rank = T.rank_of(core)
    if rank is None:
        return
    n = len(T.cores)
    cores = T.cores
    Q = {"g": g, "v": g.vector, "s": g.scalar, "t": g.tensor, "y": g.sync}

    ops = []
    log = {}
    exts = {}
    tip = {}
    gate = []

    def bits(a):
        if a[0] == "ps":
            return sum(1 << k for k in range(a[1] // 512, (a[2] - 1) // 512 + 1))
        if a[3] == 1:
            return ((1 << (a[2] - a[1])) - 1) << a[1]
        return sum(1 << k for k in range(a[1], a[2], a[3]))

    def ext(sem, count, mine, late):
        if sem not in exts:
            exts[sem] = len(ops)
            ops.append({"ext": (sem, count), "q": None, "deps": set(), "behind": {mine}, "busy": 0, "late": late})
        return exts[sem]

    def op(q, fn, rd, wr, busy, after=(), dma=False, group=None, late=0):
        me = len(ops)
        deps = set(after)
        behind = {tip[q]} if q in tip and q in "gty" else set()
        for a, w in [(a, False) for a in rd] + [(a, True) for a in wr]:
            m = bits(a)
            for (o, om, ow, oq) in log.get(a[0], []):
                if om & m and (w or ow or (a[0] == "ps" and oq != q)) and o != group:
                    deps.add(o)
        behind |= set(gate)
        tip[q] = me
        ops.append({"q": q, "fn": fn, "deps": deps, "behind": behind, "busy": busy, "late": late, "dma": dma,
                    "group": group})
        for a, w in [(a, False) for a in rd] + [(a, True) for a in wr]:
            m = bits(a)
            if w:
                log[a[0]] = [e for e in log.get(a[0], []) if e[1] & ~m]
            log.setdefault(a[0], []).append((me, m, w, q))
        return me

    def size(a):
        return len(range(a[1], a[2], a[3]))

    def cost(out, *ins, off=None, halves=True):
        if off is not None:
            return FIX + GATHER * size(out)
        narrow = halves and all(SCRATCH[a[0]][2] in ("bfloat16", "uint16") for a in (out,) + ins)
        return K["add"] + max(FIX - K["add"], CYCLE * size(out) * (0.5 if narrow else 1.0))

    def A(name, a, b, s=1):
        return (name, a, b, s)

    def ap(a):
        return T[a[0]][:, a[1]:a[2]] if a[3] == 1 else T[a[0]][:, a[1]:a[2]:a[3]]

    def isap(a):
        return isinstance(a, tuple)

    def src(a, off):
        return ap(a) if off is None else ap(a).indirect(ap(off))

    def vts(out, in0, s1, s2, o0, o1=None, off=None, after=()):
        rd = [in0] + [s for s in (s1, s2, off) if isap(s)]
        f = lambda s: ap(s) if isap(s) else s
        more = () if o1 is None else (o1,)
        return op("v", lambda: g.vector.tensor_scalar(ap(out), src(in0, off), f(s1), None if o1 is None else f(s2),
                                                      o0, *more), rd, [out], cost(out, in0, off=off), after)

    def vtt(out, in0, in1, o, off=None, after=()):
        return op("v", lambda: g.vector.tensor_tensor(ap(out), src(in0, off), ap(in1), o),
                  [in0, in1] + ([off] if off else []), [out], cost(out, off=off, halves=False), after)

    def vcopy(out, in_):
        return op("v", lambda: g.vector.tensor_copy(ap(out), ap(in_)), [in_], [out], cost(out, in_))

    def vscatter(win, off, in_):
        return op("v", lambda: g.vector.tensor_copy(ap(win).indirect(ap(off)), ap(in_)), [in_, off], [win],
                  FIX + SCATTER * size(in_))

    def vscan(out, d0, d1, o0, o1, init=0.0):
        return op("v", lambda: g.vector.tensor_tensor_scan(ap(out), ap(d0), ap(d1), ap(init) if isap(init) else init,
                                                           o0, o1),
                  [d0, d1] + ([init] if isap(init) else []), [out], cost(out, d0, d1))

    def vsum(out, d, init=0.0):
        return vscan(out, d, d, ALU.add, ALU.max, init)

    def vseg(out, d):
        return vscan(out, A("seg", 0, out[2] - out[1]), d, ALU.mult, ALU.add)

    def vhold(out, row, mask):
        return vscan(out, row, A(mask, 0, out[2] - out[1]), ALU.max, ALU.mult)

    def vtr(out, in_, after=()):
        return op("v", lambda: g.vector.transpose(ap(out), ap(in_)), [in_], [out], cost(out, in_), after)

    def vset(out, c):
        return op("v", lambda: g.vector.memset(ap(out), c), [], [out], cost(out))

    def quant(c, a, b, tile, e0):
        t, o, s = A(tile, e0, e0 + 4 * (b - a)), A(c, a, b), A(c + "s", a, b)
        return op("v", lambda: g.vector.quantize_mx(ap(o), ap(s), ap(t)), [t], [o, s], 0.29 * CYCLE * size(t))

    def act(out, in_, func, bias=None, scale=None, acc=None, off=None, after=()):
        rd = [in_] + [s for s in (bias, scale, off) if isap(s)]
        kw = {}
        if bias is not None:
            kw["bias"] = bias
        if scale is not None:
            kw["scale"] = scale

        def fn():
            k = {a: (ap(b) if isap(b) else b) for a, b in kw.items()}
            if acc is not None:
                k["accum_out"] = ap(acc)
            return g.scalar.activation(ap(out), src(in_, off), func, **k)
        return op("s", fn, rd, [out] + ([acc] if acc else []),
                  cost(out, off=off, halves=False) + (20 if acc or off else 0), after)

    def scaled(q, out, in_, c, off=None):
        if q == "v":
            return vts(out, in_, c, None, ALU.mult, off=off)
        return act(out, in_, ACT.Copy, scale=c, off=off)

    def zero(a):
        return scaled("s", a, A("ones", 0, size(a)), 0.0)

    def pick(dst, win, w, off, after=(), w0=0):
        m = 16 * (off[2] - off[1])
        o, i = A(dst, 0, m), A(win, w0, w0 + w)
        op("v", lambda: g.vector.tensor_copy(ap(o).bitcast(dt.uint32), ap(i).bitcast(dt.uint32).indirect(ap(off))),
           [i, off], [o], cost(o, off=off), after)
        o2, i2 = A(dst + "s", 0, m), A(win + "s", w0, w0 + w)
        op("s", lambda: g.scalar.activation(ap(o2), ap(i2).indirect(ap(off)), ACT.Copy), [i2, off], [o2],
           cost(o, off=off), after)

    def mm(bank, w, w0, x, x0, m, after=(), start=True, stop=True, group=None):
        o = A("ps", 512 * bank, 512 * bank + m)
        r = [A(w, w0, w0 + 128), A(w + "s", w0, w0 + 128), A(x, x0, x0 + m), A(x + "s", x0, x0 + m)]
        return op("t", lambda: g.tensor.matmul_mx(ap(o), ap(r[0]), ap(r[1]), ap(r[2]), ap(r[3]), start, stop),
                  r, [o], 0.85 * CYCLE * (m + 16), after, group=group)

    def iota(out, pattern, base, cm, whole=False):
        if whole:
            return op("g", lambda: g.iota(ap(out), pattern, base, cm), [], [out], 130 + 2 * CYCLE * size(out))
        return op("g", lambda: g.iota(ap(out), pattern, base, cm, allow_small_or_imprecise_dtypes=True), [], [out],
                  130 + 2 * CYCLE * size(out))

    def dma(q, fn, rd, wr, late=2000):
        return op(q, fn, rd, wr, 50, dma=True, late=late)

    sent = [0]

    def send(ways, after=()):
        def fn():
            f = lambda a: ap(a).bitcast(dt.uint8) if SCRATCH[a[0]][2] == F8 else ap(a)
            tr = []
            for r, engines, sem, pieces in ways:
                ad = topo.addr(cores[r])
                for (a, b), es in zip(pieces, deal(engines, len(pieces))):
                    tr.append(RemoteDMATransfer(dst_ids=[DstId(rid=ad[0], pnc=ad[1])], remote_sem=T.sem[sem],
                                                dma_engine_mask=sum(1 << e for e in es), src=f(a), dst=f(b)))
            g.remote_dma_fused(tr, local_sem=T.sem.lsent)
        sent[0] += sum(len(w[1]) for w in ways)
        return op("g", fn, [] if after else [a for w in ways for a, b in w[3]], [], CALL, after)

    def both(s, dsts):
        return split_engines(topo, cores[s], cores[dsts[0]], cores[dsts[1]])

    def fwd(r):
        return [(r + 1) % n, (r + 2) % n]

    def back(r):
        return [(r - 1) % n, (r - 2) % n]

    def count(s, dsts):
        return len(both(s, dsts)[dsts.index(rank)])

    def slot(s, r):
        return sorted(back(r)).index(s)

    def handed(s):
        a, b = [topo.chip(cores[r]) for r in fwd(s)]
        return K["hand"] and a == b != topo.chip(cores[s])

    def codes_count(s):
        if not handed(s):
            return count(s, fwd(s))
        r = fwd(s)[0]
        return len(topo.engines(cores[s if r == rank else r], core))

    ncodes = sum(codes_count(s) for s in back(rank))
    nfwd = sum(count(s, fwd(s)) for s in back(rank))
    nback = [count(e, back(e)) for e in fwd(rank)]

    dma("s", lambda: g.scalar.dma_start(T.ut[:], T.u[:]), [], [A("ut", 0, 512)], 1900)
    for h in range(2):
        dma("y", lambda h=h: g.sync.dma_start(T.xin[:, 512 * h:512 * h + 512], T.x[:, 512 * h:512 * h + 512]),
            [], [A("xin", 512 * h, 512 * h + 512)], 2800 + 900 * h)

    FT = [0, 128, 256, 384, 512, 640, 768]
    pi = lambda k, m=1: A("pi", k, k + m)
    pf = lambda k, m=1: A("pf", k, k + m)
    row = lambda name: A(name, 0, 256)
    iota(pi(0, 2), [[12, 2]], 0, 1, True)
    iota(A("li", 0, 16), [[1, 16]], 0, 0, True)
    iota(row("r16"), [[0, 16], [1, 16]], 1, 0)
    iota(A("g1", 0, 512), [[1, 8], [0, 64]], 0, 0)
    iota(row("jd"), [[1, 256]], 1, 0)
    vset(A("ones", 0, 512), 1.0)
    vts(pi(4, 2), pi(0, 2), 15, None, ALU.bitwise_and)
    vts(pi(6), pi(0), 4, None, ALU.logical_shift_right)
    vts(pf(0), pi(4), 1.0, None, ALU.add)
    vcopy(pf(1), pi(4))
    vcopy(pf(4), pi(6))
    vts(A("rl", 0, 8), A("li", 0, 8), 16.0, None, ALU.mult)
    vts(A("cl", 0, 2), pi(4, 2), 16.0, 112.0, ALU.mult, ALU.min)
    for a in (0, 256):
        act(A("seg", a, a + 256), row("r16"), ACT.Sign, bias=-1.0)
    act(row("hold"), row("seg"), ACT.Identity, bias=-5 * BIG, scale=5 * BIG)
    vts(row("negm"), row("r16"), pf(0), -BIG, ALU.not_equal, ALU.mult)
    vts(A("g2", 0, 512), A("g1", 0, 512), pf(4), None, ALU.is_equal)
    vts(A("g2", 512, 1024), A("g1", 0, 512), pf(4), -1.0, ALU.is_equal, ALU.mult)
    quant("gq", 0, 128, "g2", 0)
    quant("gq", 128, 256, "g2", 512)
    vts(row("la"), row("r16"), pf(0), -1024.0, ALU.is_equal, ALU.mult)
    vts(row("lb"), row("r16"), pf(1), 2048.0, ALU.is_equal, ALU.mult)
    vtt(row("lat"), row("la"), row("lb"), ALU.add)
    vts(pf(5), pf(1), -1.0, 15.0, ALU.mult, ALU.add)
    vts(pf(6), pf(1), 0.0, 2048.0, ALU.is_equal, ALU.mult)
    vts(pf(7), pf(1), 15.0, -1024.0, ALU.is_equal, ALU.mult)
    vts(pf(8), pf(5), pf(6), pf(7), ALU.add, ALU.add)
    act(pf(9), pf(6), ACT.Identity, bias=1024.0, scale=-1.0)
    vts(A("cc", 0, 16), A("li", 0, 16), 16.0, pf(8), ALU.mult, ALU.add)
    for a in (0, 4):
        zero(A("ft", 4 * (FT[a] + 80), 4 * FT[a + 1]))
        zero(A("ft", 4 * (FT[a + 1] + 16), 4 * FT[a + 2]))
    zero(A("acc", 0, 25, 24))

    def for_lists():
        vts(pi(8, 2), pi(4, 2), 2, None, ALU.logical_shift_right)
        vts(pi(10), pi(0), 3, None, ALU.bitwise_and)
        vcopy(pf(2, 2), pi(8, 2))
        vcopy(A("el", 0, 8), A("li", 0, 8))
        vts(A("c4", 0, 4), A("li", 0, 4), pf(2), UP, ALU.is_equal, ALU.mult)
        vts(A("c4", 4, 8), A("li", 0, 4), pf(3), DOWN, ALU.not_equal, ALU.max)
        vtt(A("c4", 8, 12), A("c4", 0, 4), A("c4", 4, 8), ALU.max)
        for j in range(4):
            act(A("m4", j, 256, 4), A("ones", 0, 64), ACT.Copy, scale=A("c4", 8 + j, 9 + j))
        vts(pf(10), pf(2), 0.0, 4.0 / (UP * DOWN), ALU.is_equal, ALU.mult)
        vts(pf(11), pf(10), 4.0 / UP, None, ALU.max)
        vts(pf(12), pi(10), -4.0, None, ALU.add)
        for a in (A("at", 256, 512), A("pc", 15, 256, 16), A("pc", 1295, 1792, 16), A("pc", 2831, 3072, 16)):
            zero(a)

    def for_proposals():
        vtt(pi(12), pi(6), pi(0), ALU.add)
        vts(pi(13), pi(0), 4, None, ALU.bitwise_and)
        vts(pi(14), pi(12), 1, None, ALU.bitwise_and)
        vcopy(pf(15), pi(14))
        vts(pf(25), pi(13), -20.0, 80.0, ALU.mult, ALU.add)
        vts(pf(26), pf(25), pf(15), 15.0, ALU.mult, ALU.add)
        vts(A("fl", 0, 1), pi(10), 16.0, pf(26), ALU.mult, ALU.add)
        for b in range(4):
            zero(A("et", 512 * b, 512 * b + 512))

    def for_queue():
        vts(pf(27), pi(0), 1.0, None, ALU.add)
        for b in range(4):
            vts(A("et", 512 * b + b, 512 * b + 512, 4), A("jd", 0, 128), pf(27), None, ALU.is_equal)
        quant("eq", 0, 512, "et", 0)
        vts(pi(11), pi(0), 31, None, ALU.bitwise_and)
        vcopy(pf(13), pi(11))
        act(pf(14), pf(12), ACT.Identity, bias=4.0)
        act(pf(18), pf(12), ACT.Identity, bias=512.0)
        scaled("s", pf(19), pf(1), 0.0078125)
        vcopy(A("xl", 0, 8), A("lj", 0, 8))
        vts(A("kl", 0, 1), pi(13), 2.0, pf(14), ALU.mult, ALU.add)
        vts(A("keyc", 0, 128), A("fq", 0, 128), pf(13), 0.0078125, ALU.add, ALU.mult)
        vts(A("qown", 0, 16), A("li", 0, 16), 0.125, pf(19), ALU.mult, ALU.add)
        scaled("s", A("kr", 128, 130), A("ones", 0, 2), -1024.0)
        scaled("s", A("ids", 0, 128), A("jd", 0, 128), TINY)
        vts(pf(16), pf(2), 0.0, -128.0 * UP, ALU.not_equal, ALU.mult)
        vts(pf(17), pf(16), -128.0 * UP * DOWN, None, ALU.min)

    def for_ls():
        quant("vq", 0, 128, "vt", 0)
        vts(pf(24), pf(1), 0.0, 16.0, ALU.is_equal, ALU.mult)
        vts(pf(20), pf(24), pf(1), None, ALU.add)
        vts(pf(21), pf(1), 0.0, -128.0 * UP, ALU.not_equal, ALU.mult)
        vts(pf(22), pf(21), -128.0 * UP * DOWN, None, ALU.min)
        vts(pf(23), pf(24), 1.0 / (16.0 * UP * DOWN), 1.0 / UP, ALU.mult, ALU.max)
        vts(row("la"), row("r16"), pf(0), UP, ALU.is_equal, ALU.mult)
        vts(row("lb"), row("r16"), pf(20), DOWN, ALU.not_equal, ALU.max)
        vtt(row("m16"), row("la"), row("lb"), ALU.max)
        act(A("tbl", 0, 128), A("jd", 0, 128), ACT.Identity, bias=255.0)
        act(A("qrow", 0, 128), A("jd", 0, 128), ACT.Identity, bias=-63.9921875, scale=-0.0078125)

    def once(now, make):
        if now:
            gate.append(len(ops) - 1)
            make()
            gate.pop()

    quant("uq", 0, 128, "ut", 0)
    pick("ur0", "uq", 128, A("rl", 0, 8))
    pick("upk", "uq", 128, A("cl", 0, 2))
    mine = send([(s, es, "au", [(A("upk", 0, 8), A("uland", 32 * j, 32 * j + 8)),
                                (A("upks", 0, 32), A("ulands", 32 * j, 32 * j + 32))])
                 for j, (s, es) in enumerate(zip(back(rank), both(rank, back(rank))))])
    au = ext("au", sum(nback), mine, 5500)
    iota(A("lj", 0, 8), [[8, 2], [1, 4]], 4, 0, True)
    iota(A("fq", 0, 128), [[32, 4], [0, 32]], 0, 0)

    def scores(h, tile):
        quant("xq", 128 * h, 128 * h + 128, tile, 512 * h)
        for k in range(2):
            mm(4 * (1 - h) + k, "ur0", 0, "xq", 128 * h, 128)

    KS, SV = K["ks"], K["sv"]
    outs = []
    for h in range(2):
        scores(h, "xin")

    for t in range(R):
        first, last = t == 0, t == R - 1
        X = A("xin" if first else "xt", 0, 1024)

        for h in range(2):
            a, b, o = 128 * h, 128 * h + 128, 2048 * (1 - h)
            vtt(A("d1", a, b), A("ps", o, o + 128), A("negm", a, b), ALU.add)
            vscan(A("hs", a, b), A("hold", a, b), A("d1", a, b), ALU.add, ALU.max)
        own = lambda c: A("hs", 16 * c + 15, 16 * c + 16)
        act(A("ssend", 16 * t, 16 * t + 16), A("hs", 15, 256, 16), ACT.Copy)
        mine = send([(s, es, "s%s%d" % ("ab"[j], t),
                      [(A("ssend", 16 * t, 16 * t + 16), A("sland", 32 * t + 16 * j, 32 * t + 16 * j + 16))])
                     for j, (s, es) in enumerate(zip(back(rank), both(rank, back(rank))))])
        e1, e2 = ext("sa%d" % t, nback[0], mine, 3800), ext("sb%d" % t, nback[1], mine, 3800)

        for h in range(2):
            a, b, o = 128 * h, 128 * h + 128, 2048 * (1 - h)
            diag = A("ft", 4 * FT[4 * h], 4 * FT[4 * h + 1], 4)
            vtt(diag, A("ps", o, o + 128), A("hs", a, b), ALU.is_le)
            vseg(A("nes", a, b), diag)
            vtt(A("base", 8 * h, 8 * h + 8), A("cc", 8 * h, 8 * h + 8), A("nes", a + 15, b, 16), ALU.subtract)
        sums = {(0, 0): ("acc", 0, 1), (2, 8): ("acc", 24, 1)}
        for part, blocks in enumerate((range(7, 0, -1), range(7, -1, -1), range(15, 8, -1))):
            for c in blocks:
                how, across = K["blocks"][part][c - blocks[-1]], part == 1
                m, k = (128, c) if across else (16 * (c % 8), 8 - c % 8)
                e, o, at = 4 * FT[2 * part + k // 4], 2048 * (part == 0) + 512 * (how == "s"), 8 * part + c
                flags, seen, sign = A("ft", e + k % 4, e + 4 * m, 4), A("ps", o, o + m), A("sg", 128 * at, 128 * at + m)
                if how == "s":
                    sums[part, c] = ("acc", at, 1)
                    act(sign, seen, ACT.Sign, bias=own(c), scale=-1.0)
                    act(flags, sign, ACT.Relu, scale=-1.0 if across else 1.0, acc=A("acc", at, at + 1))
                else:
                    sums[part, c] = ("scn", 128 * at + 127, 128)
                    vts(flags, seen, own(c), None, ALU.is_gt if across else ALU.is_lt)
                    vsum(A("scn", 128 * at + 128 - m, 128 * at + 128), flags)

        def along(out, step, base, part, c0):
            a = c0
            for c in range(c0 + 1, c0 + 9):
                if c == c0 + 8 or sums[part, c][0] != sums[part, a][0]:
                    name, at, by = sums[part, a]
                    vtt(A(out, step * a + step - 1, step * c, step), A(base, a, c),
                        A(name, at, at + by * (c - a - 1) + 1, by), ALU.add if part == 1 else ALU.subtract)
                    a = c

        for a, b in K["quants"]:
            quant("fc", a, b + (64 if first and b % 128 else 0), "ft", 4 * a)
        once(first, for_lists)
        along("bas2", 1, "base", 0, 0)
        along("lat", 16, "bas2", 1, 0)
        along("lat", 16, "base", 2, 8)
        for h, tiles in enumerate((FT[:2], FT[2:6])):
            grp = None
            for a in tiles:
                grp = mm(2 + h, "gq", 128 * (a in FT[2:4]), "fc", a, 128, start=a == tiles[0], stop=a == tiles[-1],
                         group=grp)
            a, b, o = 128 * h, 128 * h + 128, 1024 + 512 * h
            vscan(A("ce", a, b), A("ps", o, o + 128), A("lat", a, b), ALU.min, ALU.add, 4096.0)
            vts(A("roff", 8 * h, 8 * h + 8), A("ce", a + 15, b, 16), pf(9), None, ALU.add)
            vscatter(row("ob"), A("roff", 8 * h, 8 * h + 8), A("jd", a, b))
        if first:
            dma("y", lambda: g.sync.dma_start(T.wq[:].bitcast(dt.uint8), T.wc[:]), [A("ce", 0, 1)], [A("wq", 0, 512)])
            dma("y", lambda: g.sync.dma_start(T.wqs[:], T.ws[:]), [], [A("wqs", 0, 512)])
        if t == 1:
            dma("y", lambda: g.sync.dma_start(T.vt[:], T.v[:]), [A("ce", 0, 1)], [A("vt", 0, 512)])
        once(first, for_proposals)
        if first:
            pick("ur1", "uland", 8, A("el", 0, 8), [au])
            pick("ur2", "uland", 8, A("el", 0, 8), [au], 32)

        for a, b in ((0, 64), (64, 256)):
            vhold(A("oh", a, b), A("ob", a, b), "m4")
            vts(A("ol", a // 4, b // 4), A("oh", a + 3, b, 4), pf(11), pf(12), ALU.mult, ALU.add)
        scaled("s", A("at", 128, 256), X, 1.0, A("ol", 8, 16))
        scaled("v", A("at", 0, 128), X, 1.0, A("ol", 0, 8))
        quant("qa", 128 * t, 128 * t + 128, "at", 0)
        mm(0, "ur2", 0, "qa", 128 * t, 128)
        mm(1, "ur1", 0, "qa", 128 * t, 128)
        mm(2, "ur1", 0, "qa", 128 * t, 128)
        land = lambda s, r: 128 * t + 64 * slot(s, r)
        piece = lambda name, e, a, b: [(A(name + e, a, a + 64), A("aland" + e, b, b + 64))]
        ways = list(zip(fwd(rank), both(rank, fwd(rank))))
        if handed(rank):
            ways = [(fwd(rank)[0], topo.engines(core, cores[fwd(rank)[0]]))]
        for e in ("", "s"):
            codes = send([(r, es, "aa%d" % t, piece("qa", e, 128 * t, land(rank, r))) for r, es in ways])

        for c in range(32):
            flag, score = A("cmp", 1024 * (c // 16) + c % 16, 1024 * (c // 16) + 1024, 16), A("sland", 32 * t + c, 32 * t + c + 1)
            if c < K["ps"]:
                act(A("sp", 64 * c, 64 * c + 64), A("ps", 512, 576), ACT.Sign, bias=score, scale=-1.0, after=[e1])
                act(flag, A("sp", 64 * c, 64 * c + 64), ACT.Relu)
            else:
                o = 1024 * (c < 16)
                vts(flag, A("ps", o, o + 64), score, None, ALU.is_lt, after=[e1 if c < 16 else e2])
        for e in range(2):
            for a in (0, 512):
                vseg(A("pc", 1536 * e + 256 + a, 1536 * e + 768 + a), A("cmp", 1024 * e + a, 1024 * e + 512 + a))
        for e in range(2):
            vtr(A("pt", 160 * e, 160 * e + 64), A("pc", 1536 * e + 271, 1536 * e + 1280, 16))
            vtr(A("pt", 160 * e + 64, 160 * e + 160), A("pc", 1536 * e + 15, 1536 * e + 1536, 16))
            vseg(A("pp", 160 * e, 160 * e + 160), A("pt", 160 * e, 160 * e + 160))
        vts(A("pm", 0, 16), A("pp", 160, 320), 64.0, None, ALU.max, off=A("fl", 0, 1))
        vtt(A("fsend", 16 * t, 16 * t + 16), A("pp", 0, 160), A("pm", 0, 16), ALU.max, off=A("fl", 0, 1))
        once(first, for_queue)
        once(t == 1, for_ls)
        place = lambda r: 16 * t + 8 * slot(rank, r)
        mine = send([(r, es, "af%d" % t, [(A("fsend", 16 * t, 16 * t + 8), A("fland", place(r), place(r) + 8))])
                     for r, es in zip(fwd(rank), both(rank, fwd(rank)))])
        af = ext("af%d" % t, nfwd, mine, 1500)

        s = back(rank)[0]
        aa = ext("aa%d" % t, 2 * ncodes, *((codes, 5000) if handed(s) or not K["hand"] else (mine, 4000)))
        if handed(s):
            r = fwd(s)[1]
            for e in ("", "s"):
                send([(r, topo.engines(core, cores[r]), "aa%d" % t, piece("aland", e, land(s, rank), land(s, r)))], [aa])
        vset(A("wb", 0, 320), 1.0)
        scaled("s", A("vh", 512 + 4 * SV, 1280), X, 0.5, A("ol", 16 + SV // 4, 64))
        scaled("v", A("vh", 512, 512 + 4 * SV), X, 0.5, A("ol", 16, 16 + SV // 4))
        for b in range(4):
            mm(4 + b, "eq", 128 * b, "aland", 128 * t, 128, [aa])
            act(A("vh", b, 512, 4), A("ps", 2048 + 512 * b, 2048 + 512 * b + 128), ACT.Copy, scale=0.5)
        if last:
            act(A("tbl", 128, 320), A("ob", 64, 256), ACT.Identity, bias=-1.0)

        came = A("fland", 16 * t, 16 * t + 16)
        vtt(A("kx", 0, 128), came, A("keyc", 0, 128), ALU.add, off=A("xl", 0, 8), after=[af])
        vtt(A("ko", 0, 16), came, A("qown", 0, 16), ALU.add, off=A("kl", 0, 1), after=[af])
        vts(A("pb", 0, 16), came, 255.0, -192.0, ALU.min, ALU.add, off=A("kl", 0, 1), after=[af])
        vts(A("pa", 0, 16), came, 255.0, None, ALU.min, off=A("kl", 0, 1), after=[af])
        vtr(A("kr", 0, 128), A("kx", 0, 128))
        for c in range(8):
            part = A("cmp", 128 * c, 128 * c + 128)
            if c < KS:
                act(A("jk", 256 * c, 256 * c + 129), A("kr", 0, 129), ACT.Sign, bias=A("ko", c, c + 1), scale=-1.0,
                    acc=A("ksum", c, c + 1))
                vts(A("poff", c, c + 1), A("ksum", c, c + 1), 0.5, A("pa", c, c + 1), ALU.mult, ALU.add)
            else:
                vts(part, A("kr", 0, 128), A("ko", c, c + 1), None, ALU.is_lt)
                vscan(A("scn", 128 * c, 128 * c + 128), part, A("ones", 0, 128), ALU.add, ALU.mult, A("pb", c, c + 1))
        vts(A("poff", KS, 8), A("scn", 128 * KS + 127, 1024, 128), 129.0, None, ALU.add)
        vscatter(A("wb", 0, 320), A("poff", 0, 8), A("ids", 0, 128))
        vsum(row("cu"), row("wb"))
        vhold(row("wh"), row("wb"), "m4")
        vhold(row("ch"), row("cu"), "m4")
        vts(A("lw", 0, 64), A("wh", 3, 256, 4), 1.0 / TINY, pf(17), ALU.mult, ALU.add)
        vtt(A("lf", 0, 64), A("ch", 3, 256, 4), A("lw", 0, 64), ALU.min)
        vts(A("ll", 0, 64), A("lf", 0, 64), pf(11), pf(18), ALU.mult, ALU.add)
        if last:
            vhold(row("wi"), row("wb"), "m16")
            vhold(row("ci"), row("cu"), "m16")
            act(A("lx", 0, 16), A("wi", 15, 256, 16), ACT.Identity, bias=pf(22), scale=1.0 / TINY)
            vtt(A("lx", 16, 32), A("ci", 15, 256, 16), A("lx", 0, 16), ALU.min)
            vts(A("lk", 0, 16), A("lx", 16, 32), pf(23), 127.0, ALU.mult, ALU.add)
            act(A("lsb", 0, 256), A("tbl", 0, 320), ACT.Copy, off=A("lk", 0, 16))
            vtt(A("lsb", 256, 384), A("kr", 0, 128), A("qrow", 0, 128), ALU.add)
            outs.append(dma("s", lambda: g.scalar.dma_start(T.ls[:], T.lsb[0:128:16, :]), [A("lsb", 0, 384)], []))

        V = A("vh", 0, 1280)
        cuts = [int(w[1:]) for w in K["gather"].split()] + [256]
        for w, a, b in zip(K["gather"].split(), cuts, cuts[1:]):
            scaled(w[0], A("gg", 4 * a, 4 * b), V, 1.0, A("ll", a // 4, b // 4))
        vtt(A("zt", 0, 4), A("gg", 0, 4), A("gg", 0, 4), ALU.add)
        for a, b in ((4, 512), (512, 768), (768, 1024)):
            vtt(A("zt", a, b), A("gg", a, b), A("gg", a - 4, b - 4), ALU.add)
        bank = lambda h, b: 4 * (1 - h) + b
        plane = lambda name, h, b: A(name, 512 * h + b, 512 * h + 512, 4)
        for h in range(2):
            quant("zq", 128 * h, 128 * h + 128, "zt", 512 * h)
            scaled("s", A("z32", 512 * h, 512 * h + 512), A("zt", 512 * h, 512 * h + 512), 32.0)
            for b in range(4):
                mm(bank(h, b), "wq", 128 * b, "zq", 128 * h, 128)
        for h in range(2):
            for b in range(4):
                vtt(plane("x32", h, b), A("ps", 512 * bank(h, b), 512 * bank(h, b) + 128), plane("z32", h, b), ALU.add)
                scaled(K["xc"][4 * h + b], plane("xt", h, b), plane("x32", h, b), 0.03125)
            if not last:
                scores(h, "xt")
                continue
            a, b = 128 * h, 128 * h + 128
            quant("xq", a, b, "xt", 4 * a)
            mm(4 + h, "vq", 0, "xq", a, 128)
            scaled("sv"[h], A("yb", a, b), A("ps", 2048 + 512 * h, 2048 + 512 * h + 128), 1.0)
            outs.append(dma("y", lambda a=a, b=b: g.sync.dma_start(T.oc[:, 4 * a:4 * b], T.xq[:, a:b].bitcast(dt.uint8)),
                            [A("xq", a, b)], [], 3000 - 600 * h))
            if h == 0:
                outs.append(dma("s", lambda: g.scalar.dma_start(T.y[:, 0:128], T.yb[:, 0:128]), [A("yb", 0, 128)], [],
                                2500))
    for k in range(4):
        outs.append(dma("sy"[k % 2], lambda k=k: Q["sy"[k % 2]].dma_start(T.osc[4 * k:4 * k + 4, :],
                                                                         T.xqs[32 * k:32 * k + 4, :]),
                        [A("xqs", 0, 256)], []))
    outs.append(dma("y", lambda: g.sync.dma_start(T.y[:, 128:256], T.yb[:, 128:256]), [A("yb", 128, 256)], []))
    op("g", lambda: g.wait_ge(T.sem.lsent, sent[0]), [], [], 0, outs)

    N = len(ops)
    pre = [[(d, (K["near"] if ops[d]["q"] == o["q"] else WAKE) + ops[d]["late"]) for d in o["deps"]]
           + [(d, 0) for d in o["behind"]] for o in ops]
    post = [[] for o in ops]
    for i in range(N):
        for d, w in pre[i]:
            post[d].append((i, w))
    busy, queue = [o["busy"] for o in ops], [o["q"] for o in ops]

    def lay(before, after, key):
        end, taken = [0] * N, {k: [] for k in Q}
        open_ = [len(b) for b in before]
        can = sorted([(key[i], i) for i in range(N) if not open_[i]], reverse=True)
        while can:
            i = can.pop()[1]
            at = max([0] + [end[d] + w for d, w in before[i]])
            if queue[i] is not None:
                spans = taken[queue[i]]
                k = len(spans)
                while k and spans[k - 1][1] > at:
                    k -= 1
                while k < len(spans) and spans[k][0] < at + busy[i]:
                    at = max(at, spans[k][1])
                    k += 1
                spans.insert(k, (at, at + busy[i]))
            end[i] = at + busy[i]
            for j, w in after[i]:
                open_[j] -= 1
                if not open_[j]:
                    can.append((key[j], j))
            can.sort(reverse=True)
        return end

    def relay(key):
        end = lay(pre, post, key)
        way = lay(post, pre, [-e for e in end])
        return lay(pre, post, [-w for w in way])

    kind = handed(rank)
    if kind not in LAID:
        way = [0] * N
        for i in range(N - 1, -1, -1):
            way[i] = busy[i] + max([0] + [w + way[j] for j, w in post[i]])
        end = relay([-w for w in way])
        seed = [1]

        def some(a, b):
            seed[0] = seed[0] * 48271 % 2147483647
            return a + (b - a) * seed[0] / 2147483647

        for _ in range(K["shakes"]):
            mid, span = some(0, max(end)), some(500, 4000)
            new = relay([end[i] - busy[i] + (some(-400, 400) if abs(end[i] - mid) < span else 0) for i in range(N)])
            if max(new) <= max(end):
                end = new
        LAID[kind] = end
    end = LAID[kind]
    order = sorted(range(N), key=lambda i: (end[i] - busy[i], end[i], i))

    known = {k: 0 for k in Q}
    place_of = {i: k for k, i in enumerate(order)}
    bunches = []
    for i in order:
        o = ops[i]
        o["k"] = 1 << i
        if o["q"] is None:
            o["bunch"] = {"at": o["ext"], "k": o["k"]}
            continue
        o["waits"], fresh = [], {}
        for d in sorted(o["deps"], key=lambda d: -place_of[d]):
            if not known[o["q"]] >> d & 1:
                if "bunch" not in ops[d]:
                    if ops[d]["dma"] not in fresh:
                        fresh[ops[d]["dma"]] = {"calls": [], "k": 0, "dma": ops[d]["dma"]}
                        bunches.append(fresh[ops[d]["dma"]])
                    ops[d]["bunch"] = fresh[ops[d]["dma"]]
                    ops[d]["bunch"]["calls"].append(d)
                    ops[d]["bunch"]["k"] |= ops[d]["k"]
                if not any(b is ops[d]["bunch"] for b in o["waits"]):
                    o["waits"].append(ops[d]["bunch"])
                known[o["q"]] |= ops[d]["bunch"]["k"]
        o["ki"] = known[o["q"]]
        o["k"] |= o["ki"] | (0 if o["group"] is None else ops[o["group"]]["k"])
    pools = {False: [["c%d" % i, 0, 0] for i in range(NCS)], True: [["d%d" % i, 0, 0] for i in range(NDS)]}
    for b in sorted(bunches, key=lambda b: min(place_of[d] for d in b["calls"])):
        s = [p for p in pools[b["dma"]] if all(ops[d]["ki"] & p[2] == p[2] for d in b["calls"])][0]
        s[1] += len(b["calls"]) * (16 if b["dma"] else 1)
        s[2] = sum(1 << d for d in b["calls"])
        b["at"] = (s[0], s[1])

    for i in order:
        o = ops[i]
        if o["q"] is not None:
            for b in o["waits"]:
                Q[o["q"]].wait_ge(T.sem[b["at"][0]], b["at"][1])
            ins = o["fn"]()
            if "bunch" in o:
                ins.then_inc(T.sem[o["bunch"]["at"][0]], 16 if o["dma"] else 1)
